import numpy as np, ml_dtypes
CORES = [35,38,43,46]
N = 4
import mx_ref
BF = ml_dtypes.bfloat16
def entries(a):
    return np.ascontiguousarray(a.T).reshape(-1)
def table(e):
    return np.ascontiguousarray(np.reshape(e, (-1, 16)).T).astype(np.int32)
def gentries(a):
    return np.ascontiguousarray(a.reshape(8, 16, -1).transpose(0, 2, 1)).reshape(8, -1)
def gtable(e):
    e = np.asarray(e); return np.ascontiguousarray(e.reshape(8, -1, 16).transpose(0, 2, 1)).reshape(128, -1).astype(np.int32)
def gcols(t, e):
    v = np.concatenate([t.reshape(8, 16, -1, 4), np.zeros((8, 16, 1, 4), BF)], axis=2)
    return np.ascontiguousarray(np.stack([v[g][:, e[g]] for g in range(8)])).reshape(128, -1)
def tile(rs):
    return np.stack(rs, axis=2).reshape(128, -1).astype(BF)
def pick(q, e):
    c = np.concatenate([q[0].reshape(128, -1, 4), np.zeros((128, 1, 4), np.uint8)], axis=1); s = np.concatenate([q[1], np.ones((16, 1), np.uint8)], axis=1)
    return (np.ascontiguousarray(c[:, e].reshape(128, -1)), np.ascontiguousarray(s[:, e]))
def join(*qs):
    return (np.concatenate([q[0] for q in qs], axis=1), np.concatenate([q[1] for q in qs], axis=1))
def put(q, e, v):
    c, s = q[0].reshape(128, -1, 4).copy(), q[1].copy(); c[:, e] = v[0].reshape(128, -1, 4); s[:, e] = v[1]
    return (c.reshape(128, -1), s)
def pk(c, s):
    return (np.ascontiguousarray(c), mx_ref.live(s))
def emit(q):
    return q[0], q[1]
def packed(v, rng):
    q = [mx_ref.quantize(np.ascontiguousarray(v[r])) for r in range(N)]
    return np.stack([a for a, b in q]), np.stack([mx_ref.plane(b, rng) for a, b in q])
def values_of_codes():
    e, c = np.zeros((128, 128, 4), np.float32), np.zeros((128, 2, 4), np.uint8)
    e[np.arange(128), np.arange(128), 0] = 1
    c[:127, :, 0] = np.arange(256).reshape(2, 128).T[:127]
    return mx_ref.matmul(mx_ref.quantize(e.reshape(128, 512).astype(BF)), (c.reshape(128, 8), np.full((16, 2), 127, np.uint8))).T.reshape(-1).astype(np.float64)
CODE_VALUE, SCALE_VALUE = values_of_codes(), 2.0 ** (np.arange(256) - 127.0)
def decode(q):
    return (CODE_VALUE[q[0]].reshape(16, 8, -1, 4) * SCALE_VALUE[q[1]][:, None, :, None] + 0.0).reshape(128, -1).astype(np.float32)
def f(rng, *shape):
    return mx_ref.flush((rng.standard_normal(shape, dtype=np.float32) * np.exp2(rng.integers(-2, 3, shape[:-1] + (1,)))).astype(BF))
def wide(rng, *shape, cols=0):
    v = rng.standard_normal(shape, dtype=np.float32) * np.exp2(rng.integers(-12, 13, shape)).astype(np.float32)
    if cols: v *= np.repeat(np.exp2(rng.integers(-cols, cols + 1, shape[:-2] + (1, shape[-1] // 4))) * (rng.random(shape[:-2] + (1, shape[-1] // 4)) > 0.0625), 4, axis=-1).astype(np.float32)
    return mx_ref.flush(v.astype(BF))
C, K, M = 384, 96, 4
DIST = [1, 2, 3]
def big(v):
    v = v.astype(np.float32)
    v[np.abs(v) < np.float32(2.0 ** -16)] = 0
    return v.astype(BF)
def numbers_of(rng):
    return {"x": big(f(rng, N, 128, 4 * C)), "u": np.array(f(rng, N, 128, 512)), "v": np.array(f(rng, N, 128, 512))}
def trees(rng):
    j = np.arange(C)
    return np.maximum(j - 1 - np.floor(rng.random((N, C)) ** 3 * j).astype(np.int64), 0)
def flags(rng):
    a = (rng.random((N, 8, C)) < 0.5) * 1
    a[:, :, 0] = 1
    return a
def lists_of(e, a):
    return {"par": np.stack([table(e[r]) for r in range(N)]), "fl": np.stack([gtable(a[r]) for r in range(N)])}
def layers(rng):
    return big(f(rng, N, 128, 2048)).reshape(N, 8, 16, 4, 8, 16, 4)
def carry(w, parts, k):
    k = np.asarray(k, np.float32).astype(BF)
    w[:, :, :, :, :, parts] = 0
    for g in range(8):
        for i in parts:
            for b in range(4): w[:, g, i, b, g, i, b] = k[:, g]
    return w
def weights(rng, w):
    c, p = packed(np.ascontiguousarray(w).reshape(N, 128, 2048), rng)
    return {"wc": c, "ws": p}
def setup_inputs(rng):
    return {**numbers_of(rng), **lists_of(trees(rng), flags(rng)), **weights(rng, layers(rng))}
def setup_inputs_ties(rng):
    d = numbers_of(rng)
    first = int(rng.integers(N))
    ones = [(first + 1) % N, (first + 2) % N]
    x = d["x"].reshape(N, 8, 16, C, 4)
    for r in range(N):
        a = x[r][:, :8, :3].copy()
        a[:, :, 2] = 0
        x[r][:, :8] = a[:, :, rng.permutation(C) % 3]
    x[first, :, :8] = 0
    x[ones, :, :8] = 1
    u = d["u"].reshape(N, 8, 16, 128, 4)
    z = u.copy()
    u[:, :, :, ::16] = 0
    u[:, :, :, 1::16] = 0
    for g in range(8):
        for i in (16 * g, 16 * g + 1):
            u[:, g, :8, i] = z[:, g, :8, i]
            for r in ones: u[r, g, :8, i] = np.abs(z[r, g, :8, i])
    w = carry(layers(rng), list(range(8)), np.full((N, 8), 32.0))
    return {"x": x.reshape(N, 128, 4 * C), "u": u.reshape(N, 128, 512), "v": d["v"], **lists_of(trees(rng), flags(rng)), **weights(rng, w)}
def setup_inputs_near(rng):
    d = numbers_of(rng)
    x = np.zeros((N, 8, 16, C, 4), np.float32)
    a = (N, 8, 8, C, 4)
    x[:, :, 8:] = rng.choice([-1.0, 1.0], a) * (1.0 + (2 * rng.integers(0, 64, a) + 1) * 2.0 ** -7) * np.exp2(-rng.integers(8, 15, a).astype(np.float64))
    x[:, :, 8 + int(rng.integers(8)), :, int(rng.integers(4))] = np.where(np.arange(8) % 2 == 1, 1.75, 1.96875)[None, :, None]
    x[:, :, 8:] *= np.exp2(rng.integers(-1, 2, (N, 8, 1, C, 1)).astype(np.float32))
    u = d["u"].reshape(N, 128, 128, 4)
    u[:, :, ::16] = 0
    u[:, :, 1::16] = 0
    o = rng.permutation(N) % 2
    m = flags(rng)
    for r in range(N):
        k = 2.0 ** -30 if o[r] == 0 else 1.0
        s = rng.integers(-1, 2, (8, 2, C)) * k
        t = np.concatenate([1.125 * s, -1.25 * s], axis=1)
        for g in rng.permutation(8)[:4]:
            j = int(rng.integers(C))
            t[g, :2, j] = 2.0 ** 30 * rng.choice([-1.0, 1.0], 2)
            t[g, 2:, j] = 0
            m[r, g, j] = 1
        x[r, :, :4, :, 0] = t
        for h in range(0, 128, 16):
            for b in range(2):
                u[r, h + b, h + b, 0] = 1.125 * k
                u[r, h + 2 + b, h + b, 0] = k
    w = np.zeros((N, 8, 16, 4, 8, 16, 4), np.float32).astype(BF)
    w = carry(w, list(range(8)), np.full((N, 8), 32.0))
    w = carry(w, list(range(8, 16)), np.where(np.arange(8) % 2 == 1, 36.0, 32.0) * np.ones((N, 1)))
    return {"x": x.reshape(N, 128, 4 * C).astype(BF), "u": u.reshape(N, 128, 512), "v": d["v"], **lists_of(trees(rng), m), **weights(rng, w)}
def setup_inputs_chain(rng):
    d = numbers_of(rng)
    u = d["u"].reshape(N, 128, 128, 4)
    g = int(rng.integers(8))
    u[:, :, 16 * g:16 * g + 2] = 0
    d["u"] = u.reshape(N, 128, 512)
    o = rng.permutation(N) % 4
    e = np.stack([np.maximum(np.arange(C) - 1, 0)] * N)
    m = np.zeros((N, 8, C), np.int64)
    for r in range(N):
        if o[r] == 1: m[r, np.arange(8), rng.integers(1, C // 4, 8)] = 1
        if o[r] == 2:
            e[r] = 0
            m[r, rng.permutation(8)[:4]] = 1
        if o[r] == 3: m[r] = 1
    m[:, :, 0] = 1
    return {**d, **lists_of(e, m), **weights(rng, layers(rng))}
def setup_inputs_huge(rng):
    d = numbers_of(rng)
    c = rng.choice([-1.0, 1.0], (N, 8, 1, C, 1))
    c[int(rng.integers(N))] = -1
    x = c * (0.8 + 0.2 * rng.random((N, 8, 16, C, 4))) * 2.0 ** 30
    u = d["u"].reshape(N, 8, 16, 128, 4)
    u[:, :, :, ::16] = 0
    u[:, :, :, 1::16] = 0
    for g in range(8):
        for b in range(2):
            for h in rng.permutation(8)[:1 + 2 * ((g + b) % 4)]:
                u[:, h, :, 16 * g + b] = (2.0 ** 30 * (0.9 + 0.1 * rng.random((N, 16, 4)))).astype(np.float32).astype(BF)
    w = carry(np.zeros((N, 8, 16, 4, 8, 16, 4), np.float32).astype(BF), list(range(16)), 32.0 * rng.choice([-1.0, 1.0], (N, 8)))
    return {"x": x.astype(np.float32).reshape(N, 128, 4 * C).astype(BF), "u": u.reshape(N, 128, 512), "v": d["v"], **lists_of(trees(rng), flags(rng)), **weights(rng, w)}
def setup_inputs_spread(rng):
    d = setup_inputs(rng)
    d["x"] = big(wide(rng, N, 128, 4 * C, cols=6))
    return d
def check_inputs(d):
    b = []
    for k in ("x", "u", "v"):
        a = np.abs(d[k].astype(np.float32))
        if not (np.isfinite(a).all() and ((a == 0) | (a >= 2.0 ** -30) & (a <= 2.0 ** 30)).all()): b.append("a value of " + k)
    none, least, most = [emit(mx_ref.quantize(np.full((128, 16), k, np.float32).astype(BF)))[1][0, 0] for k in (0.0, 2.0 ** -30, 2.0 ** 30)]
    for r in range(N):
        e = entries(d["par"][r])
        if e[0] != 0 or ((e[1:] < 0) | (e[1:] >= np.arange(1, C))).any(): b.append("par: an entry out of range")
        m = gentries(d["fl"][r])
        if ((m != 0) & (m != 1)).any(): b.append("fl: an entry that is neither 0 nor 1")
        if (m[:, 0] != 1).any(): b.append("fl: column 0 isn't flagged in every group")
        if ((d["wc"][r] == 0x7F) | (d["wc"][r] == 0xFF)).any(): b.append("wc: a code that is no number")
        s = mx_ref.live(d["ws"][r])
        if ((s != none) & ((s < least) | (s > most))).any(): b.append("ws: a scale out of range")
    return b
def inherited(now, flag, up):
    a = np.where(flag == 1, np.arange(C), up[:, None])
    for i in range(9): a = np.take_along_axis(a, a, axis=2)
    return [gcols(now[r], a[r]) for r in range(N)]
def reference(x, u, v, par, fl, wc, ws):
    qu = [mx_ref.quantize(u[r]) for r in range(N)]
    lay = [pk(wc[r], ws[r]) for r in range(N)]
    now = [x[r] for r in range(N)]
    up = np.stack([entries(par[r]) for r in range(N)])
    flag = np.stack([gentries(fl[r]) for r in range(N)])
    for h in DIST:
        e = inherited(now, flag, up)
        sym, came, new = [], [], []
        for r in range(N):
            q = mx_ref.quantize(e[r])
            s = mx_ref.matmul(qu[r], q)
            sym.append(2 * (s[::16] > 0) + (s[1::16] > 0))
            k = pick(q, np.arange(0, C, M))
            t = tile([mx_ref.matmul(pick(lay[r], np.arange(128 * b, 128 * b + 128)), k) * np.float32(0.03125) for b in range(4)])
            came.append(decode(mx_ref.quantize(t)).astype(BF))
        for r in range(N):
            d = (r + h) % N
            key, lock = sym[d][:, ::M], sym[r]
            master = lock[:, up[r]]
            agree = (key[:, None] == lock[:, :, None]) | (key[:, None] == master[:, :, None])
            best = np.argmax(np.count_nonzero(agree, axis=0), axis=1)
            far = key[:, best]
            wanted = (far != lock) & (far != master)
            left = (far != lock) & (far == master)
            new.append(gcols(np.concatenate([now[r], came[d]], axis=1), np.where(wanted, C + best, np.arange(C))))
            flag[r] = np.where(wanted, 1, np.where(left, 0, flag[r]))
        now = new
    e = inherited(now, flag, up)
    y, ofl = np.zeros((N, 128, C), np.float32), np.zeros((N, 8, C), np.float32)
    oc, osc = np.zeros((N, 128, 4 * C), np.uint8), np.zeros((N, 16, C), np.uint8)
    for r in range(N):
        q = mx_ref.quantize(e[r])
        y[r] = mx_ref.matmul(mx_ref.quantize(v[r]), q)
        ofl[r] = flag[r]
        oc[r], osc[r] = emit(q)
    return {"y": y, "ofl": ofl, "oc": oc, "osc": osc}

@@ -1,0 +1,518 @@
+from concourse.mybir import dt, AluOpType as A, ActivationFunctionType as F
+
+C, K = 384, 96
+DIST = [1, 2, 3]
+TW = C + 3 * K
+BIG = float(2 ** 21)
+FP8, U8, U16, I32, F32, BF = "float8_e4m3fn_x4", "uint8", "uint16", "int32", "float32", "bfloat16"
+
+
+def _sb(n, d):
+    return ("sbuf", [128, n], d)
+
+
+SCRATCH = {
+    "XR": _sb(4 * C, BF), "TAB": _sb(4 * TW, BF), "ET": _sb(4 * C, BF), "HT": _sb(512, BF), "UT": _sb(512, BF),
+    "VT": _sb(512, BF), "ONE": _sb(520, BF), "EC": _sb(520, BF),
+    "QU0": _sb(128, FP8), "SU0": _sb(128, U8), "QU": _sb(128, FP8), "SU": _sb(128, U8), "QV": _sb(128, FP8),
+    "SV": _sb(128, U8), "QW": _sb(512, FP8), "SW": _sb(512, U8), "QC": _sb(512, FP8), "SC": _sb(512, U8),
+    "LQ": _sb(128 + 3 * K, FP8), "LS": _sb(128 + 3 * K, U8),
+    "PI": _sb(1, I32), "CI": _sb(12, I32), "CF": _sb(40, F32),
+    "T16": _sb(144, F32), "M1": _sb(288, F32), "MM": _sb(144, F32), "IO": _sb(C, F32),
+    "PT": _sb(C, F32), "R6": _sb(6, F32), "RTX": _sb(48, F32), "RX": _sb(C, F32), "SCN": _sb(128, F32),
+    "HR": _sb(128, F32), "KD": _sb(288, F32), "JJ": _sb(144, F32), "SELF": _sb(8, F32),
+    "LPAR": _sb(2, U16), "LU": _sb(8, U16), "LA": _sb(8, U16), "LP": _sb(8, U16), "LTX": _sb(4, U16),
+    "LFW": _sb(6, U16), "LL": _sb(18, U16), "LFL": _sb(4, U16), "LEX": _sb(6, U16), "PU": _sb(4, U16),
+    "PL": _sb(16, U16), "LS16": _sb(6, U16), "LM": _sb(8, U16), "LT": _sb(18, U16), "KL": _sb(4, U16),
+    "PTR": _sb(24, U16),
+    "PR": _sb(32, I32), "PF": _sb(16, F32), "PD": _sb(16, F32), "FLR": _sb(C, I32),
+    "RA": _sb(96, F32), "SCO": _sb(144, F32), "WA": _sb(96, F32), "DA": _sb(144, F32),
+    "WH": _sb(176, F32), "WX": _sb(96, F32), "WC": _sb(96, F32), "DI": _sb(32, I32), "DF": _sb(48, F32),
+    "VA": _sb(96, F32), "VB": _sb(96, F32), "AA": _sb(96, F32), "AB": _sb(96, F32), "HB": _sb(176, F32),
+    "HX": _sb(96, F32), "CP": _sb(C, F32), "YY": _sb(C, F32), "OI": _sb(96, I32), "OJ": _sb(96, I32),
+    "SK": _sb(112, BF), "YK": _sb(192, BF), "ZL": _sb(144, F32),
+    "SG": _sb(C, BF), "T1H": _sb(288, BF), "T2H": _sb(288, BF), "LMH": _sb(96, BF), "LMC": _sb(288, BF),
+    "TA": _sb(C, F32), "TP": _sb(128, F32), "TQ": _sb(64, F32), "TT": _sb(64, F32), "MP": _sb(144, F32),
+    "AC": _sb(288, F32), "ACI": _sb(96, I32), "CHI": _sb(288, I32), "CHF": _sb(288, F32), "CHS": _sb(288, F32),
+    "KI": _sb(8, I32), "RF": _sb(24, F32), "XF": _sb(96, BF), "FW": _sb(96, BF), "UP": _sb(240, F32),
+    "OF": _sb(48, F32), "YO": _sb(C, F32),
+}
+for _r in range(4):
+    SCRATCH["QE%d" % _r] = _sb(C, FP8)
+    SCRATCH["SE%d" % _r] = _sb(C, U8)
+for _r in range(3):
+    SCRATCH["TX%d" % _r] = _sb(48, U16)
+    SCRATCH["AR%d" % _r] = _sb(48, U16)
+    SCRATCH["QH%d" % _r] = _sb(128, FP8)
+    SCRATCH["SH%d" % _r] = _sb(128, U8)
+for _n in ("PK", "PA", "PH0", "PH1", "PH2", "PH3"):
+    SCRATCH[_n] = ("psum", [128, 512], F32)
+
+SEMAPHORES = ["cv", "cs", "ct", "cg", "dpar", "dx", "du", "dfl", "dw", "dv", "dout", "dend", "sent",
+              "ra0", "ra1", "ra2", "rh0", "rh1", "rh2"]
+
+
+def rank_program(g, core, T, topo):
+    rank = T.rank_of(core)
+    if rank is None:
+        return
+    N = len(T.cores)
+    Q = {"v": g.vector, "s": g.scalar, "t": g.tensor, "g": g, "y": g.sync}
+    total = {n: 0 for n in SEMAPHORES}
+    seen = {q: {} for q in Q}
+    log = {}
+
+    def V(name, c0=0, c1=None, st=1, p0=0, p1=128, ps=1):
+        if c1 is None:
+            c1 = SCRATCH[name][1][1]
+        t = T[name]
+        ap = t[p0:p1:ps, c0:c1] if ps > 1 else (t[p0:p1, c0:c1] if st == 1 else t[p0:p1, c0:c1:st])
+        return (ap, [(name, p0, p1, frozenset(range(c0, c1, st)))])
+
+    def col(k):
+        return V("CF", k, k + 1)
+
+    def ind(win, off, words=False):
+        ap = win[0].bitcast(dt.uint32) if words else win[0]
+        return (ap.indirect(off[0]), win[1] + off[1])
+
+    def wait(q, sem, val):
+        if seen[q].get(sem, 0) < val:
+            Q[q].wait_ge(T.sem[sem], val)
+            seen[q][sem] = val
+
+    def meet(q, rd, wr):
+        need = {}
+        for regs, writing in ((rd, False), (wr, True)):
+            for (name, p0, p1, cols) in regs:
+                bank = SCRATCH[name][0] == "psum"
+                for (w, q2, a0, a1, cs, sem, val) in log.get(name, []):
+                    if bank:
+                        hit = w or writing or q2 != q
+                    else:
+                        hit = (w or writing) and a0 < p1 and p0 < a1 and not cols.isdisjoint(cs)
+                    if hit:
+                        need[sem] = max(need.get(sem, 0), total[sem] if val is None else val)
+        for sem in need:
+            wait(q, sem, need[sem])
+
+    def note(q, regs, writing, sem, val):
+        for (name, p0, p1, cols) in regs:
+            log.setdefault(name, []).append((writing, q, p0, p1, cols, sem, val))
+
+    def op(q, fn, outs, ins):
+        w = [r for o in outs for r in o[1]]
+        rd = [r for o in ins if isinstance(o, tuple) for r in o[1]]
+        meet(q, rd, w)
+        sem = "c" + q
+        fn().then_inc(T.sem[sem], 1)
+        total[sem] += 1
+        note(q, rd, False, sem, total[sem])
+        note(q, w, True, sem, total[sem])
+
+    def a_(x):
+        return x[0] if isinstance(x, tuple) else x
+
+    def cp(o, i):
+        op("v", lambda: g.vector.tensor_copy(o[0], i[0]), [o], [i])
+
+    def tt(o, a, b, f):
+        op("v", lambda: g.vector.tensor_tensor(o[0], a[0], b[0], f), [o], [a, b])
+
+    def ts(o, a, s1, f0, s2=None, f1=None):
+        if f1 is None:
+            op("v", lambda: g.vector.tensor_scalar(o[0], a[0], a_(s1), None, f0), [o], [a, s1])
+        else:
+            op("v", lambda: g.vector.tensor_scalar(o[0], a[0], a_(s1), a_(s2), f0, f1), [o], [a, s1, s2])
+
+    def ms(o, c):
+        op("v", lambda: g.vector.memset(o[0], c), [o], [])
+
+    def scan(o, d0, d1, f0, f1):
+        op("v", lambda: g.vector.tensor_tensor_scan(o[0], d0[0], d1[0], 0.0, f0, f1), [o], [d0, d1])
+
+    def tr(o, i):
+        op("v", lambda: g.vector.transpose(o[0], i[0]), [o], [i])
+
+    def quant(qo, so, i):
+        op("v", lambda: g.vector.quantize_mx(qo[0], so[0], i[0]), [qo, so], [i])
+
+    def act(o, i, f, bias=None, scale=None):
+        kw = {}
+        if bias is not None:
+            kw["bias"] = a_(bias)
+        if scale is not None:
+            kw["scale"] = a_(scale)
+        op("s", lambda: g.scalar.activation(o[0], i[0], f, **kw), [o], [i, bias, scale])
+
+    def mm(o, wq, wsc, xq, xsc):
+        op("t", lambda: g.tensor.matmul_mx(o[0], wq[0], wsc[0], xq[0], xsc[0], True, True), [o], [wq, wsc, xq, xsc])
+
+    def iota(o, pat, base, cm=0, small=True):
+        if small:
+            op("g", lambda: g.iota(o[0], pat, base, cm, allow_small_or_imprecise_dtypes=True), [o], [])
+        else:
+            op("g", lambda: g.iota(o[0], pat, base, cm), [o], [])
+
+    def dma(q, sem, o, i):
+        meet(q, i[1] if isinstance(i, tuple) else [], o[1] if isinstance(o, tuple) else [])
+        Q[q].dma_start(a_(o), a_(i)).then_inc(T.sem[sem], 16)
+        total[sem] += 16
+        if isinstance(i, tuple):
+            note(q, i[1], False, sem, None)
+        if isinstance(o, tuple):
+            note(q, o[1], True, sem, None)
+
+    def u8(x):
+        return (x[0].bitcast(dt.uint8), x[1])
+
+    NE = 8
+
+    def send(dst, sem, o, i):
+        meet("g", i[1], [])
+        rid, pid, _se = topo.addr(dst)
+        m = 0
+        for e in topo.engines(core, dst)[:NE]:
+            m |= 1 << e
+        g.remote_dma(o[0], i[0], T.sem[sem], T.sem["sent"], pid, rid, m)
+        total["sent"] += NE
+
+    def landed(sem, x):
+        total[sem] += NE
+        note("far", x[1], True, sem, None)
+
+    for r in range(3):
+        landed("ra%d" % r, V("AR%d" % r))
+        landed("rh%d" % r, V("LQ", 128 + K * r, 128 + K * r + K))
+        landed("rh%d" % r, V("LS", 128 + K * r, 128 + K * r + K))
+
+    dma("y", "dpar", V("PR", 0, 24, 1, 0, 16), T.par[:, :])
+    dma("s", "dpar", V("PR", 0, 24, 1, 16, 32), T.par[:, :])
+    ms(V("FLR"), 0)
+    for G in range(8):
+        dma("y", "dfl", V("FLR", 0, C, 1, 16 * G, 16 * G + 16, 2), T.fl[:, :])
+    dma("s", "dx", V("XR"), T.x[:, :])
+    dma("s", "du", V("UT"), T.u[:, :])
+    dma("y", "dw", u8(V("QW")), T.wc[:, :])
+    dma("y", "dw", V("SW"), T.ws[:, :])
+    dma("y", "dv", V("VT"), T.v[:, :])
+
+    iota(V("PI"), [[0, 1]], 0, 1, False)
+    iota(V("IO", 0, 96), [[1, 96]], 0)
+    iota(V("T16"), [[0, 9], [1, 16]], 0)
+    iota(V("PT", 0, 48), [[-16384 - 16, 3], [-1023, 16]], 1024 * 1024 + 80)
+    iota(V("PT", 48, 96), [[-16384 + 16, 3], [-1023, 16]], (1024 - 48) * 1024)
+    iota(V("R6"), [[16, 3], [0, 2]], 0)
+    iota(V("IO", 96, C), [[1, C - 96]], 96)
+    iota(V("RTX", 0, 24), [[1, 4], [8, 6]], 96)
+    iota(V("RTX", 24, 48), [[16, 3], [1, 8]], 0)
+    for s in range(6):
+        iota(V("RX", s, 96, 6), [[4, 4], [96, 4]], 16 * [0, 5, 2, 1, 4, 3][s])
+        iota(V("RX", 96 + s, 192, 6), [[0, 16]], 16 * ([5, 0, 3, 2, 1, 4][s] - [0, 5, 2, 1, 4, 3][s]) + 2)
+    iota(V("SCN", 0, 16), [[4, 4], [0, 4]], 0)
+    iota(V("SCN", 16, 32), [[1, 4], [0, 4]], 0)
+    iota(V("ONE"), [[0, 520]], 1)
+    op("g", lambda: g.affine_select(T.EC[:, :], T.ONE[:, :], [[-1, 520]], A.is_equal, 0.0, 3, 4), [V("EC")], [V("ONE")])
+
+    ms(V("PR", 24, 32), 0)
+    cI, cI3, cI12, cIh, cB0, cG, cH16, cA, cB1, cH = range(10)
+    for k, (sh, m) in enumerate([(0, 15), (0, 3), (0, 12), (1, 7), (0, 1), (4, 7), (0, 16), (5, 3), (1, 1), (4, 1)]):
+        ts(V("CI", k, k + 1), V("PI"), sh, A.logical_shift_right, m, A.bitwise_and)
+    ms(V("LT"), 0)
+    cp(V("CF", 0, 10), V("CI", 0, 10))
+    (cG48, cI1, cFix, cG3, cFl, cK1, cK2, cWk, cM0, cKl, cK80, cMa, cMb, cD, cTop, cJ, cJx, cUk, cCA,
+     cP1, cP2, cLk) = range(10, 32)
+    JJ, JX, JB = V("JJ", 0, 48), V("JJ", 48, 96), V("JJ", 96, 144)
+    ms(V("WH", 0, 16), 0.0)
+    ts(col(cI1), col(cI), 1.0, A.add)
+    ts(col(cG48), col(cG), 48.0, A.mult)
+    ts(V("LPAR", 0, 1), col(cG), 3.0, A.mult, col(cI3), A.add)
+    ts(col(cFix), col(cI), 15.0, A.is_lt, BIG, A.mult)
+    ts(V("SELF", 0, 3), V("IO", 0, 3), 16.0, A.mult, col(cI), A.add)
+    ts(V("SELF", 4, 7), V("IO", 0, 3), 16.0, A.mult, col(cG48), A.add)
+
+    def columns(rows):
+        for k, src, sc, bi in rows:
+            act(col(k), col(src), F.Identity, bi, sc)
+
+    columns([(cUk, cIh, 16.0, col(cB0)), (cG3, cG, 3.0, 0.0), (cLk, cG, 48.0, col(cI)), (cJx, cG, 49200.0, 1024.0),
+             (cFl, cI, 24.0, col(cG3)), (cD, cG, -48.0, 16.0)])
+    for a in range(1, 4):
+        act(V("PT", 96 * a, 96 * a + 96), V("PT", 0, 96), F.Identity, float(-96 * a * 1023), 1.0)
+    act(JX, V("IO", 0, 48), F.Identity, col(cJx), 1025.0)
+    columns([(cM0, cH, 1.0, -1.0), (cMa, cA, 96.0, 32.0), (cTop, cH16, -64.0, 1024.0),
+             (cMb, cA, -96.0, 1040.0), (cK1, cB0, -1.0, 2.0), (cK2, cB1, -3.0, 4.0),
+             (cKl, cH16, -5.0, 95.0), (cK80, cH16, 6.0, -17.0), (cJ, cG, 49152.0, 1024.0),
+             (cCA, cI3, 32.0, col(cH16)), (cP1, cI12, 1.0, 2.0), (cP2, cI3, 4.0, 18.0), (cWk, cK1, col(cK2), 0.0)])
+    ts(V("M1", 0, 144), V("T16"), col(cI), A.is_equal, -3.0 * BIG, A.mult)
+    ts(V("M1", 144, 288), V("T16"), col(cI1), A.is_equal, BIG, A.mult)
+
+    def const(o, c):
+        act(o, V("PT", 0, len(o[1][0][3])), F.Identity, c, 0.0)
+
+    for a in range(1, 4):
+        cp(V("PR", 0, 24, 1, 32 * a, 32 * a + 32), V("PR", 0, 24, 1, 0, 32))
+    tt(V("MM", 0, 48), V("M1", 0, 48), V("M1", 144, 192), A.add)
+    cp(V("PF"), ind(V("PR"), V("LPAR", 0, 1)))
+    ms(V("WH", 96, 112), 0.0)
+    tt(V("PD", 4, 7), V("PF", 0, 3), V("SELF", 4, 7), A.is_lt)
+    ts(V("PD", 0, 3), V("PF", 0, 3), col(cG48), A.subtract)
+    tt(V("PD", 8, 11), V("PD", 4, 7), V("SELF", 0, 3), A.mult)
+    cp(V("PU", 0, 3), V("PF", 0, 3))
+    tt(V("PD", 12, 15), V("PD", 0, 3), V("PD", 8, 11), A.max)
+    ms(V("HB", 0, 16), 0.0)
+    cp(V("PL", 0, 3), V("PD", 12, 15))
+    ms(V("HB", 96, 112), 0.0)
+    cp(V("RA", 0, 48), ind(V("IO", 0, 48), V("PL", 0, 3)))
+    act(V("WA", 0, 48), ind(V("PT"), V("PU", 0, 3)), F.Copy)
+    act(V("DA", 0, 48), ind(V("IO"), V("PU", 0, 3)), F.Identity, col(cD), 1.0)
+    const(V("CP", 96, C), 0.0)
+    const(V("YY"), 0.0)
+
+    def local(k, vin):
+        src = vin if k == 0 else ("AA" if k % 2 else "AB")
+        off = V("PL", 4 * k, 4 * k + 3)
+        if k == 3:
+            tt(V("HB", 16, 64), ind(V(src, 0, 48), off), V(src, 48, 96), A.max)
+            return
+        dst = "AB" if k % 2 else "AA"
+        tt(V(dst, 0, 48), ind(V(src, 0, 48), off), V(src, 48, 96), A.max)
+        tt(V(dst, 48, 96), ind(V(src, 48, 96), off), V(src, 0, 48), A.max)
+
+    def seq(hb, c):
+        own = V(hb, 16 + 16 * c, 32 + 16 * c)
+        tt(own, ind(V(hb, 0, 16 + 16 * c), V("LS16", 2 * c, 2 * c + 1)), own, A.max)
+        cp(V(hb, 96 - 16 * c, 112 - 16 * c), V(hb, 16 * c, 16 * c + 16))
+
+    def swap(hb, hx):
+        tr(V(hx), V(hb, 16, 112))
+        tr(V(hb, 112, 176), V(hx, 16, 80))
+
+    def mid(hb, out):
+        tt(V(out, 0, 48), ind(V(hb, 96, 176), V("LM", 0, 3)), V(hb, 16, 64), A.max)
+        tt(V(out, 48, 96), ind(V(hb, 0, 64), V("LM", 4, 7)), V(hb, 112, 160), A.max)
+
+    def top():
+        def part(a, p0=0):
+            return V("CP", 96 * a, 96 * a + 96, 1, p0, p0 + 32)
+
+        def turn(a):
+            tr(V("YY", 96 * a, 96 * a + 96, 1, 0, 32), part(a))
+
+        cp(part(1), part(0, 32))
+        act(part(2), part(0, 64), F.Copy)
+        act(part(3), part(0, 96), F.Copy)
+        turn(0)
+        for a in range(1, 4):
+            tt(V("CP", 96 * a, 96 * a + 96), ind(V("CP", 0, 96 * a), V("LT", 6 * a - 6, 6 * a)),
+               V("CP", 96 * a, 96 * a + 96), A.max)
+            if a > 1:
+                turn(a - 1)
+        turn(3)
+        cp(V("OI"), ind(V("YY"), V("LEX")))
+        ts(V("OJ", 0, 96, 1, 0, 32), V("OI", 0, 96, 1, 0, 32), 1023, A.bitwise_and)
+        for a in range(4):
+            cp(V("PTR", 0, 24, 1, 32 * a, 32 * a + 32), V("OJ", 24 * a, 24 * a + 24, 1, 0, 32))
+
+    fill = [
+        lambda: ts(V("LU"), V("IO", 0, 8), 0.0, A.mult, col(cUk), A.add),
+        lambda: ts(V("LL", 0, 6), V("R6"), col(cLk), A.add),
+        lambda: cp(V("LL", 6, 12, 2), V("PF", 0, 3)),
+        lambda: ts(V("LFL", 0, 3), V("IO", 0, 3), col(cFl), A.add),
+        lambda: cp(V("LL", 7, 12, 2), V("PF", 0, 3)),
+        lambda: ts(V("LL", 12, 15), V("R6", 0, 6, 2), col(cLk), A.add),
+    ]
+    ra, rb = V("RA", 0, 48), V("RA", 48, 96)
+    for k in range(3):
+        cp(rb, ind(ra, V("PL", 4 * k, 4 * k + 3)))
+        fill[2 * k]()
+        scan(V("SCO", 0, 48), V("MM", 0, 48), rb, A.add, A.max)
+        fill[2 * k + 1]()
+        ts(V("PL", 4 * k + 4, 4 * k + 7), V("SCO", 15, 48, 16), col(cFix), A.subtract)
+        ra, rb = rb, ra
+    p3 = V("PL", 12, 15)
+    cp(V("DA", 48, 96), ind(V("DA", 0, 48), p3))
+    act(V("WA", 48, 96), ind(V("WA", 0, 48), p3), F.Copy)
+    tt(V("MM", 48, 144), V("M1", 48, 144), V("M1", 192, 288), A.add)
+    cp(V("DA", 96, 144), ind(V("DA", 48, 96), p3))
+    act(V("WH", 16, 64), ind(V("WA", 48, 96), p3), F.Copy)
+    for b in range(4):
+        act(V("TAB", TW * b, TW * b + C), V("XR", b, 4 * C, 4), F.Copy)
+    cp(V("LL", 15, 18), V("PF", 0, 3))
+    scan(V("SCO", 0, 48), V("MM", 0, 48), V("DA", 96, 144), A.add, A.max)
+    tt(V("VA", 0, 48), ind(V("FLR"), V("LFL", 0, 3)), JX, A.mult)
+    ts(V("LS16", 0, 6, 2), V("SCO", 15, 48, 16), col(cFix), A.subtract)
+    tt(V("VA", 48, 96), ind(V("FLR"), V("LFL", 0, 3)), JX, A.mult)
+    seq("WH", 1)
+    seq("WH", 2)
+    local(0, "VA")
+    tr(V("WX"), V("WH", 16, 112))
+    local(1, "VA")
+    tr(V("WH", 112, 176), V("WX", 16, 80))
+    local(2, "VA")
+    scan(V("SCO"), V("MM"), V("WH", 16, 160), A.add, A.max)
+    local(3, "VA")
+    ts(V("DI", 0, 9), V("SCO", 15, 144, 16), col(cFix), A.subtract)
+    seq("HB", 1)
+    ts(V("DI", 10, 13), V("DI", 6, 9), 10, A.logical_shift_right)
+    ts(V("DI", 20, 23), V("DI", 0, 3), 1023, A.bitwise_and)
+    seq("HB", 2)
+    ts(V("LM", 4, 7), V("DI", 10, 13), col(cMb), A.subtract, col(cM0), A.mult)
+    ts(V("LM", 0, 3), V("DI", 20, 23), col(cMa), A.subtract, col(cH), A.mult)
+    tr(V("HX"), V("HB", 16, 112))
+    mid("WH", "WC")
+    tr(V("HB", 112, 176), V("HX", 16, 80))
+    act(V("RX", 192, 288), V("RX", 96, 192), F.Identity, 0.0, col(cH))
+    scan(V("SCO", 0, 96), V("MM", 0, 96), V("WC"), A.add, A.max)
+    mid("HB", "CP")
+    ts(V("DI", 0, 6), V("SCO", 15, 96, 16), col(cFix), A.subtract)
+    tt(V("RX", 288, C), V("RX", 192, 288), V("RX", 0, 96), A.add)
+    ts(V("DI", 10, 16), V("DI", 0, 6), 10, A.logical_shift_right)
+    ts(V("DI", 20, 26), V("DI", 0, 6), 1023, A.bitwise_and)
+    scan(V("MP", 0, 96), V("MM", 0, 96), V("RX", 288, C), A.add, A.max)
+    ts(V("DF", 0, 6), V("DI", 10, 16), col(cM0), A.mult, col(cTop), A.add)
+    ts(V("DF", 10, 16), V("DI", 20, 26), col(cH), A.mult)
+    ts(V("LEX"), V("MP", 15, 96, 16), col(cFix), A.subtract)
+    tt(V("DF", 30, 36), V("DF", 0, 6), V("DF", 10, 16), A.add)
+    quant(V("QU0"), V("SU0"), V("UT"))
+    for a in range(1, 4):
+        cp(V("LT", 6 * a - 6, 6 * a, 1, 0, 32), V("DF", 30, 36, 1, 32 * a, 32 * a + 32))
+    top()
+    act(V("SU"), ind(V("SU0"), V("LU")), F.Copy)
+    const(V("HT", C, 512), 0.0)
+    const(V("HT", 0, C), 0.0)
+
+    def inherit(r):
+        n = C + K * r
+        for b in (0, 1):
+            cp(V("ET", b, 4 * C, 4), ind(V("TAB", TW * b, TW * b + n), V("PTR")))
+        for b in (2, 3):
+            act(V("ET", b, 4 * C, 4), ind(V("TAB", TW * b, TW * b + n), V("PTR")), F.Copy)
+        if r == 0:
+            op("v", lambda: g.vector.tensor_copy(T.QU[:, :].bitcast(dt.uint32), ind(V("QU0"), V("LU"), True)[0]),
+               [V("QU")], [V("QU0"), V("LU")])
+            const(V("LMC"), 0.0)
+            act(V("SCN", 32, 64), V("SCN", 0, 32), F.Copy)
+            const(V("HR"), 16.0)
+            act(V("SCN", 64, 128), V("SCN", 0, 64), F.Copy)
+            const(V("HR", 0, 128, 4), 0.0)
+        quant(V("QE%d" % r), V("SE%d" % r), V("ET"))
+
+    vin, vout = "VA", "VB"
+    for r, h in enumerate(DIST):
+        dst = T.cores[(rank - h) % N]
+        qe, se = V("QE%d" % r), V("SE%d" % r)
+        inherit(r)
+        mm(V("PK", 0, C), V("QU"), V("SU"), qe, se)
+        if r == 0:
+            scan(V("MP", 96, 144), V("MM", 0, 48), V("RTX"), A.add, A.max)
+            quant(V("LQ", 0, 128), V("LS", 0, 128), V("HT"))
+            ts(V("LTX", 0, 3), V("MP", 111, 144, 16), col(cFix), A.subtract)
+        for b in range(4):
+            mm(V("PH%d" % b, 0, C), V("QW", 128 * b, 128 * b + 128), V("SW", 128 * b, 128 * b + 128), qe, se)
+        ts(V("SK", 0, 96), V("PK", 0, C, 4), 0.0, A.is_gt, col(cWk), A.mult)
+        ts(V("SK", 96, 112), V("PK", 0, 64, 4), 0.0, A.is_gt, col(cWk), A.mult)
+        act(V("SG"), V("PK", 0, C), F.Sign)
+        act(V("T1H"), ind(V("SG"), V("LL")), F.Relu, None, col(cWk))
+        tr(V("YK", 0, 96), V("SK", 0, 96))
+        tr(V("YK", 96, 192), V("SK", 16, 112))
+        tt(V("ZL", 0, 96), V("YK", 0, 192, 2), V("YK", 1, 192, 2), A.add)
+        tt(V("ZL", 96, 144), V("ZL", 0, 96, 2), V("ZL", 1, 96, 2), A.add)
+        cp(V("TX%d" % r), ind(V("ZL"), V("LTX", 0, 3)))
+        send(dst, "ra%d" % r, V("AR%d" % r), V("TX%d" % r))
+        for b in range(4):
+            act(V("HT", b, C, 4), V("PH%d" % b, 0, C, 4), F.Copy, None, 0.03125)
+        if r == 0:
+            ts(V("LA"), V("IO", 0, 8), 2.0, A.mult, col(cCA), A.add)
+            ts(V("LP", 0, 4), V("IO", 0, 4), 32.0, A.mult, col(cP1), A.add)
+            ts(V("LP", 4, 8), V("IO", 0, 4), 32.0, A.mult, col(cP2), A.add)
+            ts(V("LFW"), V("R6"), 0.5, A.mult, col(cIh), A.add)
+            const(V("KD"), -1.0)
+            act(JJ, V("IO", 0, 48), F.Identity, col(cJ), 1024.0)
+            const(V("KD", 16, 288, 16), -17.0)
+            const(V("KD", 48, 288, 96), 63.0)
+            const(V("KD", 0, 288, 96), 4096.0)
+            const(V("KD", 80, 288, 96), col(cK80))
+        act(JB, JJ, F.Identity, float(C + K * r), 1.0)
+        tr(V("T2H"), V("T1H"))
+        tt(V("LMC", 0, 288, 2), V("T2H", 0, 288, 2), V("T2H", 1, 288, 2), A.add)
+        tt(V("TA", 0, 128), ind(V("LMC", 0, 128), V("LA")), V("SCN"), A.not_equal)
+        tt(V("TA", 128, 256), ind(V("LMC", 96, 224), V("LA")), V("SCN"), A.not_equal)
+        tr(V("LMH"), V("LMC", 192, 288))
+        tt(V("TA", 256, C), V("TA", 0, 128), V("TA", 128, 256), A.mult)
+        quant(V("QH%d" % r), V("SH%d" % r), V("HT"))
+        scan(V("TP"), V("HR"), V("TA", 256, C), A.mult, A.add)
+        tt(V("MP", 0, 48), V("LMH", 0, 48), V("LMH", 48, 96), A.is_equal)
+        cp(V("TQ"), ind(V("TP"), V("LP", 0, 4)))
+        ts(V("MP", 48, 96), V("MP", 0, 48), 100.0, A.mult)
+        tt(V("TT"), ind(V("TP"), V("LP", 4, 8)), V("TQ"), A.add)
+        tt(V("MP", 96, 144), V("MP", 48, 96), V("LMH", 48, 96), A.add)
+        lo = 128 + K * r
+        send(dst, "rh%d" % r, u8(V("LQ", lo, lo + K)), u8(V("QH%d" % r, 0, K)))
+        send(dst, "rh%d" % r, V("LS", lo, lo + K), V("SH%d" % r, 0, K))
+        if r == 0:
+            for b in range(4):
+                quant(V("QC", 128 * b, 128 * b + 128), V("SC", 128 * b, 128 * b + 128), V("EC", 3 - b, 515 - b))
+        if r == 1:
+            quant(V("QV"), V("SV"), V("VT"))
+        ar = "AR%d" % r
+        cp(V("RF"), V(ar, 24, 48))
+        cp(V("AC", 0, 96), ind(V("TT", 0, 16), V(ar, 0, 6)))
+        act(V("XF"), ind(V("RF"), V("LFW")), F.Copy)
+        tt(V("AC", 96, 192), ind(V("TT", 16, 32), V(ar, 6, 12)), V("AC", 0, 96), A.add)
+        tt(V("AC", 192, 288), ind(V("TT", 32, 48), V(ar, 12, 18)), V("AC", 96, 192), A.add)
+        tt(V("ACI"), ind(V("TT", 48, 64), V(ar, 18, 24)), V("AC", 192, 288), A.add)
+        for c in range(3):
+            ts(V("CHI", 96 * c, 96 * c + 96), V("ACI"), 8 - 4 * c, A.logical_shift_right, 15, A.bitwise_and)
+        ts(V("CHF"), V("CHI"), 128.0, A.mult)
+        scan(V("CHS"), V("KD"), V("CHF"), A.add, A.min)
+        tr(V("FW"), V("XF"))
+        ts(V("KI", 0, 3), V("CHS", 95, 288, 96), col(cKl), A.add)
+        ts(V("KI", 4, 7), V("KI", 0, 3), 127, A.bitwise_and)
+        cp(V("KL", 0, 3), V("KI", 4, 7))
+        for b in range(4):
+            mm(V("PH%d" % b, 0, 128), V("QC", 128 * b, 128 * b + 128), V("SC", 128 * b, 128 * b + 128),
+               V("LQ", lo - 32, lo + K), V("LS", lo - 32, lo + K))
+        for b in range(4):
+            act(V("TAB", TW * b + C + K * r, TW * b + C + K * r + K), V("PH%d" % b, 32, 128), F.Copy)
+        kl = V("KL", 0, 3)
+        tt(V("UP", 0, 48), ind(V("IO", 0, 96), kl), JB, A.add)
+        tt(V("UP", 48, 96), ind(V("FW"), kl), V("LMH", 0, 48), A.not_equal)
+        tt(V("UP", 96, 144), ind(V("FW"), kl), V("MP", 96, 144), A.not_equal)
+        tt(V("UP", 144, 192), V("UP", 0, 48), V("UP", 48, 96), A.mult)
+        tt(V("UP", 192, 240), V("UP", 144, 192), V(vin, 0, 48), A.max)
+        tt(V(vout, 0, 48), V("UP", 192, 240), V("UP", 96, 144), A.mult)
+        tt(V(vout, 48, 96), V("UP", 192, 240), V("UP", 96, 144), A.mult)
+        vin, vout = vout, vin
+        for k in range(4):
+            local(k, vin)
+            if k == 0 and r == 2:
+                act(V("OF"), V(vin, 0, 48), F.Sign)
+                for G in range(8):
+                    dma("y", "dout", T.ofl[:, 48 * G:48 * G + 48], V("OF", 0, 48, 1, 16 * G, 16 * G + 16, 2))
+        seq("HB", 1)
+        seq("HB", 2)
+        swap("HB", "HX")
+        mid("HB", "CP")
+        top()
+
+    n = C + K * 3
+    for half, name in enumerate(("PK", "PA")):
+        lo, hi = 192 * half, 192 * half + 192
+        off = V("PTR", 12 * half, 12 * half + 12)
+        for b in (0, 1):
+            cp(V("ET", 4 * lo + b, 4 * hi, 4), ind(V("TAB", TW * b, TW * b + n), off))
+        for b in (2, 3):
+            act(V("ET", 4 * lo + b, 4 * hi, 4), ind(V("TAB", TW * b, TW * b + n), off), F.Copy)
+        quant(V("QE3", lo, hi), V("SE3", lo, hi), V("ET", 4 * lo, 4 * hi))
+        mm(V(name, 0, 192), V("QV"), V("SV"), V("QE3", lo, hi), V("SE3", lo, hi))
+        dma("y", "dend", T.oc[:, 4 * lo:4 * hi], u8(V("QE3", lo, hi)))
+    act(V("YO", 0, 192), V("PK", 0, 192), F.Copy)
+    cp(V("YO", 192, C), V("PA", 0, 192))
+    dma("s", "dend", T.y[:, 0:192], V("YO", 0, 192))
+    for k in range(4):
+        dma("y" if k % 2 else "s", "dend", T.osc[4 * k:4 * k + 4, :], V("SE3", 0, C, 1, 32 * k, 32 * k + 4))
+    dma("y", "dend", T.y[:, 192:C], V("YO", 192, C))
+    for sem in SEMAPHORES:
+        if total[sem]:
+            wait("g", sem, total[sem])

@@ -18,19 +18,18 @@ SCRATCH = {
     "SV": _sb(128, U8), "QW": _sb(512, FP8), "SW": _sb(512, U8), "QC": _sb(512, FP8), "SC": _sb(512, U8),
     "LQ": _sb(128 + 3 * K, FP8), "LS": _sb(128 + 3 * K, U8),
     "PI": _sb(1, I32), "CI": _sb(12, I32), "CF": _sb(40, F32),
-    "T16": _sb(144, F32), "M1": _sb(288, F32), "MM": _sb(144, F32), "IO": _sb(C, F32),
+    "T16": _sb(144, F32), "M1": _sb(288, F32), "MM": _sb(144, F32), "IO": _sb(96, F32),
     "PT": _sb(C, F32), "R6": _sb(6, F32), "RTX": _sb(48, F32), "RX": _sb(C, F32), "SCN": _sb(128, F32),
-    "HR": _sb(128, F32), "KD": _sb(288, F32), "JJ": _sb(144, F32), "SELF": _sb(8, F32),
+    "HR": _sb(128, F32), "KD": _sb(96, F32), "JJ": _sb(144, F32), "D01": _sb(192, F32),
     "LPAR": _sb(2, U16), "LU": _sb(8, U16), "LA": _sb(8, U16), "LP": _sb(8, U16), "LTX": _sb(4, U16),
     "LFW": _sb(6, U16), "LL": _sb(18, U16), "LFL": _sb(4, U16), "LEX": _sb(6, U16), "PU": _sb(4, U16),
-    "PL": _sb(16, U16), "LS16": _sb(6, U16), "LM": _sb(8, U16), "LT": _sb(18, U16), "KL": _sb(4, U16),
-    "PTR": _sb(24, U16),
-    "PR": _sb(32, I32), "PF": _sb(16, F32), "PD": _sb(16, F32), "FLR": _sb(C, I32),
-    "RA": _sb(96, F32), "SCO": _sb(144, F32), "WA": _sb(96, F32), "DA": _sb(144, F32),
+    "PL": _sb(24, U16), "LM": _sb(8, U16), "LT": _sb(18, U16), "KL": _sb(4, U16), "PTR": _sb(24, U16),
+    "PR": _sb(32, I32), "PF": _sb(16, F32), "FLR": _sb(C, I32),
+    "RA": _sb(128, F32), "SCO": _sb(144, F32), "WA": _sb(128, F32), "WB": _sb(128, F32),
     "WH": _sb(176, F32), "WX": _sb(96, F32), "WC": _sb(96, F32), "DI": _sb(32, I32), "DF": _sb(48, F32),
-    "VA": _sb(96, F32), "VB": _sb(96, F32), "AA": _sb(96, F32), "AB": _sb(96, F32), "HB": _sb(176, F32),
+    "VA": _sb(128, F32), "VB": _sb(128, F32), "AA": _sb(128, F32), "AB": _sb(128, F32), "HB": _sb(176, F32),
     "HX": _sb(96, F32), "CP": _sb(C, F32), "YY": _sb(C, F32), "OI": _sb(96, I32), "OJ": _sb(96, I32),
-    "SK": _sb(112, BF), "YK": _sb(192, BF), "ZL": _sb(144, F32),
+    "SK": _sb(112, BF), "YK": _sb(192, BF), "ZL": _sb(192, F32),
     "SG": _sb(C, BF), "T1H": _sb(288, BF), "T2H": _sb(288, BF), "LMH": _sb(96, BF), "LMC": _sb(288, BF),
     "TA": _sb(C, F32), "TP": _sb(128, F32), "TQ": _sb(64, F32), "TT": _sb(64, F32), "MP": _sb(144, F32),
     "AC": _sb(288, F32), "ACI": _sb(96, I32), "CHI": _sb(288, I32), "CHF": _sb(288, F32), "CHS": _sb(288, F32),
@@ -198,14 +197,13 @@ def rank_program(g, core, T, topo):
     dma("y", "dv", V("VT"), T.v[:, :])
 
     iota(V("PI"), [[0, 1]], 0, 1, False)
-    iota(V("IO", 0, 96), [[1, 96]], 0)
+    iota(V("IO"), [[1, 96]], 0)
     iota(V("T16"), [[0, 9], [1, 16]], 0)
     iota(V("PT", 0, 48), [[-16384 - 16, 3], [-1023, 16]], 1024 * 1024 + 80)
     iota(V("PT", 48, 96), [[-16384 + 16, 3], [-1023, 16]], (1024 - 48) * 1024)
     iota(V("R6"), [[16, 3], [0, 2]], 0)
-    iota(V("IO", 96, C), [[1, C - 96]], 96)
-    iota(V("RTX", 0, 24), [[1, 4], [8, 6]], 96)
-    iota(V("RTX", 24, 48), [[16, 3], [1, 8]], 0)
+    iota(V("RTX", 0, 24), [[4, 4], [32, 6]], 3)
+    iota(V("RTX", 24, 48), [[32, 3], [2, 8]], 1)
     for s in range(6):
         iota(V("RX", s, 96, 6), [[4, 4], [96, 4]], 16 * [0, 5, 2, 1, 4, 3][s])
         iota(V("RX", 96 + s, 192, 6), [[0, 16]], 16 * ([5, 0, 3, 2, 1, 4][s] - [0, 5, 2, 1, 4, 3][s]) + 2)
@@ -220,68 +218,65 @@ def rank_program(g, core, T, topo):
         ts(V("CI", k, k + 1), V("PI"), sh, A.logical_shift_right, m, A.bitwise_and)
     ms(V("LT"), 0)
     cp(V("CF", 0, 10), V("CI", 0, 10))
-    (cG48, cI1, cFix, cG3, cFl, cK1, cK2, cWk, cM0, cKl, cK80, cMa, cMb, cD, cTop, cJ, cJx, cUk, cCA,
-     cP1, cP2, cLk) = range(10, 32)
+    (cI1, cFix, cG3, cFl, cK1, cK2, cWk, cM0, cKl, cK80, cMa, cMb, cD, cTop, cJ, cJx, cUk, cCA,
+     cP1, cP2, cLk) = range(10, 31)
     JJ, JX, JB = V("JJ", 0, 48), V("JJ", 48, 96), V("JJ", 96, 144)
     ms(V("WH", 0, 16), 0.0)
+    ms(V("RA"), 0.0)
     ts(col(cI1), col(cI), 1.0, A.add)
-    ts(col(cG48), col(cG), 48.0, A.mult)
+    ts(col(cD), col(cG), -48.0, A.mult, 16.0, A.add)
     ts(V("LPAR", 0, 1), col(cG), 3.0, A.mult, col(cI3), A.add)
     ts(col(cFix), col(cI), 15.0, A.is_lt, BIG, A.mult)
-    ts(V("SELF", 0, 3), V("IO", 0, 3), 16.0, A.mult, col(cI), A.add)
-    ts(V("SELF", 4, 7), V("IO", 0, 3), 16.0, A.mult, col(cG48), A.add)
 
     def columns(rows):
         for k, src, sc, bi in rows:
             act(col(k), col(src), F.Identity, bi, sc)
 
-    columns([(cUk, cIh, 16.0, col(cB0)), (cG3, cG, 3.0, 0.0), (cLk, cG, 48.0, col(cI)), (cJx, cG, 49200.0, 1024.0),
-             (cFl, cI, 24.0, col(cG3)), (cD, cG, -48.0, 16.0)])
+    def const(o, c):
+        act(o, V("PT", 0, len(o[1][0][3])), F.Identity, c, 0.0)
+
     for a in range(1, 4):
         act(V("PT", 96 * a, 96 * a + 96), V("PT", 0, 96), F.Identity, float(-96 * a * 1023), 1.0)
+    columns([(cUk, cIh, 16.0, col(cB0)), (cG3, cG, 3.0, 0.0), (cLk, cG, 48.0, col(cI)), (cJx, cG, 49200.0, 1024.0),
+             (cFl, cI, 24.0, col(cG3))])
+    for name in ("WA", "WB", "VA", "AA", "AB", "VB"):
+        for lo in (0, 64):
+            const(V(name, lo, lo + 16), 0.0)
+    ts(V("M1", 0, 144), V("T16"), col(cI), A.is_equal, -3.0 * BIG, A.mult)
+    ts(V("M1", 144, 288), V("T16"), col(cI1), A.is_equal, BIG, A.mult)
+
+    ms(V("WH", 96, 112), 0.0)
+    tt(V("MM", 0, 48), V("M1", 0, 48), V("M1", 144, 192), A.add)
+    for a in range(1, 4):
+        cp(V("PR", 0, 24, 1, 32 * a, 32 * a + 32), V("PR", 0, 24, 1, 0, 32))
+    ms(V("HB", 0, 16), 0.0)
+    cp(V("PF"), ind(V("PR"), V("LPAR", 0, 1)))
+    ms(V("HB", 96, 112), 0.0)
+    ts(V("PL", 0, 3), V("PF", 0, 3), col(cD), A.add)
+    cp(V("PU", 0, 3), V("PF", 0, 3))
+    cp(V("RA", 16, 64), ind(V("IO", 0, 64), V("PL", 0, 3)))
+    for lo in (16, 80):
+        act(V("WA", lo, lo + 48), ind(V("PT"), V("PU", 0, 3)), F.Copy)
     act(JX, V("IO", 0, 48), F.Identity, col(cJx), 1025.0)
     columns([(cM0, cH, 1.0, -1.0), (cMa, cA, 96.0, 32.0), (cTop, cH16, -64.0, 1024.0),
              (cMb, cA, -96.0, 1040.0), (cK1, cB0, -1.0, 2.0), (cK2, cB1, -3.0, 4.0),
              (cKl, cH16, -5.0, 95.0), (cK80, cH16, 6.0, -17.0), (cJ, cG, 49152.0, 1024.0),
              (cCA, cI3, 32.0, col(cH16)), (cP1, cI12, 1.0, 2.0), (cP2, cI3, 4.0, 18.0), (cWk, cK1, col(cK2), 0.0)])
-    ts(V("M1", 0, 144), V("T16"), col(cI), A.is_equal, -3.0 * BIG, A.mult)
-    ts(V("M1", 144, 288), V("T16"), col(cI1), A.is_equal, BIG, A.mult)
-
-    def const(o, c):
-        act(o, V("PT", 0, len(o[1][0][3])), F.Identity, c, 0.0)
-
-    for a in range(1, 4):
-        cp(V("PR", 0, 24, 1, 32 * a, 32 * a + 32), V("PR", 0, 24, 1, 0, 32))
-    tt(V("MM", 0, 48), V("M1", 0, 48), V("M1", 144, 192), A.add)
-    cp(V("PF"), ind(V("PR"), V("LPAR", 0, 1)))
-    ms(V("WH", 96, 112), 0.0)
-    tt(V("PD", 4, 7), V("PF", 0, 3), V("SELF", 4, 7), A.is_lt)
-    ts(V("PD", 0, 3), V("PF", 0, 3), col(cG48), A.subtract)
-    tt(V("PD", 8, 11), V("PD", 4, 7), V("SELF", 0, 3), A.mult)
-    cp(V("PU", 0, 3), V("PF", 0, 3))
-    tt(V("PD", 12, 15), V("PD", 0, 3), V("PD", 8, 11), A.max)
-    ms(V("HB", 0, 16), 0.0)
-    cp(V("PL", 0, 3), V("PD", 12, 15))
-    ms(V("HB", 96, 112), 0.0)
-    cp(V("RA", 0, 48), ind(V("IO", 0, 48), V("PL", 0, 3)))
-    act(V("WA", 0, 48), ind(V("PT"), V("PU", 0, 3)), F.Copy)
-    act(V("DA", 0, 48), ind(V("IO"), V("PU", 0, 3)), F.Identity, col(cD), 1.0)
     const(V("CP", 96, C), 0.0)
     const(V("YY"), 0.0)
 
-    def local(k, vin):
-        src = vin if k == 0 else ("AA" if k % 2 else "AB")
+    def double(k, src, dst):
         off = V("PL", 4 * k, 4 * k + 3)
-        if k == 3:
-            tt(V("HB", 16, 64), ind(V(src, 0, 48), off), V(src, 48, 96), A.max)
-            return
-        dst = "AB" if k % 2 else "AA"
-        tt(V(dst, 0, 48), ind(V(src, 0, 48), off), V(src, 48, 96), A.max)
-        tt(V(dst, 48, 96), ind(V(src, 48, 96), off), V(src, 0, 48), A.max)
+        tt(V(dst, 16, 64), ind(V(src, 0, 64), off), V(src, 80, 128), A.max)
+        if k < 3:
+            tt(V(dst, 80, 128), ind(V(src, 64, 128), off), V(src, 16, 64), A.max)
+
+    def local(k, vin):
+        double(k, (vin, "AA", "AB", "AA")[k], ("AA", "AB", "AA", "HB")[k])
 
     def seq(hb, c):
         own = V(hb, 16 + 16 * c, 32 + 16 * c)
-        tt(own, ind(V(hb, 0, 16 + 16 * c), V("LS16", 2 * c, 2 * c + 1)), own, A.max)
+        tt(own, ind(V(hb, 0, 16 + 16 * c), V("PL", 16 + 2 * c, 17 + 2 * c)), own, A.max)
         cp(V(hb, 96 - 16 * c, 112 - 16 * c), V(hb, 16 * c, 16 * c + 16))
 
     def swap(hb, hx):
@@ -302,12 +297,10 @@ def rank_program(g, core, T, topo):
         cp(part(1), part(0, 32))
         act(part(2), part(0, 64), F.Copy)
         act(part(3), part(0, 96), F.Copy)
-        turn(0)
         for a in range(1, 4):
+            turn(a - 1)
             tt(V("CP", 96 * a, 96 * a + 96), ind(V("CP", 0, 96 * a), V("LT", 6 * a - 6, 6 * a)),
                V("CP", 96 * a, 96 * a + 96), A.max)
-            if a > 1:
-                turn(a - 1)
         turn(3)
         cp(V("OI"), ind(V("YY"), V("LEX")))
         ts(V("OJ", 0, 96, 1, 0, 32), V("OI", 0, 96, 1, 0, 32), 1023, A.bitwise_and)
@@ -317,32 +310,28 @@ def rank_program(g, core, T, topo):
     fill = [
         lambda: ts(V("LU"), V("IO", 0, 8), 0.0, A.mult, col(cUk), A.add),
         lambda: ts(V("LL", 0, 6), V("R6"), col(cLk), A.add),
-        lambda: cp(V("LL", 6, 12, 2), V("PF", 0, 3)),
         lambda: ts(V("LFL", 0, 3), V("IO", 0, 3), col(cFl), A.add),
-        lambda: cp(V("LL", 7, 12, 2), V("PF", 0, 3)),
-        lambda: ts(V("LL", 12, 15), V("R6", 0, 6, 2), col(cLk), A.add),
+        lambda: double(0, "WA", "WB"),
+        lambda: (cp(V("LL", 6, 12, 2), V("PF", 0, 3)), cp(V("LL", 7, 12, 2), V("PF", 0, 3))),
+        lambda: tt(V("MM", 48, 144), V("M1", 48, 144), V("M1", 192, 288), A.add),
+        lambda: double(1, "WB", "WA"),
+        lambda: (ts(V("LL", 12, 15), V("R6", 0, 6, 2), col(cLk), A.add), cp(V("LL", 15, 18), V("PF", 0, 3))),
+        lambda: double(2, "WA", "WB"),
+        lambda: tt(V("VA", 16, 64), ind(V("FLR"), V("LFL", 0, 3)), JX, A.mult),
+        lambda: double(3, "WB", "WH"),
+        lambda: tt(V("VA", 80, 128), ind(V("FLR"), V("LFL", 0, 3)), JX, A.mult),
     ]
-    ra, rb = V("RA", 0, 48), V("RA", 48, 96)
-    for k in range(3):
-        cp(rb, ind(ra, V("PL", 4 * k, 4 * k + 3)))
-        fill[2 * k]()
-        scan(V("SCO", 0, 48), V("MM", 0, 48), rb, A.add, A.max)
-        fill[2 * k + 1]()
-        ts(V("PL", 4 * k + 4, 4 * k + 7), V("SCO", 15, 48, 16), col(cFix), A.subtract)
+    ra, rb = 0, 64
+    for k in range(4):
+        cp(V("RA", rb + 16, rb + 64), ind(V("RA", ra, ra + 64), V("PL", 4 * k, 4 * k + 3)))
+        fill[3 * k]()
+        scan(V("SCO", 0, 48), V("MM", 0, 48), V("RA", rb + 16, rb + 64), A.add, A.max)
+        fill[3 * k + 1]()
+        ts(V("PL", 4 * k + 4, 4 * k + 7) if k < 3 else V("PL", 16, 22, 2), V("SCO", 15, 48, 16), col(cFix), A.subtract)
+        fill[3 * k + 2]()
         ra, rb = rb, ra
-    p3 = V("PL", 12, 15)
-    cp(V("DA", 48, 96), ind(V("DA", 0, 48), p3))
-    act(V("WA", 48, 96), ind(V("WA", 0, 48), p3), F.Copy)
-    tt(V("MM", 48, 144), V("M1", 48, 144), V("M1", 192, 288), A.add)
-    cp(V("DA", 96, 144), ind(V("DA", 48, 96), p3))
-    act(V("WH", 16, 64), ind(V("WA", 48, 96), p3), F.Copy)
     for b in range(4):
         act(V("TAB", TW * b, TW * b + C), V("XR", b, 4 * C, 4), F.Copy)
-    cp(V("LL", 15, 18), V("PF", 0, 3))
-    scan(V("SCO", 0, 48), V("MM", 0, 48), V("DA", 96, 144), A.add, A.max)
-    tt(V("VA", 0, 48), ind(V("FLR"), V("LFL", 0, 3)), JX, A.mult)
-    ts(V("LS16", 0, 6, 2), V("SCO", 15, 48, 16), col(cFix), A.subtract)
-    tt(V("VA", 48, 96), ind(V("FLR"), V("LFL", 0, 3)), JX, A.mult)
     seq("WH", 1)
     seq("WH", 2)
     local(0, "VA")
@@ -369,17 +358,21 @@ def rank_program(g, core, T, topo):
     tt(V("RX", 288, C), V("RX", 192, 288), V("RX", 0, 96), A.add)
     ts(V("DI", 10, 16), V("DI", 0, 6), 10, A.logical_shift_right)
     ts(V("DI", 20, 26), V("DI", 0, 6), 1023, A.bitwise_and)
-    scan(V("MP", 0, 96), V("MM", 0, 96), V("RX", 288, C), A.add, A.max)
+    quant(V("QU0"), V("SU0"), V("UT"))
     ts(V("DF", 0, 6), V("DI", 10, 16), col(cM0), A.mult, col(cTop), A.add)
     ts(V("DF", 10, 16), V("DI", 20, 26), col(cH), A.mult)
-    ts(V("LEX"), V("MP", 15, 96, 16), col(cFix), A.subtract)
+    scan(V("MP", 0, 96), V("MM", 0, 96), V("RX", 288, C), A.add, A.max)
     tt(V("DF", 30, 36), V("DF", 0, 6), V("DF", 10, 16), A.add)
-    quant(V("QU0"), V("SU0"), V("UT"))
+    op("v", lambda: g.vector.tensor_copy(T.QU[:, :].bitcast(dt.uint32), ind(V("QU0"), V("LU"), True)[0]),
+       [V("QU")], [V("QU0"), V("LU")])
     for a in range(1, 4):
         cp(V("LT", 6 * a - 6, 6 * a, 1, 0, 32), V("DF", 30, 36, 1, 32 * a, 32 * a + 32))
+    ts(V("LEX"), V("MP", 15, 96, 16), col(cFix), A.subtract)
     top()
     act(V("SU"), ind(V("SU0"), V("LU")), F.Copy)
+    const(V("D01"), 1.0)
     const(V("HT", C, 512), 0.0)
+    const(V("D01", 0, 192, 4), 0.0)
     const(V("HT", 0, C), 0.0)
 
     def inherit(r):
@@ -389,8 +382,6 @@ def rank_program(g, core, T, topo):
         for b in (2, 3):
             act(V("ET", b, 4 * C, 4), ind(V("TAB", TW * b, TW * b + n), V("PTR")), F.Copy)
         if r == 0:
-            op("v", lambda: g.vector.tensor_copy(T.QU[:, :].bitcast(dt.uint32), ind(V("QU0"), V("LU"), True)[0]),
-               [V("QU")], [V("QU0"), V("LU")])
             const(V("LMC"), 0.0)
             act(V("SCN", 32, 64), V("SCN", 0, 32), F.Copy)
             const(V("HR"), 16.0)
@@ -408,6 +399,8 @@ def rank_program(g, core, T, topo):
             scan(V("MP", 96, 144), V("MM", 0, 48), V("RTX"), A.add, A.max)
             quant(V("LQ", 0, 128), V("LS", 0, 128), V("HT"))
             ts(V("LTX", 0, 3), V("MP", 111, 144, 16), col(cFix), A.subtract)
+        if r == 1:
+            quant(V("QV"), V("SV"), V("VT"))
         for b in range(4):
             mm(V("PH%d" % b, 0, C), V("QW", 128 * b, 128 * b + 128), V("SW", 128 * b, 128 * b + 128), qe, se)
         ts(V("SK", 0, 96), V("PK", 0, C, 4), 0.0, A.is_gt, col(cWk), A.mult)
@@ -416,8 +409,7 @@ def rank_program(g, core, T, topo):
         act(V("T1H"), ind(V("SG"), V("LL")), F.Relu, None, col(cWk))
         tr(V("YK", 0, 96), V("SK", 0, 96))
         tr(V("YK", 96, 192), V("SK", 16, 112))
-        tt(V("ZL", 0, 96), V("YK", 0, 192, 2), V("YK", 1, 192, 2), A.add)
-        tt(V("ZL", 96, 144), V("ZL", 0, 96, 2), V("ZL", 1, 96, 2), A.add)
+        scan(V("ZL"), V("D01"), V("YK"), A.mult, A.add)
         cp(V("TX%d" % r), ind(V("ZL"), V("LTX", 0, 3)))
         send(dst, "ra%d" % r, V("AR%d" % r), V("TX%d" % r))
         for b in range(4):
@@ -429,18 +421,21 @@ def rank_program(g, core, T, topo):
             ts(V("LFW"), V("R6"), 0.5, A.mult, col(cIh), A.add)
             const(V("KD"), -1.0)
             act(JJ, V("IO", 0, 48), F.Identity, col(cJ), 1024.0)
-            const(V("KD", 16, 288, 16), -17.0)
-            const(V("KD", 48, 288, 96), 63.0)
-            const(V("KD", 0, 288, 96), 4096.0)
-            const(V("KD", 80, 288, 96), col(cK80))
+            const(V("KD", 16, 96, 16), -17.0)
+            const(V("KD", 0, 1), 4096.0)
+            const(V("KD", 48, 49), 63.0)
+            const(V("KD", 80, 81), col(cK80))
         act(JB, JJ, F.Identity, float(C + K * r), 1.0)
-        tr(V("T2H"), V("T1H"))
-        tt(V("LMC", 0, 288, 2), V("T2H", 0, 288, 2), V("T2H", 1, 288, 2), A.add)
+        for x in range(3):
+            tr(V("T2H", 96 * x, 96 * x + 96), V("T1H", 96 * x, 96 * x + 96))
+        for x in range(3):
+            tt(V("LMC", 96 * x, 96 * x + 96, 2), V("T2H", 96 * x, 96 * x + 96, 2),
+               V("T2H", 96 * x + 1, 96 * x + 96, 2), A.add)
         tt(V("TA", 0, 128), ind(V("LMC", 0, 128), V("LA")), V("SCN"), A.not_equal)
         tt(V("TA", 128, 256), ind(V("LMC", 96, 224), V("LA")), V("SCN"), A.not_equal)
-        tr(V("LMH"), V("LMC", 192, 288))
-        tt(V("TA", 256, C), V("TA", 0, 128), V("TA", 128, 256), A.mult)
         quant(V("QH%d" % r), V("SH%d" % r), V("HT"))
+        tt(V("TA", 256, C), V("TA", 0, 128), V("TA", 128, 256), A.mult)
+        tr(V("LMH"), V("LMC", 192, 288))
         scan(V("TP"), V("HR"), V("TA", 256, C), A.mult, A.add)
         tt(V("MP", 0, 48), V("LMH", 0, 48), V("LMH", 48, 96), A.is_equal)
         cp(V("TQ"), ind(V("TP"), V("LP", 0, 4)))
@@ -453,41 +448,44 @@ def rank_program(g, core, T, topo):
         if r == 0:
             for b in range(4):
                 quant(V("QC", 128 * b, 128 * b + 128), V("SC", 128 * b, 128 * b + 128), V("EC", 3 - b, 515 - b))
-        if r == 1:
-            quant(V("QV"), V("SV"), V("VT"))
         ar = "AR%d" % r
-        cp(V("RF"), V(ar, 24, 48))
         cp(V("AC", 0, 96), ind(V("TT", 0, 16), V(ar, 0, 6)))
+        cp(V("AC", 96, 192), ind(V("TT", 16, 32), V(ar, 6, 12)))
+        tt(V("AC", 192, 288), ind(V("TT", 32, 48), V(ar, 12, 18)), V("AC", 0, 96), A.add)
+        tt(V("CHS", 0, 96), ind(V("TT", 48, 64), V(ar, 18, 24)), V("AC", 96, 192), A.add)
+        cp(V("RF"), V(ar, 24, 48))
+        tt(V("ACI"), V("AC", 192, 288), V("CHS", 0, 96), A.add)
+        tt(V("RF", 1, 24, 2), V("RF", 1, 24, 2), V("RF", 0, 24, 2), A.subtract)
         act(V("XF"), ind(V("RF"), V("LFW")), F.Copy)
-        tt(V("AC", 96, 192), ind(V("TT", 16, 32), V(ar, 6, 12)), V("AC", 0, 96), A.add)
-        tt(V("AC", 192, 288), ind(V("TT", 32, 48), V(ar, 12, 18)), V("AC", 96, 192), A.add)
-        tt(V("ACI"), ind(V("TT", 48, 64), V(ar, 18, 24)), V("AC", 192, 288), A.add)
         for c in range(3):
             ts(V("CHI", 96 * c, 96 * c + 96), V("ACI"), 8 - 4 * c, A.logical_shift_right, 15, A.bitwise_and)
-        ts(V("CHF"), V("CHI"), 128.0, A.mult)
-        scan(V("CHS"), V("KD"), V("CHF"), A.add, A.min)
+        for c in range(3):
+            ts(V("CHF", 96 * c, 96 * c + 96), V("CHI", 96 * c, 96 * c + 96), 256.0, A.mult, col(cKl), A.add)
+        for c in range(3):
+            scan(V("CHS", 96 * c, 96 * c + 96), V("KD"), V("CHF", 96 * c, 96 * c + 96), A.add, A.min)
+        for c in range(3):
+            ts(V("KI", c, c + 1), V("CHS", 96 * c + 95, 96 * c + 96), 1.0 / 256.0, A.mult)
         tr(V("FW"), V("XF"))
-        ts(V("KI", 0, 3), V("CHS", 95, 288, 96), col(cKl), A.add)
-        ts(V("KI", 4, 7), V("KI", 0, 3), 127, A.bitwise_and)
-        cp(V("KL", 0, 3), V("KI", 4, 7))
+        for c in range(3):
+            ts(V("KL", c, c + 1), V("KI", c, c + 1), -256.0, A.mult, V("CHS", 96 * c + 95, 96 * c + 96), A.add)
         for b in range(4):
             mm(V("PH%d" % b, 0, 128), V("QC", 128 * b, 128 * b + 128), V("SC", 128 * b, 128 * b + 128),
                V("LQ", lo - 32, lo + K), V("LS", lo - 32, lo + K))
         for b in range(4):
             act(V("TAB", TW * b + C + K * r, TW * b + C + K * r + K), V("PH%d" % b, 32, 128), F.Copy)
         kl = V("KL", 0, 3)
-        tt(V("UP", 0, 48), ind(V("IO", 0, 96), kl), JB, A.add)
+        tt(V("UP", 0, 48), ind(V("IO"), kl), JB, A.add)
         tt(V("UP", 48, 96), ind(V("FW"), kl), V("LMH", 0, 48), A.not_equal)
         tt(V("UP", 96, 144), ind(V("FW"), kl), V("MP", 96, 144), A.not_equal)
         tt(V("UP", 144, 192), V("UP", 0, 48), V("UP", 48, 96), A.mult)
-        tt(V("UP", 192, 240), V("UP", 144, 192), V(vin, 0, 48), A.max)
-        tt(V(vout, 0, 48), V("UP", 192, 240), V("UP", 96, 144), A.mult)
-        tt(V(vout, 48, 96), V("UP", 192, 240), V("UP", 96, 144), A.mult)
+        tt(V("UP", 192, 240), V("UP", 144, 192), V(vin, 16, 64), A.max)
+        tt(V(vout, 16, 64), V("UP", 192, 240), V("UP", 96, 144), A.mult)
+        tt(V(vout, 80, 128), V("UP", 192, 240), V("UP", 96, 144), A.mult)
         vin, vout = vout, vin
         for k in range(4):
             local(k, vin)
             if k == 0 and r == 2:
-                act(V("OF"), V(vin, 0, 48), F.Sign)
+                act(V("OF"), V(vin, 16, 64), F.Sign)
                 for G in range(8):
                     dma("y", "dout", T.ofl[:, 48 * G:48 * G + 48], V("OF", 0, 48, 1, 16 * G, 16 * G + 16, 2))
         seq("HB", 1)
@@ -510,9 +508,9 @@ def rank_program(g, core, T, topo):
     act(V("YO", 0, 192), V("PK", 0, 192), F.Copy)
     cp(V("YO", 192, C), V("PA", 0, 192))
     dma("s", "dend", T.y[:, 0:192], V("YO", 0, 192))
-    for k in range(4):
-        dma("y" if k % 2 else "s", "dend", T.osc[4 * k:4 * k + 4, :], V("SE3", 0, C, 1, 32 * k, 32 * k + 4))
     dma("y", "dend", T.y[:, 192:C], V("YO", 192, C))
+    for k in range(4):
+        dma("s", "dend", T.osc[4 * k:4 * k + 4, :], V("SE3", 0, C, 1, 32 * k, 32 * k + 4))
     for sem in SEMAPHORES:
         if total[sem]:
             wait("g", sem, total[sem])

@@ -4,6 +4,8 @@ C, K = 384, 96
 DIST = [1, 2, 3]
 TW = C + 3 * K
 BIG = float(2 ** 21)
+S = 1.0 / BIG
+CUT = 256
 FP8, U8, U16, I32, F32, BF = "float8_e4m3fn_x4", "uint8", "uint16", "int32", "float32", "bfloat16"
 
 
@@ -20,7 +22,7 @@ SCRATCH = {
     "PI": _sb(1, I32), "CI": _sb(12, I32), "CF": _sb(40, F32),
     "T16": _sb(144, F32), "M1": _sb(288, F32), "MM": _sb(144, F32), "IO": _sb(96, F32),
     "PT": _sb(C, F32), "R6": _sb(6, F32), "RTX": _sb(48, F32), "RX": _sb(C, F32), "SCN": _sb(128, F32),
-    "HR": _sb(128, F32), "KD": _sb(96, F32), "JJ": _sb(144, F32), "D01": _sb(192, F32),
+    "HR": _sb(128, F32), "KD": _sb(96, F32), "JJ": _sb(240, F32), "D01": _sb(192, F32),
     "LPAR": _sb(2, U16), "LU": _sb(8, U16), "LA": _sb(8, U16), "LP": _sb(8, U16), "LTX": _sb(4, U16),
     "LFW": _sb(6, U16), "LL": _sb(18, U16), "LFL": _sb(4, U16), "LEX": _sb(6, U16), "PU": _sb(4, U16),
     "PL": _sb(24, U16), "LM": _sb(8, U16), "LT": _sb(18, U16), "KL": _sb(4, U16), "PTR": _sb(24, U16),
@@ -220,12 +222,12 @@ def rank_program(g, core, T, topo):
     cp(V("CF", 0, 10), V("CI", 0, 10))
     (cI1, cFix, cG3, cFl, cK1, cK2, cWk, cM0, cKl, cK80, cMa, cMb, cD, cTop, cJ, cJx, cUk, cCA,
      cP1, cP2, cLk) = range(10, 31)
-    JJ, JX, JB = V("JJ", 0, 48), V("JJ", 48, 96), V("JJ", 96, 144)
+    JJ, JX, JB, JK = V("JJ", 0, 48), V("JJ", 48, 96), V("JJ", 96, 144), V("JJ", 144, 240)
     ms(V("WH", 0, 16), 0.0)
     ms(V("RA"), 0.0)
     ts(col(cI1), col(cI), 1.0, A.add)
-    ts(col(cD), col(cG), -48.0, A.mult, 16.0, A.add)
     ts(V("LPAR", 0, 1), col(cG), 3.0, A.mult, col(cI3), A.add)
+    ts(col(cD), col(cG), -48.0, A.mult, 16.0, A.add)
     ts(col(cFix), col(cI), 15.0, A.is_lt, BIG, A.mult)
 
     def columns(rows):
@@ -235,32 +237,35 @@ def rank_program(g, core, T, topo):
     def const(o, c):
         act(o, V("PT", 0, len(o[1][0][3])), F.Identity, c, 0.0)
 
+    columns([(cUk, cIh, 16.0, col(cB0)), (cG3, cG, 3.0, 0.0), (cLk, cG, 48.0, col(cI)),
+             (cJx, cG, 49200.0 * S, 1024.0 * S), (cFl, cI, 24.0, col(cG3))])
     for a in range(1, 4):
         act(V("PT", 96 * a, 96 * a + 96), V("PT", 0, 96), F.Identity, float(-96 * a * 1023), 1.0)
-    columns([(cUk, cIh, 16.0, col(cB0)), (cG3, cG, 3.0, 0.0), (cLk, cG, 48.0, col(cI)), (cJx, cG, 49200.0, 1024.0),
-             (cFl, cI, 24.0, col(cG3))])
     for name in ("WA", "WB", "VA", "AA", "AB", "VB"):
         for lo in (0, 64):
             const(V(name, lo, lo + 16), 0.0)
     ts(V("M1", 0, 144), V("T16"), col(cI), A.is_equal, -3.0 * BIG, A.mult)
     ts(V("M1", 144, 288), V("T16"), col(cI1), A.is_equal, BIG, A.mult)
 
-    ms(V("WH", 96, 112), 0.0)
-    tt(V("MM", 0, 48), V("M1", 0, 48), V("M1", 144, 192), A.add)
     for a in range(1, 4):
         cp(V("PR", 0, 24, 1, 32 * a, 32 * a + 32), V("PR", 0, 24, 1, 0, 32))
+    tt(V("MM", 0, 48), V("M1", 0, 48), V("M1", 144, 192), A.add)
     ms(V("HB", 0, 16), 0.0)
     cp(V("PF"), ind(V("PR"), V("LPAR", 0, 1)))
     ms(V("HB", 96, 112), 0.0)
+    ms(V("WH", 96, 112), 0.0)
     ts(V("PL", 0, 3), V("PF", 0, 3), col(cD), A.add)
     cp(V("PU", 0, 3), V("PF", 0, 3))
+    cp(V("LL", 6, 12, 2), V("PF", 0, 3))
     cp(V("RA", 16, 64), ind(V("IO", 0, 64), V("PL", 0, 3)))
+    cp(V("LL", 7, 12, 2), V("PF", 0, 3))
+    cp(V("LL", 15, 18), V("PF", 0, 3))
     for lo in (16, 80):
         act(V("WA", lo, lo + 48), ind(V("PT"), V("PU", 0, 3)), F.Copy)
-    act(JX, V("IO", 0, 48), F.Identity, col(cJx), 1025.0)
+    act(JX, V("IO", 0, 48), F.Identity, col(cJx), 1025.0 * S)
     columns([(cM0, cH, 1.0, -1.0), (cMa, cA, 96.0, 32.0), (cTop, cH16, -64.0, 1024.0),
              (cMb, cA, -96.0, 1040.0), (cK1, cB0, -1.0, 2.0), (cK2, cB1, -3.0, 4.0),
-             (cKl, cH16, -5.0, 95.0), (cK80, cH16, 6.0, -17.0), (cJ, cG, 49152.0, 1024.0),
+             (cKl, cH16, -5.0, 95.0), (cK80, cH16, 6.0, -17.0), (cJ, cG, 49152.0 * S, 1024.0 * S),
              (cCA, cI3, 32.0, col(cH16)), (cP1, cI12, 1.0, 2.0), (cP2, cI3, 4.0, 18.0), (cWk, cK1, col(cK2), 0.0)])
     const(V("CP", 96, C), 0.0)
     const(V("YY"), 0.0)
@@ -287,7 +292,7 @@ def rank_program(g, core, T, topo):
         tt(V(out, 0, 48), ind(V(hb, 96, 176), V("LM", 0, 3)), V(hb, 16, 64), A.max)
         tt(V(out, 48, 96), ind(V(hb, 0, 64), V("LM", 4, 7)), V(hb, 112, 160), A.max)
 
-    def top():
+    def top(beside):
         def part(a, p0=0):
             return V("CP", 96 * a, 96 * a + 96, 1, p0, p0 + 32)
 
@@ -297,12 +302,15 @@ def rank_program(g, core, T, topo):
         cp(part(1), part(0, 32))
         act(part(2), part(0, 64), F.Copy)
         act(part(3), part(0, 96), F.Copy)
+        beside()
+        turn(0)
         for a in range(1, 4):
-            turn(a - 1)
             tt(V("CP", 96 * a, 96 * a + 96), ind(V("CP", 0, 96 * a), V("LT", 6 * a - 6, 6 * a)),
                V("CP", 96 * a, 96 * a + 96), A.max)
+            if a > 1:
+                turn(a - 1)
         turn(3)
-        cp(V("OI"), ind(V("YY"), V("LEX")))
+        ts(V("OI"), ind(V("YY"), V("LEX")), BIG, A.mult)
         ts(V("OJ", 0, 96, 1, 0, 32), V("OI", 0, 96, 1, 0, 32), 1023, A.bitwise_and)
         for a in range(4):
             cp(V("PTR", 0, 24, 1, 32 * a, 32 * a + 32), V("OJ", 24 * a, 24 * a + 24, 1, 0, 32))
@@ -312,14 +320,14 @@ def rank_program(g, core, T, topo):
         lambda: ts(V("LL", 0, 6), V("R6"), col(cLk), A.add),
         lambda: ts(V("LFL", 0, 3), V("IO", 0, 3), col(cFl), A.add),
         lambda: double(0, "WA", "WB"),
-        lambda: (cp(V("LL", 6, 12, 2), V("PF", 0, 3)), cp(V("LL", 7, 12, 2), V("PF", 0, 3))),
+        lambda: ts(V("LL", 12, 15), V("R6", 0, 6, 2), col(cLk), A.add),
         lambda: tt(V("MM", 48, 144), V("M1", 48, 144), V("M1", 192, 288), A.add),
         lambda: double(1, "WB", "WA"),
-        lambda: (ts(V("LL", 12, 15), V("R6", 0, 6, 2), col(cLk), A.add), cp(V("LL", 15, 18), V("PF", 0, 3))),
-        lambda: double(2, "WA", "WB"),
         lambda: tt(V("VA", 16, 64), ind(V("FLR"), V("LFL", 0, 3)), JX, A.mult),
-        lambda: double(3, "WB", "WH"),
+        lambda: double(2, "WA", "WB"),
         lambda: tt(V("VA", 80, 128), ind(V("FLR"), V("LFL", 0, 3)), JX, A.mult),
+        lambda: double(3, "WB", "WH"),
+        lambda: local(0, "VA"),
     ]
     ra, rb = 0, 64
     for k in range(4):
@@ -334,79 +342,98 @@ def rank_program(g, core, T, topo):
         act(V("TAB", TW * b, TW * b + C), V("XR", b, 4 * C, 4), F.Copy)
     seq("WH", 1)
     seq("WH", 2)
-    local(0, "VA")
-    tr(V("WX"), V("WH", 16, 112))
     local(1, "VA")
-    tr(V("WH", 112, 176), V("WX", 16, 80))
+    tr(V("WX"), V("WH", 16, 112))
     local(2, "VA")
-    scan(V("SCO"), V("MM"), V("WH", 16, 160), A.add, A.max)
+    tr(V("WH", 112, 176), V("WX", 16, 80))
     local(3, "VA")
-    ts(V("DI", 0, 9), V("SCO", 15, 144, 16), col(cFix), A.subtract)
+    scan(V("SCO"), V("MM"), V("WH", 16, 160), A.add, A.max)
     seq("HB", 1)
+    ts(V("DI", 0, 9), V("SCO", 15, 144, 16), col(cFix), A.subtract)
+    seq("HB", 2)
     ts(V("DI", 10, 13), V("DI", 6, 9), 10, A.logical_shift_right)
     ts(V("DI", 20, 23), V("DI", 0, 3), 1023, A.bitwise_and)
-    seq("HB", 2)
+    tr(V("HX"), V("HB", 16, 112))
     ts(V("LM", 4, 7), V("DI", 10, 13), col(cMb), A.subtract, col(cM0), A.mult)
     ts(V("LM", 0, 3), V("DI", 20, 23), col(cMa), A.subtract, col(cH), A.mult)
-    tr(V("HX"), V("HB", 16, 112))
-    mid("WH", "WC")
     tr(V("HB", 112, 176), V("HX", 16, 80))
     act(V("RX", 192, 288), V("RX", 96, 192), F.Identity, 0.0, col(cH))
+    mid("WH", "WC")
+    tt(V("RX", 288, C), V("RX", 192, 288), V("RX", 0, 96), A.add)
     scan(V("SCO", 0, 96), V("MM", 0, 96), V("WC"), A.add, A.max)
     mid("HB", "CP")
     ts(V("DI", 0, 6), V("SCO", 15, 96, 16), col(cFix), A.subtract)
-    tt(V("RX", 288, C), V("RX", 192, 288), V("RX", 0, 96), A.add)
+    quant(V("QU0"), V("SU0"), V("UT"))
     ts(V("DI", 10, 16), V("DI", 0, 6), 10, A.logical_shift_right)
     ts(V("DI", 20, 26), V("DI", 0, 6), 1023, A.bitwise_and)
-    quant(V("QU0"), V("SU0"), V("UT"))
+    scan(V("MP", 0, 96), V("MM", 0, 96), V("RX", 288, C), A.add, A.max)
     ts(V("DF", 0, 6), V("DI", 10, 16), col(cM0), A.mult, col(cTop), A.add)
     ts(V("DF", 10, 16), V("DI", 20, 26), col(cH), A.mult)
-    scan(V("MP", 0, 96), V("MM", 0, 96), V("RX", 288, C), A.add, A.max)
+    ts(V("LEX"), V("MP", 15, 96, 16), col(cFix), A.subtract)
     tt(V("DF", 30, 36), V("DF", 0, 6), V("DF", 10, 16), A.add)
     op("v", lambda: g.vector.tensor_copy(T.QU[:, :].bitcast(dt.uint32), ind(V("QU0"), V("LU"), True)[0]),
        [V("QU")], [V("QU0"), V("LU")])
     for a in range(1, 4):
         cp(V("LT", 6 * a - 6, 6 * a, 1, 0, 32), V("DF", 30, 36, 1, 32 * a, 32 * a + 32))
-    ts(V("LEX"), V("MP", 15, 96, 16), col(cFix), A.subtract)
-    top()
-    act(V("SU"), ind(V("SU0"), V("LU")), F.Copy)
+    top(lambda: act(V("SU"), ind(V("SU0"), V("LU")), F.Copy))
     const(V("D01"), 1.0)
     const(V("HT", C, 512), 0.0)
     const(V("D01", 0, 192, 4), 0.0)
     const(V("HT", 0, C), 0.0)
 
-    def inherit(r):
+    PARTS = ((0, CUT, "PK"), (CUT, C, "PA"))
+
+    def inherit(r, wq, wsc, between):
         n = C + K * r
-        for b in (0, 1):
-            cp(V("ET", b, 4 * C, 4), ind(V("TAB", TW * b, TW * b + n), V("PTR")))
-        for b in (2, 3):
-            act(V("ET", b, 4 * C, 4), ind(V("TAB", TW * b, TW * b + n), V("PTR")), F.Copy)
-        if r == 0:
-            const(V("LMC"), 0.0)
-            act(V("SCN", 32, 64), V("SCN", 0, 32), F.Copy)
-            const(V("HR"), 16.0)
-            act(V("SCN", 64, 128), V("SCN", 0, 64), F.Copy)
-            const(V("HR", 0, 128, 4), 0.0)
-        quant(V("QE%d" % r), V("SE%d" % r), V("ET"))
+
+        def plane(b, part):
+            lo, hi, _bank = PARTS[part]
+            o = V("ET", 4 * lo + b, 4 * hi, 4)
+            i = ind(V("TAB", TW * b, TW * b + n), V("PTR", lo // 16, hi // 16))
+            if b < 2:
+                cp(o, i)
+            else:
+                act(o, i, F.Copy)
+
+        def product(part):
+            lo, hi, bank = PARTS[part]
+            quant(V("QE%d" % r, lo, hi), V("SE%d" % r, lo, hi), V("ET", 4 * lo, 4 * hi))
+            mm(V(bank, 0, hi - lo), wq, wsc, V("QE%d" % r, lo, hi), V("SE%d" % r, lo, hi))
+
+        for b, part in ((0, 0), (2, 0), (1, 0), (3, 0), (0, 1), (2, 1), (3, 1)):
+            plane(b, part)
+        product(0)
+        plane(1, 1)
+        between()
+        product(1)
 
     vin, vout = "VA", "VB"
     for r, h in enumerate(DIST):
         dst = T.cores[(rank - h) % N]
         qe, se = V("QE%d" % r), V("SE%d" % r)
-        inherit(r)
-        mm(V("PK", 0, C), V("QU"), V("SU"), qe, se)
+        inherit(r, V("QU"), V("SU"), lambda: None)
+        if r == 0:
+            const(V("LMC"), 0.0)
+        for b in range(4):
+            mm(V("PH%d" % b, 0, C), V("QW", 128 * b, 128 * b + 128), V("SW", 128 * b, 128 * b + 128), qe, se)
+        ts(V("SK", 0, CUT // 4), V("PK", 0, CUT, 4), 0.0, A.is_gt, col(cWk), A.mult)
+        ts(V("SK", 96, 112), V("PK", 0, 64, 4), 0.0, A.is_gt, col(cWk), A.mult)
+        act(V("SG", 0, CUT), V("PK", 0, CUT), F.Sign)
         if r == 0:
             scan(V("MP", 96, 144), V("MM", 0, 48), V("RTX"), A.add, A.max)
             quant(V("LQ", 0, 128), V("LS", 0, 128), V("HT"))
             ts(V("LTX", 0, 3), V("MP", 111, 144, 16), col(cFix), A.subtract)
         if r == 1:
             quant(V("QV"), V("SV"), V("VT"))
-        for b in range(4):
-            mm(V("PH%d" % b, 0, C), V("QW", 128 * b, 128 * b + 128), V("SW", 128 * b, 128 * b + 128), qe, se)
-        ts(V("SK", 0, 96), V("PK", 0, C, 4), 0.0, A.is_gt, col(cWk), A.mult)
-        ts(V("SK", 96, 112), V("PK", 0, 64, 4), 0.0, A.is_gt, col(cWk), A.mult)
-        act(V("SG"), V("PK", 0, C), F.Sign)
-        act(V("T1H"), ind(V("SG"), V("LL")), F.Relu, None, col(cWk))
+        ts(V("SK", CUT // 4, 96), V("PA", 0, C - CUT, 4), 0.0, A.is_gt, col(cWk), A.mult)
+        act(V("SG", CUT, C), V("PA", 0, C - CUT), F.Sign)
+        for x in range(3):
+            act(V("T1H", 96 * x, 96 * x + 96), ind(V("SG"), V("LL", 6 * x, 6 * x + 6)), F.Relu, None, col(cWk))
+        if r == 0:
+            act(V("SCN", 32, 64), V("SCN", 0, 32), F.Copy)
+            const(V("HR"), 16.0)
+            act(V("SCN", 64, 128), V("SCN", 0, 64), F.Copy)
+            const(V("HR", 0, 128, 4), 0.0)
         tr(V("YK", 0, 96), V("SK", 0, 96))
         tr(V("YK", 96, 192), V("SK", 16, 112))
         scan(V("ZL"), V("D01"), V("YK"), A.mult, A.add)
@@ -420,12 +447,13 @@ def rank_program(g, core, T, topo):
             ts(V("LP", 4, 8), V("IO", 0, 4), 32.0, A.mult, col(cP2), A.add)
             ts(V("LFW"), V("R6"), 0.5, A.mult, col(cIh), A.add)
             const(V("KD"), -1.0)
-            act(JJ, V("IO", 0, 48), F.Identity, col(cJ), 1024.0)
+            act(JJ, V("IO", 0, 48), F.Identity, col(cJ), 1024.0 * S)
+            act(JK, V("IO"), F.Identity, 0.0, S)
             const(V("KD", 16, 96, 16), -17.0)
             const(V("KD", 0, 1), 4096.0)
             const(V("KD", 48, 49), 63.0)
             const(V("KD", 80, 81), col(cK80))
-        act(JB, JJ, F.Identity, float(C + K * r), 1.0)
+        act(JB, JJ, F.Identity, float(C + K * r) * S, 1.0)
         for x in range(3):
             tr(V("T2H", 96 * x, 96 * x + 96), V("T1H", 96 * x, 96 * x + 96))
         for x in range(3):
@@ -433,9 +461,9 @@ def rank_program(g, core, T, topo):
                V("T2H", 96 * x + 1, 96 * x + 96, 2), A.add)
         tt(V("TA", 0, 128), ind(V("LMC", 0, 128), V("LA")), V("SCN"), A.not_equal)
         tt(V("TA", 128, 256), ind(V("LMC", 96, 224), V("LA")), V("SCN"), A.not_equal)
-        quant(V("QH%d" % r), V("SH%d" % r), V("HT"))
-        tt(V("TA", 256, C), V("TA", 0, 128), V("TA", 128, 256), A.mult)
         tr(V("LMH"), V("LMC", 192, 288))
+        tt(V("TA", 256, C), V("TA", 0, 128), V("TA", 128, 256), A.mult)
+        quant(V("QH%d" % r), V("SH%d" % r), V("HT"))
         scan(V("TP"), V("HR"), V("TA", 256, C), A.mult, A.add)
         tt(V("MP", 0, 48), V("LMH", 0, 48), V("LMH", 48, 96), A.is_equal)
         cp(V("TQ"), ind(V("TP"), V("LP", 0, 4)))
@@ -445,9 +473,6 @@ def rank_program(g, core, T, topo):
         lo = 128 + K * r
         send(dst, "rh%d" % r, u8(V("LQ", lo, lo + K)), u8(V("QH%d" % r, 0, K)))
         send(dst, "rh%d" % r, V("LS", lo, lo + K), V("SH%d" % r, 0, K))
-        if r == 0:
-            for b in range(4):
-                quant(V("QC", 128 * b, 128 * b + 128), V("SC", 128 * b, 128 * b + 128), V("EC", 3 - b, 515 - b))
         ar = "AR%d" % r
         cp(V("AC", 0, 96), ind(V("TT", 0, 16), V(ar, 0, 6)))
         cp(V("AC", 96, 192), ind(V("TT", 16, 32), V(ar, 6, 12)))
@@ -465,50 +490,48 @@ def rank_program(g, core, T, topo):
             scan(V("CHS", 96 * c, 96 * c + 96), V("KD"), V("CHF", 96 * c, 96 * c + 96), A.add, A.min)
         for c in range(3):
             ts(V("KI", c, c + 1), V("CHS", 96 * c + 95, 96 * c + 96), 1.0 / 256.0, A.mult)
-        tr(V("FW"), V("XF"))
         for c in range(3):
             ts(V("KL", c, c + 1), V("KI", c, c + 1), -256.0, A.mult, V("CHS", 96 * c + 95, 96 * c + 96), A.add)
-        for b in range(4):
-            mm(V("PH%d" % b, 0, 128), V("QC", 128 * b, 128 * b + 128), V("SC", 128 * b, 128 * b + 128),
-               V("LQ", lo - 32, lo + K), V("LS", lo - 32, lo + K))
-        for b in range(4):
-            act(V("TAB", TW * b + C + K * r, TW * b + C + K * r + K), V("PH%d" % b, 32, 128), F.Copy)
+        tr(V("FW"), V("XF"))
+
+        def constants(b):
+            if r == 0:
+                quant(V("QC", 128 * b, 128 * b + 128), V("SC", 128 * b, 128 * b + 128), V("EC", 3 - b, 515 - b))
+
         kl = V("KL", 0, 3)
-        tt(V("UP", 0, 48), ind(V("IO"), kl), JB, A.add)
+        tt(V("UP", 0, 48), ind(JK, kl), JB, A.add)
         tt(V("UP", 48, 96), ind(V("FW"), kl), V("LMH", 0, 48), A.not_equal)
         tt(V("UP", 96, 144), ind(V("FW"), kl), V("MP", 96, 144), A.not_equal)
-        tt(V("UP", 144, 192), V("UP", 0, 48), V("UP", 48, 96), A.mult)
-        tt(V("UP", 192, 240), V("UP", 144, 192), V(vin, 16, 64), A.max)
-        tt(V(vout, 16, 64), V("UP", 192, 240), V("UP", 96, 144), A.mult)
-        tt(V(vout, 80, 128), V("UP", 192, 240), V("UP", 96, 144), A.mult)
+        tt(V("UP", 144, 192), V("UP", 48, 96), V(vin, 16, 64), A.add)
+        tt(V("UP", 192, 240), V("UP", 0, 48), V("UP", 96, 144), A.min)
+        constants(0)
+        tt(V(vout, 16, 64), V("UP", 144, 192), V("UP", 192, 240), A.min)
+        tt(V(vout, 80, 128), V("UP", 144, 192), V("UP", 192, 240), A.min)
         vin, vout = vout, vin
         for k in range(4):
+            if k < 3:
+                constants(k + 1)
             local(k, vin)
             if k == 0 and r == 2:
                 act(V("OF"), V(vin, 16, 64), F.Sign)
                 for G in range(8):
                     dma("y", "dout", T.ofl[:, 48 * G:48 * G + 48], V("OF", 0, 48, 1, 16 * G, 16 * G + 16, 2))
+        for b in range(4):
+            mm(V("PH%d" % b, 0, 128), V("QC", 128 * b, 128 * b + 128), V("SC", 128 * b, 128 * b + 128),
+               V("LQ", lo - 32, lo + K), V("LS", lo - 32, lo + K))
         seq("HB", 1)
         seq("HB", 2)
         swap("HB", "HX")
         mid("HB", "CP")
-        top()
+        top(lambda: [act(V("TAB", TW * b + C + K * r, TW * b + C + K * r + K), V("PH%d" % b, 32, 128), F.Copy)
+                     for b in range(4)])
 
-    n = C + K * 3
-    for half, name in enumerate(("PK", "PA")):
-        lo, hi = 192 * half, 192 * half + 192
-        off = V("PTR", 12 * half, 12 * half + 12)
-        for b in (0, 1):
-            cp(V("ET", 4 * lo + b, 4 * hi, 4), ind(V("TAB", TW * b, TW * b + n), off))
-        for b in (2, 3):
-            act(V("ET", 4 * lo + b, 4 * hi, 4), ind(V("TAB", TW * b, TW * b + n), off), F.Copy)
-        quant(V("QE3", lo, hi), V("SE3", lo, hi), V("ET", 4 * lo, 4 * hi))
-        mm(V(name, 0, 192), V("QV"), V("SV"), V("QE3", lo, hi), V("SE3", lo, hi))
-        dma("y", "dend", T.oc[:, 4 * lo:4 * hi], u8(V("QE3", lo, hi)))
-    act(V("YO", 0, 192), V("PK", 0, 192), F.Copy)
-    cp(V("YO", 192, C), V("PA", 0, 192))
-    dma("s", "dend", T.y[:, 0:192], V("YO", 0, 192))
-    dma("y", "dend", T.y[:, 192:C], V("YO", 192, C))
+    inherit(3, V("QV"), V("SV"), lambda: dma("y", "dend", T.oc[:, 0:4 * CUT], u8(V("QE3", 0, CUT))))
+    dma("y", "dend", T.oc[:, 4 * CUT:4 * C], u8(V("QE3", CUT, C)))
+    act(V("YO", 0, CUT), V("PK", 0, CUT), F.Copy)
+    cp(V("YO", CUT, C), V("PA", 0, C - CUT))
+    dma("s", "dend", T.y[:, 0:CUT], V("YO", 0, CUT))
+    dma("y", "dend", T.y[:, CUT:C], V("YO", CUT, C))
     for k in range(4):
         dma("s", "dend", T.osc[4 * k:4 * k + 4, :], V("SE3", 0, C, 1, 32 * k, 32 * k + 4))
     for sem in SEMAPHORES:

@@ -21,10 +21,10 @@ SCRATCH = {
     "LQ": _sb(128 + 3 * K, FP8), "LS": _sb(128 + 3 * K, U8),
     "PI": _sb(1, I32), "CI": _sb(12, I32), "CF": _sb(40, F32),
     "T16": _sb(144, F32), "M1": _sb(288, F32), "MM": _sb(144, F32), "IO": _sb(96, F32),
-    "PT": _sb(C, F32), "R6": _sb(6, F32), "RTX": _sb(48, F32), "RX": _sb(C, F32), "SCN": _sb(128, F32),
-    "HR": _sb(128, F32), "KD": _sb(96, F32), "JJ": _sb(240, F32), "D01": _sb(192, F32),
-    "LPAR": _sb(2, U16), "LU": _sb(8, U16), "LA": _sb(8, U16), "LP": _sb(8, U16), "LTX": _sb(4, U16),
-    "LFW": _sb(6, U16), "LL": _sb(18, U16), "LFL": _sb(4, U16), "LEX": _sb(6, U16), "PU": _sb(4, U16),
+    "PT": _sb(C, F32), "R6": _sb(6, F32), "RTX": _sb(48, F32), "RX": _sb(480, F32), "SCN": _sb(192, F32),
+    "HR": _sb(96, F32), "KD": _sb(96, F32), "JJ": _sb(240, F32), "D01": _sb(192, F32),
+    "LPAR": _sb(2, U16), "LU": _sb(8, U16), "LA": _sb(12, U16), "LP": _sb(8, U16), "LTX": _sb(4, U16),
+    "LFW": _sb(6, U16), "LL": _sb(12, U16), "LFL": _sb(4, U16), "LEX": _sb(6, U16), "PU": _sb(4, U16),
     "PL": _sb(24, U16), "LM": _sb(8, U16), "LT": _sb(18, U16), "KL": _sb(4, U16), "PTR": _sb(24, U16),
     "PR": _sb(32, I32), "PF": _sb(16, F32), "FLR": _sb(C, I32),
     "RA": _sb(128, F32), "SCO": _sb(144, F32), "WA": _sb(128, F32), "WB": _sb(128, F32),
@@ -32,8 +32,8 @@ SCRATCH = {
     "VA": _sb(128, F32), "VB": _sb(128, F32), "AA": _sb(128, F32), "AB": _sb(128, F32), "HB": _sb(176, F32),
     "HX": _sb(96, F32), "CP": _sb(C, F32), "YY": _sb(C, F32), "OI": _sb(96, I32), "OJ": _sb(96, I32),
     "SK": _sb(112, BF), "YK": _sb(192, BF), "ZL": _sb(192, F32),
-    "SG": _sb(C, BF), "T1H": _sb(288, BF), "T2H": _sb(288, BF), "LMH": _sb(96, BF), "LMC": _sb(288, BF),
-    "TA": _sb(C, F32), "TP": _sb(128, F32), "TQ": _sb(64, F32), "TT": _sb(64, F32), "MP": _sb(144, F32),
+    "SG": _sb(C, BF), "T1H": _sb(192, BF), "T2H": _sb(192, BF), "LMH": _sb(288, BF), "LMC": _sb(192, BF),
+    "TA": _sb(288, F32), "TP": _sb(96, F32), "TQ": _sb(64, F32), "TT": _sb(64, F32), "MP": _sb(144, F32),
     "AC": _sb(288, F32), "ACI": _sb(96, I32), "CHI": _sb(288, I32), "CHF": _sb(288, F32), "CHS": _sb(288, F32),
     "KI": _sb(8, I32), "RF": _sb(24, F32), "XF": _sb(96, BF), "FW": _sb(96, BF), "UP": _sb(240, F32),
     "OF": _sb(48, F32), "YO": _sb(C, F32),
@@ -209,8 +209,9 @@ def rank_program(g, core, T, topo):
     for s in range(6):
         iota(V("RX", s, 96, 6), [[4, 4], [96, 4]], 16 * [0, 5, 2, 1, 4, 3][s])
         iota(V("RX", 96 + s, 192, 6), [[0, 16]], 16 * ([5, 0, 3, 2, 1, 4][s] - [0, 5, 2, 1, 4, 3][s]) + 2)
-    iota(V("SCN", 0, 16), [[4, 4], [0, 4]], 0)
-    iota(V("SCN", 16, 32), [[1, 4], [0, 4]], 0)
+    iota(V("SCN", 96, 192), [[2, 8], [0, 4], [32, 3]], 0)
+    iota(V("SCN", 0, 12), [[4, 4], [0, 3]], 0)
+    iota(V("SCN", 12, 24), [[1, 4], [0, 3]], 0)
     iota(V("ONE"), [[0, 520]], 1)
     op("g", lambda: g.affine_select(T.EC[:, :], T.ONE[:, :], [[-1, 520]], A.is_equal, 0.0, 3, 4), [V("EC")], [V("ONE")])
 
@@ -259,14 +260,14 @@ def rank_program(g, core, T, topo):
     cp(V("LL", 6, 12, 2), V("PF", 0, 3))
     cp(V("RA", 16, 64), ind(V("IO", 0, 64), V("PL", 0, 3)))
     cp(V("LL", 7, 12, 2), V("PF", 0, 3))
-    cp(V("LL", 15, 18), V("PF", 0, 3))
     for lo in (16, 80):
         act(V("WA", lo, lo + 48), ind(V("PT"), V("PU", 0, 3)), F.Copy)
     act(JX, V("IO", 0, 48), F.Identity, col(cJx), 1025.0 * S)
     columns([(cM0, cH, 1.0, -1.0), (cMa, cA, 96.0, 32.0), (cTop, cH16, -64.0, 1024.0),
              (cMb, cA, -96.0, 1040.0), (cK1, cB0, -1.0, 2.0), (cK2, cB1, -3.0, 4.0),
              (cKl, cH16, -5.0, 95.0), (cK80, cH16, 6.0, -17.0), (cJ, cG, 49152.0 * S, 1024.0 * S),
-             (cCA, cI3, 32.0, col(cH16)), (cP1, cI12, 1.0, 2.0), (cP2, cI3, 4.0, 18.0), (cWk, cK1, col(cK2), 0.0)])
+             (cCA, cH16, -1.0, col(cFix)), (cP1, cI12, 0.75, 2.0), (cP2, cI3, 3.0, 14.0), (cWk, cK1, col(cK2), 0.0)])
+    act(V("RX", 192, 288), V("RX", 96, 192), F.Identity, 0.0, col(cH))
     const(V("CP", 96, C), 0.0)
     const(V("YY"), 0.0)
 
@@ -292,35 +293,53 @@ def rank_program(g, core, T, topo):
         tt(V(out, 0, 48), ind(V(hb, 96, 176), V("LM", 0, 3)), V(hb, 16, 64), A.max)
         tt(V(out, 48, 96), ind(V(hb, 0, 64), V("LM", 4, 7)), V(hb, 112, 160), A.max)
 
-    def top(beside):
+    NA = CUT // 16
+    NB = 24 - NA
+
+    def places(lo, n, at):
+        for a in range(4):
+            cp(V("PTR", lo, lo + n, 1, 32 * a, 32 * a + 32), V("OJ", at + n * a, at + n * a + n, 1, 0, 32))
+
+    def top(beside, fills):
         def part(a, p0=0):
             return V("CP", 96 * a, 96 * a + 96, 1, p0, p0 + 32)
 
         def turn(a):
             tr(V("YY", 96 * a, 96 * a + 96, 1, 0, 32), part(a))
 
+        def step(a):
+            tt(V("CP", 96 * a, 96 * a + 96), ind(V("CP", 0, 96 * a), V("LT", 6 * a - 6, 6 * a)),
+               V("CP", 96 * a, 96 * a + 96), A.max)
+
+        def low(lo, hi):
+            ts(V("OJ", lo, hi, 1, 0, 32), V("OI", lo, hi, 1, 0, 32), 1023, A.bitwise_and)
+
         cp(part(1), part(0, 32))
         act(part(2), part(0, 64), F.Copy)
         act(part(3), part(0, 96), F.Copy)
         beside()
         turn(0)
-        for a in range(1, 4):
-            tt(V("CP", 96 * a, 96 * a + 96), ind(V("CP", 0, 96 * a), V("LT", 6 * a - 6, 6 * a)),
-               V("CP", 96 * a, 96 * a + 96), A.max)
-            if a > 1:
-                turn(a - 1)
+        step(1)
+        fills[0]()
+        step(2)
+        turn(1)
+        fills[1]()
+        turn(2)
+        step(3)
+        ts(V("OI", 0, 4 * NA), ind(V("YY", 0, 288), V("LEX", 0, NA // 4)), BIG, A.mult)
         turn(3)
-        ts(V("OI"), ind(V("YY"), V("LEX")), BIG, A.mult)
-        ts(V("OJ", 0, 96, 1, 0, 32), V("OI", 0, 96, 1, 0, 32), 1023, A.bitwise_and)
-        for a in range(4):
-            cp(V("PTR", 0, 24, 1, 32 * a, 32 * a + 32), V("OJ", 24 * a, 24 * a + 24, 1, 0, 32))
+        low(0, 4 * NA)
+        ts(V("OI", 4 * NA, 96), ind(V("YY"), V("LEX", NA // 4, 6)), BIG, A.mult)
+        places(0, NA, 0)
+        low(4 * NA, 96)
+        fills[2]()
 
     fill = [
         lambda: ts(V("LU"), V("IO", 0, 8), 0.0, A.mult, col(cUk), A.add),
         lambda: ts(V("LL", 0, 6), V("R6"), col(cLk), A.add),
         lambda: ts(V("LFL", 0, 3), V("IO", 0, 3), col(cFl), A.add),
         lambda: double(0, "WA", "WB"),
-        lambda: ts(V("LL", 12, 15), V("R6", 0, 6, 2), col(cLk), A.add),
+        lambda: ts(V("LA", 6, 12), V("IO", 0, 6), 32.0, A.mult, col(cI), A.add),
         lambda: tt(V("MM", 48, 144), V("M1", 48, 144), V("M1", 192, 288), A.add),
         lambda: double(1, "WB", "WA"),
         lambda: tt(V("VA", 16, 64), ind(V("FLR"), V("LFL", 0, 3)), JX, A.mult),
@@ -356,17 +375,19 @@ def rank_program(g, core, T, topo):
     tr(V("HX"), V("HB", 16, 112))
     ts(V("LM", 4, 7), V("DI", 10, 13), col(cMb), A.subtract, col(cM0), A.mult)
     ts(V("LM", 0, 3), V("DI", 20, 23), col(cMa), A.subtract, col(cH), A.mult)
-    tr(V("HB", 112, 176), V("HX", 16, 80))
-    act(V("RX", 192, 288), V("RX", 96, 192), F.Identity, 0.0, col(cH))
-    mid("WH", "WC")
     tt(V("RX", 288, C), V("RX", 192, 288), V("RX", 0, 96), A.add)
+    for a in range(4):
+        act(V("RX", C + NA * a, C + NA * a + NA), V("RX", 288 + 24 * a, 288 + 24 * a + NA), F.Copy)
+        act(V("RX", C + 4 * NA + NB * a, C + 4 * NA + NB * a + NB), V("RX", 288 + 24 * a + NA, 312 + 24 * a), F.Copy)
+    mid("WH", "WC")
+    tr(V("HB", 112, 176), V("HX", 16, 80))
     scan(V("SCO", 0, 96), V("MM", 0, 96), V("WC"), A.add, A.max)
     mid("HB", "CP")
     ts(V("DI", 0, 6), V("SCO", 15, 96, 16), col(cFix), A.subtract)
     quant(V("QU0"), V("SU0"), V("UT"))
     ts(V("DI", 10, 16), V("DI", 0, 6), 10, A.logical_shift_right)
     ts(V("DI", 20, 26), V("DI", 0, 6), 1023, A.bitwise_and)
-    scan(V("MP", 0, 96), V("MM", 0, 96), V("RX", 288, C), A.add, A.max)
+    scan(V("MP", 0, 96), V("MM", 0, 96), V("RX", C, 480), A.add, A.max)
     ts(V("DF", 0, 6), V("DI", 10, 16), col(cM0), A.mult, col(cTop), A.add)
     ts(V("DF", 10, 16), V("DI", 20, 26), col(cH), A.mult)
     ts(V("LEX"), V("MP", 15, 96, 16), col(cFix), A.subtract)
@@ -375,35 +396,39 @@ def rank_program(g, core, T, topo):
        [V("QU")], [V("QU0"), V("LU")])
     for a in range(1, 4):
         cp(V("LT", 6 * a - 6, 6 * a, 1, 0, 32), V("DF", 30, 36, 1, 32 * a, 32 * a + 32))
-    top(lambda: act(V("SU"), ind(V("SU0"), V("LU")), F.Copy))
-    const(V("D01"), 1.0)
-    const(V("HT", C, 512), 0.0)
-    const(V("D01", 0, 192, 4), 0.0)
-    const(V("HT", 0, C), 0.0)
+    top(lambda: (act(V("SU"), ind(V("SU0"), V("LU")), F.Copy), const(V("D01"), 1.0), const(V("HT", C, 512), 0.0),
+                 const(V("D01", 0, 192, 4), 0.0), const(V("HT", 0, C), 0.0)), [
+        lambda: (scan(V("MP", 96, 144), V("MM", 0, 48), V("RTX"), A.add, A.max),
+                 scan(V("SCO", 0, 96), V("MM", 0, 96), V("SCN", 96, 192), A.add, A.max)),
+        lambda: ts(V("LTX", 0, 3), V("MP", 111, 144, 16), col(cFix), A.subtract),
+        lambda: ts(V("LA", 0, 6), V("SCO", 15, 96, 16), col(cCA), A.subtract)])
 
     PARTS = ((0, CUT, "PK"), (CUT, C, "PA"))
 
     def inherit(r, wq, wsc, between):
         n = C + K * r
 
-        def plane(b, part):
+        def plane(b, part, f):
             lo, hi, _bank = PARTS[part]
-            o = V("ET", 4 * lo + b, 4 * hi, 4)
-            i = ind(V("TAB", TW * b, TW * b + n), V("PTR", lo // 16, hi // 16))
-            if b < 2:
-                cp(o, i)
-            else:
-                act(o, i, F.Copy)
+            f(V("ET", 4 * lo + b, 4 * hi, 4), ind(V("TAB", TW * b, TW * b + n), V("PTR", lo // 16, hi // 16)))
 
         def product(part):
             lo, hi, bank = PARTS[part]
             quant(V("QE%d" % r, lo, hi), V("SE%d" % r, lo, hi), V("ET", 4 * lo, 4 * hi))
             mm(V(bank, 0, hi - lo), wq, wsc, V("QE%d" % r, lo, hi), V("SE%d" % r, lo, hi))
 
-        for b, part in ((0, 0), (2, 0), (1, 0), (3, 0), (0, 1), (2, 1), (3, 1)):
-            plane(b, part)
+        def scalar(o, i):
+            act(o, i, F.Copy)
+
+        plane(2, 0, scalar)
+        plane(3, 0, scalar)
+        plane(0, 0, cp)
+        places(NA, NB, 4 * NA)
+        plane(1, 0, cp)
+        for b in (2, 3, 1):
+            plane(b, 1, scalar)
+        plane(0, 1, cp)
         product(0)
-        plane(1, 1)
         between()
         product(1)
 
@@ -416,36 +441,34 @@ def rank_program(g, core, T, topo):
             const(V("LMC"), 0.0)
         for b in range(4):
             mm(V("PH%d" % b, 0, C), V("QW", 128 * b, 128 * b + 128), V("SW", 128 * b, 128 * b + 128), qe, se)
+        if r == 0:
+            quant(V("LQ", 0, 128), V("LS", 0, 128), V("HT"))
+        if r == 1:
+            quant(V("QV"), V("SV"), V("VT"))
         ts(V("SK", 0, CUT // 4), V("PK", 0, CUT, 4), 0.0, A.is_gt, col(cWk), A.mult)
         ts(V("SK", 96, 112), V("PK", 0, 64, 4), 0.0, A.is_gt, col(cWk), A.mult)
         act(V("SG", 0, CUT), V("PK", 0, CUT), F.Sign)
-        if r == 0:
-            scan(V("MP", 96, 144), V("MM", 0, 48), V("RTX"), A.add, A.max)
-            quant(V("LQ", 0, 128), V("LS", 0, 128), V("HT"))
-            ts(V("LTX", 0, 3), V("MP", 111, 144, 16), col(cFix), A.subtract)
-        if r == 1:
-            quant(V("QV"), V("SV"), V("VT"))
         ts(V("SK", CUT // 4, 96), V("PA", 0, C - CUT, 4), 0.0, A.is_gt, col(cWk), A.mult)
         act(V("SG", CUT, C), V("PA", 0, C - CUT), F.Sign)
-        for x in range(3):
+        for x in range(2):
             act(V("T1H", 96 * x, 96 * x + 96), ind(V("SG"), V("LL", 6 * x, 6 * x + 6)), F.Relu, None, col(cWk))
         if r == 0:
-            act(V("SCN", 32, 64), V("SCN", 0, 32), F.Copy)
+            act(V("SCN", 24, 48), V("SCN", 0, 24), F.Copy)
             const(V("HR"), 16.0)
-            act(V("SCN", 64, 128), V("SCN", 0, 64), F.Copy)
-            const(V("HR", 0, 128, 4), 0.0)
+            act(V("SCN", 48, 96), V("SCN", 0, 48), F.Copy)
+            const(V("HR", 0, 96, 3), 0.0)
+            ts(V("LP", 0, 4), V("IO", 0, 4), 24.0, A.mult, col(cP1), A.add)
+            ts(V("LP", 4, 8), V("IO", 0, 4), 24.0, A.mult, col(cP2), A.add)
         tr(V("YK", 0, 96), V("SK", 0, 96))
         tr(V("YK", 96, 192), V("SK", 16, 112))
+        if r == 0:
+            ts(V("LFW"), V("R6"), 0.5, A.mult, col(cIh), A.add)
         scan(V("ZL"), V("D01"), V("YK"), A.mult, A.add)
         cp(V("TX%d" % r), ind(V("ZL"), V("LTX", 0, 3)))
         send(dst, "ra%d" % r, V("AR%d" % r), V("TX%d" % r))
         for b in range(4):
             act(V("HT", b, C, 4), V("PH%d" % b, 0, C, 4), F.Copy, None, 0.03125)
         if r == 0:
-            ts(V("LA"), V("IO", 0, 8), 2.0, A.mult, col(cCA), A.add)
-            ts(V("LP", 0, 4), V("IO", 0, 4), 32.0, A.mult, col(cP1), A.add)
-            ts(V("LP", 4, 8), V("IO", 0, 4), 32.0, A.mult, col(cP2), A.add)
-            ts(V("LFW"), V("R6"), 0.5, A.mult, col(cIh), A.add)
             const(V("KD"), -1.0)
             act(JJ, V("IO", 0, 48), F.Identity, col(cJ), 1024.0 * S)
             act(JK, V("IO"), F.Identity, 0.0, S)
@@ -454,25 +477,27 @@ def rank_program(g, core, T, topo):
             const(V("KD", 48, 49), 63.0)
             const(V("KD", 80, 81), col(cK80))
         act(JB, JJ, F.Identity, float(C + K * r) * S, 1.0)
-        for x in range(3):
+        for x in range(2):
             tr(V("T2H", 96 * x, 96 * x + 96), V("T1H", 96 * x, 96 * x + 96))
-        for x in range(3):
+        for x in range(2):
             tt(V("LMC", 96 * x, 96 * x + 96, 2), V("T2H", 96 * x, 96 * x + 96, 2),
                V("T2H", 96 * x + 1, 96 * x + 96, 2), A.add)
-        tt(V("TA", 0, 128), ind(V("LMC", 0, 128), V("LA")), V("SCN"), A.not_equal)
-        tt(V("TA", 128, 256), ind(V("LMC", 96, 224), V("LA")), V("SCN"), A.not_equal)
-        tr(V("LMH"), V("LMC", 192, 288))
-        tt(V("TA", 256, C), V("TA", 0, 128), V("TA", 128, 256), A.mult)
+        for x in range(2):
+            tt(V("TA", 96 * x, 96 * x + 96), ind(V("LMC", 96 * x, 96 * x + 96), V("LA", 0, 6)), V("SCN", 0, 96),
+               A.not_equal)
+        tr(V("LMH", 96, 288), V("LMC"))
+        act(V("LMH", 0, 96), ind(V("LMH", 96, 288), V("LA", 6, 12)), F.Copy)
+        tt(V("TA", 192, 288), V("TA", 0, 96), V("TA", 96, 192), A.mult)
         quant(V("QH%d" % r), V("SH%d" % r), V("HT"))
-        scan(V("TP"), V("HR"), V("TA", 256, C), A.mult, A.add)
-        tt(V("MP", 0, 48), V("LMH", 0, 48), V("LMH", 48, 96), A.is_equal)
+        scan(V("TP"), V("HR"), V("TA", 192, 288), A.mult, A.add)
         cp(V("TQ"), ind(V("TP"), V("LP", 0, 4)))
-        ts(V("MP", 48, 96), V("MP", 0, 48), 100.0, A.mult)
+        tt(V("MP", 0, 48), V("LMH", 0, 48), V("LMH", 48, 96), A.is_equal)
         tt(V("TT"), ind(V("TP"), V("LP", 4, 8)), V("TQ"), A.add)
-        tt(V("MP", 96, 144), V("MP", 48, 96), V("LMH", 48, 96), A.add)
+        ts(V("MP", 48, 96), V("MP", 0, 48), 100.0, A.mult)
         lo = 128 + K * r
         send(dst, "rh%d" % r, u8(V("LQ", lo, lo + K)), u8(V("QH%d" % r, 0, K)))
         send(dst, "rh%d" % r, V("LS", lo, lo + K), V("SH%d" % r, 0, K))
+        tt(V("MP", 96, 144), V("MP", 48, 96), V("LMH", 48, 96), A.add)
         ar = "AR%d" % r
         cp(V("AC", 0, 96), ind(V("TT", 0, 16), V(ar, 0, 6)))
         cp(V("AC", 96, 192), ind(V("TT", 16, 32), V(ar, 6, 12)))
@@ -524,7 +549,7 @@ def rank_program(g, core, T, topo):
         swap("HB", "HX")
         mid("HB", "CP")
         top(lambda: [act(V("TAB", TW * b + C + K * r, TW * b + C + K * r + K), V("PH%d" % b, 32, 128), F.Copy)
-                     for b in range(4)])
+                     for b in range(4)], [lambda: None] * 3)
 
     inherit(3, V("QV"), V("SV"), lambda: dma("y", "dend", T.oc[:, 0:4 * CUT], u8(V("QE3", 0, CUT))))
     dma("y", "dend", T.oc[:, 4 * CUT:4 * C], u8(V("QE3", CUT, C)))

@@ -5,8 +5,18 @@ DIST = [1, 2, 3]
 TW = C + 3 * K
 BIG = float(2 ** 21)
 S = 1.0 / BIG
+TINY = 2.0 ** -120
+WHOLE = 1.5 * 2 ** 23
 CUT = 256
+OUT = C - 48
+NEAR = 1000
+PLANES = (("v", 0, 0, 16), ("v", 1, 0, 16), ("s", 2, 0, 16), ("s", 3, 0, 16),
+          ("v", 0, 16, 24), ("q", 0, 0, 16), ("v", 1, 16, 20), ("s", 2, 16, 24), ("s", 3, 16, 24), ("s", 1, 20, 24),
+          ("q", 1, 16, 24))
+SOON = 600.0
+TOP = (("step", 1), ("step", 2), ("turn", 2), ("step", 3), ("turn", 0), ("turn", 1), ("turn", 3))
 FP8, U8, U16, I32, F32, BF = "float8_e4m3fn_x4", "uint8", "uint16", "int32", "float32", "bfloat16"
+CYCLE, WAKE, FAR = 0.92, 170.0, 1600.0
 
 
 def _sb(n, d):
@@ -20,22 +30,22 @@ SCRATCH = {
     "SV": _sb(128, U8), "QW": _sb(512, FP8), "SW": _sb(512, U8), "QC": _sb(512, FP8), "SC": _sb(512, U8),
     "LQ": _sb(128 + 3 * K, FP8), "LS": _sb(128 + 3 * K, U8),
     "PI": _sb(1, I32), "CI": _sb(12, I32), "CF": _sb(40, F32),
-    "T16": _sb(144, F32), "M1": _sb(288, F32), "MM": _sb(144, F32), "IO": _sb(96, F32),
-    "PT": _sb(C, F32), "R6": _sb(6, F32), "RTX": _sb(48, F32), "RX": _sb(480, F32), "SCN": _sb(192, F32),
-    "HR": _sb(96, F32), "KD": _sb(96, F32), "JJ": _sb(240, F32), "D01": _sb(192, F32),
-    "LPAR": _sb(2, U16), "LU": _sb(8, U16), "LA": _sb(12, U16), "LP": _sb(8, U16), "LTX": _sb(4, U16),
-    "LFW": _sb(6, U16), "LL": _sb(12, U16), "LFL": _sb(4, U16), "LEX": _sb(6, U16), "PU": _sb(4, U16),
-    "PL": _sb(24, U16), "LM": _sb(8, U16), "LT": _sb(18, U16), "KL": _sb(4, U16), "PTR": _sb(24, U16),
-    "PR": _sb(32, I32), "PF": _sb(16, F32), "FLR": _sb(C, I32),
-    "RA": _sb(128, F32), "SCO": _sb(144, F32), "WA": _sb(128, F32), "WB": _sb(128, F32),
-    "WH": _sb(176, F32), "WX": _sb(96, F32), "WC": _sb(96, F32), "DI": _sb(32, I32), "DF": _sb(48, F32),
-    "VA": _sb(128, F32), "VB": _sb(128, F32), "AA": _sb(128, F32), "AB": _sb(128, F32), "HB": _sb(176, F32),
+    "T16": _sb(96, F32), "M1": _sb(192, F32), "MM": _sb(96, F32), "IO": _sb(C, F32),
+    "SRC": _sb(2 * OUT, F32), "R6": _sb(6, F32), "RTX": _sb(48, F32), "RX": _sb(192, F32), "SCN": _sb(288, F32),
+    "HR": _sb(96, F32), "KD": _sb(97, F32), "JJ": _sb(240, F32), "D01": _sb(192, BF),
+    "LU": _sb(8, U16), "LA": _sb(18, U16), "LP": _sb(8, U16), "LTX": _sb(4, U16), "LX": _sb(44, U16),
+    "LFW": _sb(6, U16), "LL": _sb(12, U16), "LFL": _sb(4, U16), "LEX": _sb(8, U16), "PW": _sb(14, U16),
+    "PL": _sb(28, U16), "LM": _sb(8, U16), "LT": _sb(18, U16), "KL": _sb(4, U16), "PTR": _sb(24, U16),
+    "PR": _sb(4, I32), "FLR": _sb(C, I32),
+    "RB": _sb(C, F32), "SCO": _sb(624, F32), "XS": _sb(OUT + 176, F32), "XO": _sb(OUT + 96, F32),
+    "WX": _sb(96, F32), "WC": _sb(96, F32),
+    "VA": _sb(320, F32), "AA": _sb(128, F32), "AB": _sb(128, F32), "HB": _sb(192, F32),
     "HX": _sb(96, F32), "CP": _sb(C, F32), "YY": _sb(C, F32), "OI": _sb(96, I32), "OJ": _sb(96, I32),
-    "SK": _sb(112, BF), "YK": _sb(192, BF), "ZL": _sb(192, F32),
-    "SG": _sb(C, BF), "T1H": _sb(192, BF), "T2H": _sb(192, BF), "LMH": _sb(288, BF), "LMC": _sb(192, BF),
-    "TA": _sb(288, F32), "TP": _sb(96, F32), "TQ": _sb(64, F32), "TT": _sb(64, F32), "MP": _sb(144, F32),
-    "AC": _sb(288, F32), "ACI": _sb(96, I32), "CHI": _sb(288, I32), "CHF": _sb(288, F32), "CHS": _sb(288, F32),
-    "KI": _sb(8, I32), "RF": _sb(24, F32), "XF": _sb(96, BF), "FW": _sb(96, BF), "UP": _sb(240, F32),
+    "YK": _sb(192, BF), "ZL": _sb(192, BF),
+    "SG": _sb(C + 64, BF), "T1H": _sb(192, BF), "T2H": _sb(192, BF), "LMH": _sb(288, BF), "LMC": _sb(192, BF),
+    "TA": _sb(288, F32), "TP": _sb(96, F32), "TQ": _sb(64, F32), "TT": _sb(64, F32), "MP": _sb(96, F32),
+    "AC": _sb(C, F32), "ACI": _sb(96, I32), "CHI": _sb(294, I32), "CHS": _sb(294, F32),
+    "KI": _sb(4, F32), "RF": _sb(24, F32), "XF": _sb(96, BF), "FW": _sb(96, BF), "UP": _sb(288, F32),
     "OF": _sb(48, F32), "YO": _sb(C, F32),
 }
 for _r in range(4):
@@ -49,7 +59,7 @@ for _r in range(3):
 for _n in ("PK", "PA", "PH0", "PH1", "PH2", "PH3"):
     SCRATCH[_n] = ("psum", [128, 512], F32)
 
-SEMAPHORES = ["cv", "cs", "ct", "cg", "dpar", "dx", "du", "dfl", "dw", "dv", "dout", "dend", "sent",
+SEMAPHORES = ["cv", "cs", "ct", "cg", "dpar", "dx", "du", "dfl", "dw", "dv", "dq", "dout", "sent",
               "ra0", "ra1", "ra2", "rh0", "rh1", "rh2"]
 
 
@@ -59,8 +69,7 @@ def rank_program(g, core, T, topo):
         return
     N = len(T.cores)
     Q = {"v": g.vector, "s": g.scalar, "t": g.tensor, "g": g, "y": g.sync}
-    total = {n: 0 for n in SEMAPHORES}
-    seen = {q: {} for q in Q}
+    calls = []
     log = {}
 
     def V(name, c0=0, c1=None, st=1, p0=0, p1=128, ps=1):
@@ -68,57 +77,112 @@ def rank_program(g, core, T, topo):
             c1 = SCRATCH[name][1][1]
         t = T[name]
         ap = t[p0:p1:ps, c0:c1] if ps > 1 else (t[p0:p1, c0:c1] if st == 1 else t[p0:p1, c0:c1:st])
-        return (ap, [(name, p0, p1, frozenset(range(c0, c1, st)))])
+        n = len(range(c0, c1, st))
+        return (ap, [(name, p0, p1, frozenset(range(c0, c1, st)))], n, SCRATCH[name][2] in (BF, U16), False)
 
-    def col(k):
-        return V("CF", k, k + 1)
+    def col(k, p0=0, p1=128):
+        return V("CF", k, k + 1, 1, p0, p1)
 
     def ind(win, off, words=False):
         ap = win[0].bitcast(dt.uint32) if words else win[0]
-        return (ap.indirect(off[0]), win[1] + off[1])
+        return (ap.indirect(off[0]), win[1] + off[1], 16 * off[2], False, True)
 
-    def wait(q, sem, val):
-        if seen[q].get(sem, 0) < val:
-            Q[q].wait_ge(T.sem[sem], val)
-            seen[q][sem] = val
+    def record(q, fn, busy, late, outs, ins, sem, inc, after=()):
+        before = set(after)
+        regs = [(r, True) for o in outs if isinstance(o, tuple) for r in o[1]]
+        regs += [(r, False) for o in ins if isinstance(o, tuple) for r in o[1]]
+        for (name, p0, p1, cols), writing in regs:
+            bank = SCRATCH[name][0] == "psum"
+            for (w, k, a0, a1, cs) in log.get(name, []):
+                if bank:
+                    hit = w or writing or calls[k][0] != q
+                else:
+                    hit = (w or writing) and a0 < p1 and p0 < a1 and not cols.isdisjoint(cs)
+                if hit:
+                    before.add(k)
+        for k in list(before):
+            if calls[k][6] != 1:
+                before.update(m for m in range(len(calls)) if calls[m][5] == calls[k][5])
+        calls.append((q, fn, busy, late, before, sem, inc))
+        for (name, p0, p1, cols), writing in regs:
+            log.setdefault(name, []).append((writing, len(calls) - 1, p0, p1, cols))
+        return len(calls) - 1
 
-    def meet(q, rd, wr):
-        need = {}
-        for regs, writing in ((rd, False), (wr, True)):
-            for (name, p0, p1, cols) in regs:
-                bank = SCRATCH[name][0] == "psum"
-                for (w, q2, a0, a1, cs, sem, val) in log.get(name, []):
-                    if bank:
-                        hit = w or writing or q2 != q
-                    else:
-                        hit = (w or writing) and a0 < p1 and p0 < a1 and not cols.isdisjoint(cs)
-                    if hit:
-                        need[sem] = max(need.get(sem, 0), total[sem] if val is None else val)
-        for sem in need:
-            wait(q, sem, need[sem])
+    def op(q, fn, outs, ins, per=1.0, fixed=None):
+        n = ins[0][2] if ins else outs[0][2]
+        if ins and ins[0][4]:
+            busy = 60.0 + 1.56 * n * CYCLE
+        elif fixed is None:
+            busy = max(64.0, per * n) * CYCLE
+        else:
+            busy = fixed + per * n * CYCLE
+        record(q, fn, busy, busy, outs, ins, "c" + q, 1)
 
-    def note(q, regs, writing, sem, val):
-        for (name, p0, p1, cols) in regs:
-            log.setdefault(name, []).append((writing, q, p0, p1, cols, sem, val))
+    def issue():
+        n = len(calls)
+        at, taken = {}, {q: [] for q in Q}
 
-    def op(q, fn, outs, ins):
-        w = [r for o in outs for r in o[1]]
-        rd = [r for o in ins if isinstance(o, tuple) for r in o[1]]
-        meet(q, rd, w)
-        sem = "c" + q
-        fn().then_inc(T.sem[sem], 1)
-        total[sem] += 1
-        note(q, rd, False, sem, total[sem])
-        note(q, w, True, sem, total[sem])
+        def place(k):
+            q, _fn, busy, _late, before = calls[k][:5]
+            for m in sorted(before):
+                if m not in at:
+                    place(m)
+            t = max([0.0] + [at[m] + calls[m][3] + WAKE for m in before])
+            if q is not None:
+                for lo, hi in taken[q]:
+                    if t + busy <= lo:
+                        break
+                    t = max(t, hi)
+                taken[q].append((t, t + busy))
+                taken[q].sort()
+            at[k] = t
+
+        chain = [0.0] * n
+        for k in range(n - 1, -1, -1):
+            chain[k] += calls[k][3] + WAKE
+            for m in calls[k][4]:
+                chain[m] = max(chain[m], chain[k])
+        early = sorted(range(marks[0], marks[1]), key=lambda k: chain[k])
+        for k in list(range(marks[0])) + list(range(marks[1], n)):
+            while early and k >= marks[1] and (chain[early[-1]] + SOON > chain[k] or k == n - 1):
+                m = early.pop()
+                if m not in at:
+                    place(m)
+            if k not in at:
+                place(k)
+        total, count, seen = {s: 0 for s in SEMAPHORES}, {}, {q: {} for q in Q}
+        whole = {s: sum(c[6] for c in calls if c[5] == s) for s in SEMAPHORES}
+        for k in sorted(range(n), key=lambda k: at[k]):
+            q, fn, busy, late, before, sem, inc = calls[k]
+            total[sem] += inc
+            count[k] = total[sem] if inc == 1 else whole[sem]
+            if q is None:
+                continue
+            need = {}
+            for m in before:
+                need[calls[m][5]] = max(need.get(calls[m][5], 0), count[m])
+            for s in need:
+                if seen[q].get(s, 0) < need[s]:
+                    Q[q].wait_ge(T.sem[s], need[s])
+                    seen[q][s] = need[s]
+            if sem == "sent":
+                fn()
+            else:
+                fn().then_inc(T.sem[sem], inc)
+        for s in SEMAPHORES:
+            g.wait_ge(T.sem[s], whole[s])
 
     def a_(x):
         return x[0] if isinstance(x, tuple) else x
 
+    def half(*xs):
+        return 0.5 if all(x[3] for x in xs) else 1.0
+
     def cp(o, i):
-        op("v", lambda: g.vector.tensor_copy(o[0], i[0]), [o], [i])
+        op("v", lambda: g.vector.tensor_copy(o[0], i[0]), [o], [i], half(o, i))
 
     def tt(o, a, b, f):
-        op("v", lambda: g.vector.tensor_tensor(o[0], a[0], b[0], f), [o], [a, b])
+        op("v", lambda: g.vector.tensor_tensor(o[0], a[0], b[0], f), [o], [a, b], 2.0)
 
     def ts(o, a, s1, f0, s2=None, f1=None):
         if f1 is None:
@@ -130,13 +194,13 @@ def rank_program(g, core, T, topo):
         op("v", lambda: g.vector.memset(o[0], c), [o], [])
 
     def scan(o, d0, d1, f0, f1):
-        op("v", lambda: g.vector.tensor_tensor_scan(o[0], d0[0], d1[0], 0.0, f0, f1), [o], [d0, d1])
+        op("v", lambda: g.vector.tensor_tensor_scan(o[0], d0[0], d1[0], 0.0, f0, f1), [o], [d0, d1], half(o, d0, d1))
 
     def tr(o, i):
-        op("v", lambda: g.vector.transpose(o[0], i[0]), [o], [i])
+        op("v", lambda: g.vector.transpose(o[0], i[0]), [o], [i], half(o, i))
 
     def quant(qo, so, i):
-        op("v", lambda: g.vector.quantize_mx(qo[0], so[0], i[0]), [qo, so], [i])
+        op("v", lambda: g.vector.quantize_mx(qo[0], so[0], i[0]), [qo, so], [i], 0.27, 12.0)
 
     def act(o, i, f, bias=None, scale=None):
         kw = {}
@@ -147,418 +211,350 @@ def rank_program(g, core, T, topo):
         op("s", lambda: g.scalar.activation(o[0], i[0], f, **kw), [o], [i, bias, scale])
 
     def mm(o, wq, wsc, xq, xsc):
-        op("t", lambda: g.tensor.matmul_mx(o[0], wq[0], wsc[0], xq[0], xsc[0], True, True), [o], [wq, wsc, xq, xsc])
+        op("t", lambda: g.tensor.matmul_mx(o[0], wq[0], wsc[0], xq[0], xsc[0], True, True), [o], [xq, xsc, wq, wsc],
+           1.0, 16.0)
 
     def iota(o, pat, base, cm=0, small=True):
         if small:
-            op("g", lambda: g.iota(o[0], pat, base, cm, allow_small_or_imprecise_dtypes=True), [o], [])
+            op("g", lambda: g.iota(o[0], pat, base, cm, allow_small_or_imprecise_dtypes=True), [o], [], 2.0, 130.0)
         else:
-            op("g", lambda: g.iota(o[0], pat, base, cm), [o], [])
+            op("g", lambda: g.iota(o[0], pat, base, cm), [o], [], 2.0, 130.0)
 
     def dma(q, sem, o, i):
-        meet(q, i[1] if isinstance(i, tuple) else [], o[1] if isinstance(o, tuple) else [])
-        Q[q].dma_start(a_(o), a_(i)).then_inc(T.sem[sem], 16)
-        total[sem] += 16
-        if isinstance(i, tuple):
-            note(q, i[1], False, sem, None)
-        if isinstance(o, tuple):
-            note(q, o[1], True, sem, None)
+        record(q, lambda: Q[q].dma_start(a_(o), a_(i)), 60.0, FAR, [o], [i], sem, 16)
 
     def u8(x):
-        return (x[0].bitcast(dt.uint8), x[1])
+        return (x[0].bitcast(dt.uint8),) + x[1:]
 
     NE = 8
 
-    def send(dst, sem, o, i):
-        meet("g", i[1], [])
+    def send(dst, sem, pairs):
         rid, pid, _se = topo.addr(dst)
         m = 0
         for e in topo.engines(core, dst)[:NE]:
             m |= 1 << e
-        g.remote_dma(o[0], i[0], T.sem[sem], T.sem["sent"], pid, rid, m)
-        total["sent"] += NE
 
-    def landed(sem, x):
-        total[sem] += NE
-        note("far", x[1], True, sem, None)
+        def one(o, i):
+            return record("g", lambda: g.remote_dma(o[0], i[0], T.sem[sem], T.sem["sent"], pid, rid, m), 200.0, 200.0,
+                          [], [i], "sent", NE)
+        sent = [one(o, i) for o, i in pairs]
+        calls.append((None, None, 0.0, FAR, set(sent), sem, NE * len(pairs)))
+        for o, _i in pairs:
+            for (name, p0, p1, cols) in o[1]:
+                log.setdefault(name, []).append((True, len(calls) - 1, p0, p1, cols))
 
-    for r in range(3):
-        landed("ra%d" % r, V("AR%d" % r))
-        landed("rh%d" % r, V("LQ", 128 + K * r, 128 + K * r + K))
-        landed("rh%d" % r, V("LS", 128 + K * r, 128 + K * r + K))
-
-    dma("y", "dpar", V("PR", 0, 24, 1, 0, 16), T.par[:, :])
-    dma("s", "dpar", V("PR", 0, 24, 1, 16, 32), T.par[:, :])
+    for G in range(8):
+        dma("ys"[G % 2], "dpar", V("PR", 0, 3, 1, 16 * G, 16 * G + 16), T.par[:, 3 * G:3 * G + 3])
     ms(V("FLR"), 0)
     for G in range(8):
         dma("y", "dfl", V("FLR", 0, C, 1, 16 * G, 16 * G + 16, 2), T.fl[:, :])
-    dma("s", "dx", V("XR"), T.x[:, :])
     dma("s", "du", V("UT"), T.u[:, :])
+    dma("s", "dx", V("XR"), T.x[:, :])
     dma("y", "dw", u8(V("QW")), T.wc[:, :])
     dma("y", "dw", V("SW"), T.ws[:, :])
     dma("y", "dv", V("VT"), T.v[:, :])
 
     iota(V("PI"), [[0, 1]], 0, 1, False)
-    iota(V("IO"), [[1, 96]], 0)
-    iota(V("T16"), [[0, 9], [1, 16]], 0)
-    iota(V("PT", 0, 48), [[-16384 - 16, 3], [-1023, 16]], 1024 * 1024 + 80)
-    iota(V("PT", 48, 96), [[-16384 + 16, 3], [-1023, 16]], (1024 - 48) * 1024)
+    iota(V("T16"), [[0, 6], [1, 16]], 0)
     iota(V("R6"), [[16, 3], [0, 2]], 0)
+    iota(V("IO"), [[1, C]], 0)
+    marks = [len(calls)]
+    iota(V("SRC", 288, OUT), [[1, 48]], -NEAR)
+    iota(V("SRC", OUT, OUT + 48), [[-16, 3], [1, 16]], 80)
+    iota(V("SRC", OUT + 288, 2 * OUT), [[-16, 3], [1, 16]], 32 - NEAR)
     iota(V("RTX", 0, 24), [[4, 4], [32, 6]], 3)
-    iota(V("RTX", 24, 48), [[32, 3], [2, 8]], 1)
-    for s in range(6):
-        iota(V("RX", s, 96, 6), [[4, 4], [96, 4]], 16 * [0, 5, 2, 1, 4, 3][s])
-        iota(V("RX", 96 + s, 192, 6), [[0, 16]], 16 * ([5, 0, 3, 2, 1, 4][s] - [0, 5, 2, 1, 4, 3][s]) + 2)
-    iota(V("SCN", 96, 192), [[2, 8], [0, 4], [32, 3]], 0)
-    iota(V("SCN", 0, 12), [[4, 4], [0, 3]], 0)
-    iota(V("SCN", 12, 24), [[1, 4], [0, 3]], 0)
+    iota(V("RTX", 24, 48), [[32, 3], [2, 8]], 17)
+    iota(V("RX", 0, 24, 2), [[32, 12]], 0)
+    iota(V("RX", 1, 24, 2), [[32, 12]], -16)
+    iota(V("RX", 1, 24, 6), [[96, 4]], 80)
+    iota(V("RX", 24, 48), [[0, 24]], 18)
+    for s, d in ((0, 82), (1, -78), (4, -46)):
+        iota(V("RX", 24 + s, 48, 6), [[0, 4]], d)
+    iota(V("SCN", 192, 288), [[2, 8], [0, 4], [32, 3]], 0)
+    iota(V("SCN", 0, 192), [[0, 16], [2, 4], [0, 3]], -3)
+    iota(V("D01", 0, 192, 4), [[0, 48]], 0)
+    iota(V("D01", 1, 192, 2), [[0, 96]], 2)
+    iota(V("D01", 2, 192, 4), [[0, 6], [-2, 2], [0, 4]], 2)
+    iota(V("HR", 0, 96, 3), [[0, 32]], 0)
+    iota(V("HR", 1, 96, 3), [[0, 32]], 16)
+    iota(V("HR", 2, 96, 3), [[0, 32]], 16)
+    iota(V("UP", 0, 144, 3), [[0, 48]], 2)
+    iota(V("UP", 2, 144, 3), [[0, 48]], 0)
+    iota(V("CHI", 96, 294, 98), [[0, 3]], 8192, 0, False)
+    iota(V("LMC", 1, 192, 2), [[0, 96]], 0)
+    iota(V("HT", C, 512), [[0, 128]], 0)
     iota(V("ONE"), [[0, 520]], 1)
-    op("g", lambda: g.affine_select(T.EC[:, :], T.ONE[:, :], [[-1, 520]], A.is_equal, 0.0, 3, 4), [V("EC")], [V("ONE")])
+    op("g", lambda: g.affine_select(T.EC[:, :], T.ONE[:, :], [[-1, 520]], A.is_equal, 0.0, 3, 4), [V("EC")], [V("ONE")],
+       2.0, 170.0)
 
-    ms(V("PR", 24, 32), 0)
-    cI, cI3, cI12, cIh, cB0, cG, cH16, cA, cB1, cH = range(10)
-    for k, (sh, m) in enumerate([(0, 15), (0, 3), (0, 12), (1, 7), (0, 1), (4, 7), (0, 16), (5, 3), (1, 1), (4, 1)]):
+    cI, cI3, cI12, cIh, cB0, cG, cH16, cH = range(8)
+    for k, (sh, m) in enumerate([(0, 15), (0, 3), (0, 12), (1, 7), (0, 1), (4, 7), (0, 16), (4, 1)]):
         ts(V("CI", k, k + 1), V("PI"), sh, A.logical_shift_right, m, A.bitwise_and)
-    ms(V("LT"), 0)
-    cp(V("CF", 0, 10), V("CI", 0, 10))
-    (cI1, cFix, cG3, cFl, cK1, cK2, cWk, cM0, cKl, cK80, cMa, cMb, cD, cTop, cJ, cJx, cUk, cCA,
-     cP1, cP2, cLk) = range(10, 31)
+    cp(V("CF", 0, 8), V("CI", 0, 8))
+    (cI1, cFix, cG3, cFl, cD3, cWk, cKl, cK80, cD, cJ, cJx, cUk, cCA, cP1, cP2, cLk, cRoot, cNear, cXs, cXo,
+     cEx) = range(10, 31)
     JJ, JX, JB, JK = V("JJ", 0, 48), V("JJ", 48, 96), V("JJ", 96, 144), V("JJ", 144, 240)
-    ms(V("WH", 0, 16), 0.0)
-    ms(V("RA"), 0.0)
     ts(col(cI1), col(cI), 1.0, A.add)
-    ts(V("LPAR", 0, 1), col(cG), 3.0, A.mult, col(cI3), A.add)
-    ts(col(cD), col(cG), -48.0, A.mult, 16.0, A.add)
+    ts(col(cD), col(cG), -48.0, A.mult, float(OUT), A.add)
+    ts(col(cRoot), col(cI), OUT - 1.0, A.add)
     ts(col(cFix), col(cI), 15.0, A.is_lt, BIG, A.mult)
-
-    def columns(rows):
-        for k, src, sc, bi in rows:
-            act(col(k), col(src), F.Identity, bi, sc)
+    for k, src, sc, bi in [
+            (cUk, cIh, 16.0, col(cB0)), (cG3, cG, 3.0, 0.0), (cLk, cG, 48.0, col(cI)), (cD3, cG, -144.0, 18.0),
+            (cJx, cG, 49200.0 * S, 1024.0 * S), (cFl, cI, 24.0, col(cG3)), (cWk, cB0, -1.0, 2.0),
+            (cKl, cH16, -5.0 / 256, 95.0 / 256), (cK80, cH16, 6.0 / 256, -17.0 / 256),
+            (cJ, cG, 49152.0 * S, 1024.0 * S), (cCA, cH16, -1.0, col(cFix)), (cP1, cI12, 0.75, 2.0),
+            (cP2, cI3, 3.0, 14.0), (cNear, cFix, 1.0, -float(NEAR)), (cXs, cH16, 24.0, col(cI)),
+            (cXo, cH16, -18.0, col(cI)), (cEx, cI3, -4.0, col(cFix))]:
+        act(col(k), col(src), F.Identity, bi, sc)
 
     def const(o, c):
-        act(o, V("PT", 0, len(o[1][0][3])), F.Identity, c, 0.0)
+        act(o, V("T16" if o[2] <= 96 else "IO", 0, o[2]), F.Identity, c, 0.0)
 
-    columns([(cUk, cIh, 16.0, col(cB0)), (cG3, cG, 3.0, 0.0), (cLk, cG, 48.0, col(cI)),
-             (cJx, cG, 49200.0 * S, 1024.0 * S), (cFl, cI, 24.0, col(cG3))])
-    for a in range(1, 4):
-        act(V("PT", 96 * a, 96 * a + 96), V("PT", 0, 96), F.Identity, float(-96 * a * 1023), 1.0)
-    for name in ("WA", "WB", "VA", "AA", "AB", "VB"):
-        for lo in (0, 64):
-            const(V(name, lo, lo + 16), 0.0)
-    ts(V("M1", 0, 144), V("T16"), col(cI), A.is_equal, -3.0 * BIG, A.mult)
-    ts(V("M1", 144, 288), V("T16"), col(cI1), A.is_equal, BIG, A.mult)
+    act(V("RB", 0, OUT), V("IO", 0, OUT), F.Copy)
+    act(V("SRC", 0, 288), V("IO", 0, 288), F.Copy)
+    act(V("SRC", OUT + 48, OUT + 96), V("IO", 0, 48), F.Copy)
+    for a in (1, 2):
+        act(V("SRC", OUT + 96 * a, OUT + 96 * a + 96), V("SRC", OUT, OUT + 96), F.Identity, 96.0 * a, 1.0)
+    for name, lo, hi in (("AA", 0, 16), ("AA", 64, 80), ("AB", 0, 16), ("AB", 64, 80), ("HB", 0, 16), ("HB", 96, 112),
+                         ("HB", 176, 192), ("XS", C, C + 48), ("XS", OUT + 160, OUT + 176), ("XO", C + 32, C + 48),
+                         ("VA", 0, 320)):
+        const(V(name, lo, hi), 0.0)
+    iota(V("CP", 96, C), [[0, C - 96]], 0)
+    iota(V("YY"), [[0, C]], 0)
+    ms(V("LT"), 0)
+    ts(V("M1", 0, 96), V("T16"), col(cI), A.is_equal, -3.0 * BIG, A.mult)
+    ts(V("M1", 96, 192), V("T16"), col(cI1), A.is_equal, BIG, A.mult)
+    tt(V("MM", 0, 48), V("M1", 0, 48), V("M1", 96, 144), A.add)
+    tt(V("MM", 48, 96), V("M1", 48, 96), V("M1", 144, 192), A.add)
+    used = [0]
 
-    for a in range(1, 4):
-        cp(V("PR", 0, 24, 1, 32 * a, 32 * a + 32), V("PR", 0, 24, 1, 0, 32))
-    tt(V("MM", 0, 48), V("M1", 0, 48), V("M1", 144, 192), A.add)
-    ms(V("HB", 0, 16), 0.0)
-    cp(V("PF"), ind(V("PR"), V("LPAR", 0, 1)))
-    ms(V("HB", 96, 112), 0.0)
-    ms(V("WH", 96, 112), 0.0)
-    ts(V("PL", 0, 3), V("PF", 0, 3), col(cD), A.add)
-    cp(V("PU", 0, 3), V("PF", 0, 3))
-    cp(V("LL", 6, 12, 2), V("PF", 0, 3))
-    cp(V("RA", 16, 64), ind(V("IO", 0, 64), V("PL", 0, 3)))
-    cp(V("LL", 7, 12, 2), V("PF", 0, 3))
-    for lo in (16, 80):
-        act(V("WA", lo, lo + 48), ind(V("PT"), V("PU", 0, 3)), F.Copy)
-    act(JX, V("IO", 0, 48), F.Identity, col(cJx), 1025.0 * S)
-    columns([(cM0, cH, 1.0, -1.0), (cMa, cA, 96.0, 32.0), (cTop, cH16, -64.0, 1024.0),
-             (cMb, cA, -96.0, 1040.0), (cK1, cB0, -1.0, 2.0), (cK2, cB1, -3.0, 4.0),
-             (cKl, cH16, -5.0, 95.0), (cK80, cH16, 6.0, -17.0), (cJ, cG, 49152.0 * S, 1024.0 * S),
-             (cCA, cH16, -1.0, col(cFix)), (cP1, cI12, 0.75, 2.0), (cP2, cI3, 3.0, 14.0), (cWk, cK1, col(cK2), 0.0)])
-    act(V("RX", 192, 288), V("RX", 96, 192), F.Identity, 0.0, col(cH))
-    const(V("CP", 96, C), 0.0)
-    const(V("YY"), 0.0)
+    def listed(row):
+        lo = used[0]
+        used[0] += row[2]
+        scan(V("SCO", lo, lo + row[2]), V("MM", 0, row[2]), row, A.add, A.max)
+        return lambda a=0, b=row[2] // 16, p0=0, p1=128: V("SCO", lo + 15 + 16 * a, lo + 16 * b, 16, p0, p1)
 
-    def double(k, src, dst):
-        off = V("PL", 4 * k, 4 * k + 3)
-        tt(V(dst, 16, 64), ind(V(src, 0, 64), off), V(src, 80, 128), A.max)
-        if k < 3:
-            tt(V(dst, 80, 128), ind(V(src, 64, 128), off), V(src, 16, 64), A.max)
-
-    def local(k, vin):
-        double(k, (vin, "AA", "AB", "AA")[k], ("AA", "AB", "AA", "HB")[k])
-
-    def seq(hb, c):
-        own = V(hb, 16 + 16 * c, 32 + 16 * c)
-        tt(own, ind(V(hb, 0, 16 + 16 * c), V("PL", 16 + 2 * c, 17 + 2 * c)), own, A.max)
-        cp(V(hb, 96 - 16 * c, 112 - 16 * c), V(hb, 16 * c, 16 * c + 16))
-
-    def swap(hb, hx):
-        tr(V(hx), V(hb, 16, 112))
-        tr(V(hb, 112, 176), V(hx, 16, 80))
-
-    def mid(hb, out):
-        tt(V(out, 0, 48), ind(V(hb, 96, 176), V("LM", 0, 3)), V(hb, 16, 64), A.max)
-        tt(V(out, 48, 96), ind(V(hb, 0, 64), V("LM", 4, 7)), V(hb, 112, 160), A.max)
-
+    ts(V("LU"), V("T16", 0, 8), 0.0, A.mult, col(cUk), A.add)
+    ts(V("LL", 0, 6), V("R6"), col(cLk), A.add)
+    ts(V("LFL", 0, 3), V("T16", 0, 3), col(cFl), A.add)
+    ts(V("LA", 12, 18), V("T16", 0, 6), 32.0, A.mult, col(cI), A.add)
+    ts(V("LP", 0, 4), V("T16", 0, 4), 24.0, A.mult, col(cP1), A.add)
+    ts(V("LP", 4, 8), V("T16", 0, 4), 24.0, A.mult, col(cP2), A.add)
+    ts(V("LFW"), V("R6"), 0.5, A.mult, col(cIh), A.add)
+    ts(V("LX", 0, 21), V("IO", 0, OUT, 16), col(cXs), A.add, -48.0, A.add)
+    ts(V("LX", 22, 43), V("IO", 0, OUT, 16), col(cXo), A.add, 288.0, A.add)
+    ts(V("LTX", 0, 3), listed(V("RTX"))(), col(cFix), A.subtract)
+    ts(V("LA", 0, 6), listed(V("SCN", 192, 288))(), col(cCA), A.subtract)
+    ts(V("LA", 6, 12), V("LA", 0, 6), 96.0, A.add)
     NA = CUT // 16
-    NB = 24 - NA
-
-    def places(lo, n, at):
-        for a in range(4):
-            cp(V("PTR", lo, lo + n, 1, 32 * a, 32 * a + 32), V("OJ", at + n * a, at + n * a + n, 1, 0, 32))
-
-    def top(beside, fills):
-        def part(a, p0=0):
-            return V("CP", 96 * a, 96 * a + 96, 1, p0, p0 + 32)
-
-        def turn(a):
-            tr(V("YY", 96 * a, 96 * a + 96, 1, 0, 32), part(a))
-
-        def step(a):
-            tt(V("CP", 96 * a, 96 * a + 96), ind(V("CP", 0, 96 * a), V("LT", 6 * a - 6, 6 * a)),
-               V("CP", 96 * a, 96 * a + 96), A.max)
-
-        def low(lo, hi):
-            ts(V("OJ", lo, hi, 1, 0, 32), V("OI", lo, hi, 1, 0, 32), 1023, A.bitwise_and)
-
-        cp(part(1), part(0, 32))
-        act(part(2), part(0, 64), F.Copy)
-        act(part(3), part(0, 96), F.Copy)
-        beside()
-        turn(0)
-        step(1)
-        fills[0]()
-        step(2)
-        turn(1)
-        fills[1]()
-        turn(2)
-        step(3)
-        ts(V("OI", 0, 4 * NA), ind(V("YY", 0, 288), V("LEX", 0, NA // 4)), BIG, A.mult)
-        turn(3)
-        low(0, 4 * NA)
-        ts(V("OI", 4 * NA, 96), ind(V("YY"), V("LEX", NA // 4, 6)), BIG, A.mult)
-        places(0, NA, 0)
-        low(4 * NA, 96)
-        fills[2]()
-
-    fill = [
-        lambda: ts(V("LU"), V("IO", 0, 8), 0.0, A.mult, col(cUk), A.add),
-        lambda: ts(V("LL", 0, 6), V("R6"), col(cLk), A.add),
-        lambda: ts(V("LFL", 0, 3), V("IO", 0, 3), col(cFl), A.add),
-        lambda: double(0, "WA", "WB"),
-        lambda: ts(V("LA", 6, 12), V("IO", 0, 6), 32.0, A.mult, col(cI), A.add),
-        lambda: tt(V("MM", 48, 144), V("M1", 48, 144), V("M1", 192, 288), A.add),
-        lambda: double(1, "WB", "WA"),
-        lambda: tt(V("VA", 16, 64), ind(V("FLR"), V("LFL", 0, 3)), JX, A.mult),
-        lambda: double(2, "WA", "WB"),
-        lambda: tt(V("VA", 80, 128), ind(V("FLR"), V("LFL", 0, 3)), JX, A.mult),
-        lambda: double(3, "WB", "WH"),
-        lambda: local(0, "VA"),
-    ]
-    ra, rb = 0, 64
-    for k in range(4):
-        cp(V("RA", rb + 16, rb + 64), ind(V("RA", ra, ra + 64), V("PL", 4 * k, 4 * k + 3)))
-        fill[3 * k]()
-        scan(V("SCO", 0, 48), V("MM", 0, 48), V("RA", rb + 16, rb + 64), A.add, A.max)
-        fill[3 * k + 1]()
-        ts(V("PL", 4 * k + 4, 4 * k + 7) if k < 3 else V("PL", 16, 22, 2), V("SCO", 15, 48, 16), col(cFix), A.subtract)
-        fill[3 * k + 2]()
-        ra, rb = rb, ra
-    for b in range(4):
-        act(V("TAB", TW * b, TW * b + C), V("XR", b, 4 * C, 4), F.Copy)
-    seq("WH", 1)
-    seq("WH", 2)
-    local(1, "VA")
-    tr(V("WX"), V("WH", 16, 112))
-    local(2, "VA")
-    tr(V("WH", 112, 176), V("WX", 16, 80))
-    local(3, "VA")
-    scan(V("SCO"), V("MM"), V("WH", 16, 160), A.add, A.max)
-    seq("HB", 1)
-    ts(V("DI", 0, 9), V("SCO", 15, 144, 16), col(cFix), A.subtract)
-    seq("HB", 2)
-    ts(V("DI", 10, 13), V("DI", 6, 9), 10, A.logical_shift_right)
-    ts(V("DI", 20, 23), V("DI", 0, 3), 1023, A.bitwise_and)
-    tr(V("HX"), V("HB", 16, 112))
-    ts(V("LM", 4, 7), V("DI", 10, 13), col(cMb), A.subtract, col(cM0), A.mult)
-    ts(V("LM", 0, 3), V("DI", 20, 23), col(cMa), A.subtract, col(cH), A.mult)
-    tt(V("RX", 288, C), V("RX", 192, 288), V("RX", 0, 96), A.add)
+    act(V("RX", 48, 72), V("RX", 24, 48), F.Identity, 0.0, col(cH))
+    tt(V("RX", 72, 96), V("RX", 48, 72), V("RX", 0, 24), A.add)
     for a in range(4):
-        act(V("RX", C + NA * a, C + NA * a + NA), V("RX", 288 + 24 * a, 288 + 24 * a + NA), F.Copy)
-        act(V("RX", C + 4 * NA + NB * a, C + 4 * NA + NB * a + NB), V("RX", 288 + 24 * a + NA, 312 + 24 * a), F.Copy)
-    mid("WH", "WC")
-    tr(V("HB", 112, 176), V("HX", 16, 80))
-    scan(V("SCO", 0, 96), V("MM", 0, 96), V("WC"), A.add, A.max)
-    mid("HB", "CP")
-    ts(V("DI", 0, 6), V("SCO", 15, 96, 16), col(cFix), A.subtract)
+        act(V("RX", 96 + a, 192, 4), V("RX", 72, 96), F.Copy)
+    ex = listed(V("RX", 96, 192))
+    ts(V("LEX", 0, NA // 4), ex(0, NA // 4), col(cEx), A.subtract)
+    ts(V("LEX", 4, 10 - NA // 4), ex(NA // 4, 6), col(cEx), A.subtract)
+    const(V("KD"), -1.0 / 256)
+    const(V("KD", 16, 96, 16), -17.0 / 256)
+    const(V("KD", 0, 1), 8192.0)
+    const(V("KD", 48, 49), 63.0 / 256)
+    const(V("KD", 80, 81), col(cK80))
+    const(V("KD", 96, 97), col(cKl))
+    act(JJ, V("IO", 0, 48), F.Identity, col(cJ), 1024.0 * S)
+    act(JX, V("IO", 0, 48), F.Identity, col(cJx), 1025.0 * S)
+    act(JK, V("IO", 0, 96), F.Identity, 0.0, S)
+
     quant(V("QU0"), V("SU0"), V("UT"))
-    ts(V("DI", 10, 16), V("DI", 0, 6), 10, A.logical_shift_right)
-    ts(V("DI", 20, 26), V("DI", 0, 6), 1023, A.bitwise_and)
-    scan(V("MP", 0, 96), V("MM", 0, 96), V("RX", C, 480), A.add, A.max)
-    ts(V("DF", 0, 6), V("DI", 10, 16), col(cM0), A.mult, col(cTop), A.add)
-    ts(V("DF", 10, 16), V("DI", 20, 26), col(cH), A.mult)
-    ts(V("LEX"), V("MP", 15, 96, 16), col(cFix), A.subtract)
-    tt(V("DF", 30, 36), V("DF", 0, 6), V("DF", 10, 16), A.add)
-    op("v", lambda: g.vector.tensor_copy(T.QU[:, :].bitcast(dt.uint32), ind(V("QU0"), V("LU"), True)[0]),
-       [V("QU")], [V("QU0"), V("LU")])
+    for lo in (0, 64):
+        off, o = V("LU", lo // 16, lo // 16 + 4), V("QU", lo, lo + 64)
+        cp((o[0].bitcast(dt.uint32),) + o[1:], ind(V("QU0"), off, True))
+        act(V("SU", lo, lo + 64), ind(V("SU0"), off), F.Copy)
+    quant(V("QV"), V("SV"), V("VT"))
+    for b in range(4):
+        quant(V("QC", 128 * b, 128 * b + 128), V("SC", 128 * b, 128 * b + 128), V("EC", 3 - b, 515 - b))
+        act(V("TAB", TW * b, TW * b + C), V("XR", b, 4 * C, 4), F.Copy)
+
+    ts(V("PW", 0, 1), V("PR", 0, 1), col(cD), A.add, col(cRoot), A.min)
+    ts(V("PW", 1, 3), V("PR", 1, 3), col(cD), A.add)
+    ts(V("PL", 24, 27), V("PR", 0, 3), 3.0, A.mult, col(cD3), A.add)
+    cp(V("LL", 6, 12, 2), V("PR", 0, 3))
+    cp(V("LL", 7, 12, 2), V("PR", 0, 3))
+
+    def up(src, dst, lo):
+        cp(V(dst, OUT, C), ind(V(src), V("PW", lo, lo + 3)))
+
+    def near(o, row):
+        ts(o, row(), col(cFix), A.subtract, 16.0 - OUT, A.add)
+
+    up("IO", "RB", 0)
+    up("RB", "IO", 0)
+    near(V("PL", 4, 7), listed(V("IO", OUT, C)))
+    up("IO", "RB", 0)
+    up("RB", "IO", 0)
+    row = listed(V("IO", OUT, C))
+    ts(V("PW", 4, 7), row(), col(cFix), A.subtract)
+    near(V("PL", 8, 11), row)
+    up("IO", "RB", 4)
+    near(V("PL", 12, 15), listed(V("RB", OUT, C)))
+    up("RB", "IO", 4)
+    up("IO", "RB", 4)
+    row = listed(V("RB", OUT, C))
+    ts(V("PW", 8, 14, 2), row(), col(cFix), A.subtract)
+    near(V("PL", 16, 22, 2), row)
+    act(V("XS", 0, OUT), ind(V("SRC"), V("LX", 0, 21)), F.Copy)
+    act(V("XO", 0, OUT), ind(V("SRC"), V("LX", 22, 43)), F.Copy)
+    for c in range(3):
+        lo, off = OUT + 16 * c, V("PW", 8 + 2 * c, 9 + 2 * c)
+        cp(V("XO", lo, lo + 16), ind(V("XO", 0, lo), off))
+        if c < 2:
+            act(V("XO", C + 16 - 16 * c, C + 32 - 16 * c), ind(V("XO", 0, lo), off), F.Copy)
+        act(V("XS", lo, lo + 16), ind(V("XS", 0, lo), off), F.Copy)
+
+    def swap(src, lo, hx, dst, at):
+        tr(V(hx), V(src, lo, lo + 96))
+        tr(V(dst, at, at + 64), V(hx, 16, 80))
+
+    def mid(hb, lo, out):
+        tt(V(out, 0, 48), ind(V(hb, lo + 96, lo + 176), V("LM", 0, 3)), V(hb, lo, lo + 48), A.max)
+        tt(V(out, 48, 96), ind(V(hb, lo, lo + 96), V("LM", 4, 7)), V(hb, lo + 96, lo + 144), A.max)
+
+    swap("XO", OUT, "WX", "XS", OUT + 96)
+    ts(V("LM", 0, 3), listed(V("XS", OUT, C))(), col(cNear), A.subtract, 64.0, A.min)
+    ts(V("LM", 4, 7), listed(V("XS", OUT + 96, OUT + 144))(), col(cNear), A.subtract, 80.0, A.min)
+    mid("XS", OUT, "WC")
+    row = listed(V("WC"))
     for a in range(1, 4):
-        cp(V("LT", 6 * a - 6, 6 * a, 1, 0, 32), V("DF", 30, 36, 1, 32 * a, 32 * a + 32))
-    top(lambda: (act(V("SU"), ind(V("SU0"), V("LU")), F.Copy), const(V("D01"), 1.0), const(V("HT", C, 512), 0.0),
-                 const(V("D01", 0, 192, 4), 0.0), const(V("HT", 0, C), 0.0)), [
-        lambda: (scan(V("MP", 96, 144), V("MM", 0, 48), V("RTX"), A.add, A.max),
-                 scan(V("SCO", 0, 96), V("MM", 0, 96), V("SCN", 96, 192), A.add, A.max)),
-        lambda: ts(V("LTX", 0, 3), V("MP", 111, 144, 16), col(cFix), A.subtract),
-        lambda: ts(V("LA", 0, 6), V("SCO", 15, 96, 16), col(cCA), A.subtract)])
+        ts(V("LT", 6 * a - 6, 6 * a, 1, 0, 32), row(0, 6, 32 * a, 32 * a + 32), col(cFix, 32 * a, 32 * a + 32),
+           A.subtract, 96.0 * a - 288.0, A.add)
+
+    for lo in (18, 178):
+        tt(V("VA", lo, lo + 142, 3), ind(V("FLR"), V("LFL", 0, 3)), JX, A.mult)
 
     PARTS = ((0, CUT, "PK"), (CUT, C, "PA"))
 
-    def inherit(r, wq, wsc, between):
-        n = C + K * r
+    def inherit(r, wq, wsc):
+        tt(V("AA", 16, 64), ind(V("VA", 0, 160), V("PL", 24, 27)), V("VA", 178, 320, 3), A.max)
+        tt(V("AA", 80, 128), ind(V("VA", 160, 320), V("PL", 24, 27)), V("VA", 18, 160, 3), A.max)
+        for k, (src, dst) in enumerate((("AA", "AB"), ("AB", "AA"), ("AA", "HB"))):
+            off = V("PL", 4 * k + 4, 4 * k + 7)
+            tt(V(dst, 16, 64), ind(V(src, 0, 64), off), V(src, 80, 128), A.max)
+            if k < 2:
+                tt(V(dst, 80, 128), ind(V(src, 64, 128), off), V(src, 16, 64), A.max)
+        for c in (1, 2):
+            own = V("HB", 16 + 16 * c, 32 + 16 * c)
+            tt(own, ind(V("HB", 0, 16 + 16 * c), V("PL", 16 + 2 * c, 17 + 2 * c)), own, A.max)
+            cp(V("HB", 96 - 16 * c, 112 - 16 * c), V("HB", 16 * c, 16 * c + 16))
+        swap("HB", 16, "HX", "HB", 112)
+        mid("HB", 16, "CP")
 
-        def plane(b, part, f):
-            lo, hi, _bank = PARTS[part]
-            f(V("ET", 4 * lo + b, 4 * hi, 4), ind(V("TAB", TW * b, TW * b + n), V("PTR", lo // 16, hi // 16)))
+        def part(a, p0=0):
+            return V("CP", 96 * a, 96 * a + 96, 1, p0, p0 + 32)
 
-        def product(part):
-            lo, hi, bank = PARTS[part]
-            quant(V("QE%d" % r, lo, hi), V("SE%d" % r, lo, hi), V("ET", 4 * lo, 4 * hi))
-            mm(V(bank, 0, hi - lo), wq, wsc, V("QE%d" % r, lo, hi), V("SE%d" % r, lo, hi))
+        marks.append(len(calls))
+        cp(part(1), part(0, 32))
+        act(part(2), part(0, 64), F.Copy)
+        act(part(3), part(0, 96), F.Copy)
+        for what, a in TOP:
+            if what == "step":
+                tt(V("CP", 96 * a, 96 * a + 96), ind(V("CP", 0, 96 * a), V("LT", 6 * a - 6, 6 * a)),
+                   V("CP", 96 * a, 96 * a + 96), A.max)
+            else:
+                tr(V("YY", 96 * a, 96 * a + 96, 1, 0, 32), part(a))
+        span = [(lo // 16, hi // 16) for lo, hi, _bank in PARTS]
+        for p, (m0, m1) in enumerate(span):
+            ts(V("OI", 4 * m0, 4 * m1), ind(V("YY", 0, -(-m1 // 6) * 96), V("LEX", 4 * p, 4 * p + (m1 - m0) // 4)),
+               BIG, A.mult)
+        for m0, m1 in span:
+            ts(V("OJ", 4 * m0, 4 * m1, 1, 0, 32), V("OI", 4 * m0, 4 * m1, 1, 0, 32), 1023, A.bitwise_and)
+        for m0, m1 in span:
+            for a in range(4):
+                cp(V("PTR", m0, m1, 1, 32 * a, 32 * a + 32), V("OJ", 4 * m0 + a, 4 * m1, 4, 0, 32))
+        for q, b, m0, m1 in PLANES:
+            if q == "q":
+                lo, hi, bank = PARTS[b]
+                quant(V("QE%d" % r, lo, hi), V("SE%d" % r, lo, hi), V("ET", 4 * lo, 4 * hi))
+                mm(V(bank, 0, hi - lo), wq, wsc, V("QE%d" % r, lo, hi), V("SE%d" % r, lo, hi))
+                continue
+            o = V("ET", 64 * m0 + b, 64 * m1, 4)
+            i = ind(V("TAB", TW * b, TW * b + C + K * r), V("PTR", m0, m1))
+            if q == "v":
+                cp(o, i)
+            else:
+                act(o, i, F.Copy)
 
-        def scalar(o, i):
-            act(o, i, F.Copy)
-
-        plane(2, 0, scalar)
-        plane(3, 0, scalar)
-        plane(0, 0, cp)
-        places(NA, NB, 4 * NA)
-        plane(1, 0, cp)
-        for b in (2, 3, 1):
-            plane(b, 1, scalar)
-        plane(0, 1, cp)
-        product(0)
-        between()
-        product(1)
-
-    vin, vout = "VA", "VB"
     for r, h in enumerate(DIST):
         dst = T.cores[(rank - h) % N]
-        qe, se = V("QE%d" % r), V("SE%d" % r)
-        inherit(r, V("QU"), V("SU"), lambda: None)
+        inherit(r, V("QU"), V("SU"))
         if r == 0:
-            const(V("LMC"), 0.0)
-        for b in range(4):
-            mm(V("PH%d" % b, 0, C), V("QW", 128 * b, 128 * b + 128), V("SW", 128 * b, 128 * b + 128), qe, se)
-        if r == 0:
-            quant(V("LQ", 0, 128), V("LS", 0, 128), V("HT"))
-        if r == 1:
-            quant(V("QV"), V("SV"), V("VT"))
-        ts(V("SK", 0, CUT // 4), V("PK", 0, CUT, 4), 0.0, A.is_gt, col(cWk), A.mult)
-        ts(V("SK", 96, 112), V("PK", 0, 64, 4), 0.0, A.is_gt, col(cWk), A.mult)
-        act(V("SG", 0, CUT), V("PK", 0, CUT), F.Sign)
-        ts(V("SK", CUT // 4, 96), V("PA", 0, C - CUT, 4), 0.0, A.is_gt, col(cWk), A.mult)
-        act(V("SG", CUT, C), V("PA", 0, C - CUT), F.Sign)
-        for x in range(2):
-            act(V("T1H", 96 * x, 96 * x + 96), ind(V("SG"), V("LL", 6 * x, 6 * x + 6)), F.Relu, None, col(cWk))
-        if r == 0:
-            act(V("SCN", 24, 48), V("SCN", 0, 24), F.Copy)
-            const(V("HR"), 16.0)
-            act(V("SCN", 48, 96), V("SCN", 0, 48), F.Copy)
-            const(V("HR", 0, 96, 3), 0.0)
-            ts(V("LP", 0, 4), V("IO", 0, 4), 24.0, A.mult, col(cP1), A.add)
-            ts(V("LP", 4, 8), V("IO", 0, 4), 24.0, A.mult, col(cP2), A.add)
-        tr(V("YK", 0, 96), V("SK", 0, 96))
-        tr(V("YK", 96, 192), V("SK", 16, 112))
-        if r == 0:
-            ts(V("LFW"), V("R6"), 0.5, A.mult, col(cIh), A.add)
+            dma("y", "dq", u8(V("LQ", 96, 128)), u8(V("QE0", 0, 32)))
+            dma("y", "dq", V("LS", 96, 128), V("SE0", 0, 32))
+        act(V("SG", 0, CUT), V("PK", 0, CUT), F.Sign, -TINY)
+        act(V("SG", CUT, C), V("PA", 0, C - CUT), F.Sign, -TINY)
+        cp(V("SG", C, C + 64, 4), V("SG", 0, 64, 4))
+        act(V("T1H", 0, 96), ind(V("SG", 0, C), V("LL", 0, 6)), F.Identity, None, col(cWk))
+        tr(V("YK", 0, 96), V("SG", 0, C, 4))
+        tr(V("YK", 96, 192), V("SG", 64, C + 64, 4))
+        ts(V("T1H", 96, 192), ind(V("SG", 0, C), V("LL", 6, 12)), col(cWk), A.mult)
         scan(V("ZL"), V("D01"), V("YK"), A.mult, A.add)
-        cp(V("TX%d" % r), ind(V("ZL"), V("LTX", 0, 3)))
-        send(dst, "ra%d" % r, V("AR%d" % r), V("TX%d" % r))
-        for b in range(4):
-            act(V("HT", b, C, 4), V("PH%d" % b, 0, C, 4), F.Copy, None, 0.03125)
-        if r == 0:
-            const(V("KD"), -1.0)
-            act(JJ, V("IO", 0, 48), F.Identity, col(cJ), 1024.0 * S)
-            act(JK, V("IO"), F.Identity, 0.0, S)
-            const(V("KD", 16, 96, 16), -17.0)
-            const(V("KD", 0, 1), 4096.0)
-            const(V("KD", 48, 49), 63.0)
-            const(V("KD", 80, 81), col(cK80))
-        act(JB, JJ, F.Identity, float(C + K * r) * S, 1.0)
-        for x in range(2):
-            tr(V("T2H", 96 * x, 96 * x + 96), V("T1H", 96 * x, 96 * x + 96))
-        for x in range(2):
-            tt(V("LMC", 96 * x, 96 * x + 96, 2), V("T2H", 96 * x, 96 * x + 96, 2),
-               V("T2H", 96 * x + 1, 96 * x + 96, 2), A.add)
-        for x in range(2):
-            tt(V("TA", 96 * x, 96 * x + 96), ind(V("LMC", 96 * x, 96 * x + 96), V("LA", 0, 6)), V("SCN", 0, 96),
-               A.not_equal)
-        tr(V("LMH", 96, 288), V("LMC"))
-        act(V("LMH", 0, 96), ind(V("LMH", 96, 288), V("LA", 6, 12)), F.Copy)
+        tr(V("T2H"), V("T1H"))
+        ts(V("TX%d" % r), ind(V("ZL"), V("LTX", 0, 3)), 0.5, A.mult, 7.5, A.add)
+        send(dst, "ra%d" % r, [(V("AR%d" % r), V("TX%d" % r))])
+        tt(V("LMC", 0, 192, 2), V("T2H", 0, 192, 2), V("T2H", 1, 192, 2), A.add)
+        tt(V("TA", 0, 192), ind(V("LMC"), V("LA", 0, 12)), V("SCN", 0, 192), A.not_equal)
         tt(V("TA", 192, 288), V("TA", 0, 96), V("TA", 96, 192), A.mult)
-        quant(V("QH%d" % r), V("SH%d" % r), V("HT"))
         scan(V("TP"), V("HR"), V("TA", 192, 288), A.mult, A.add)
         cp(V("TQ"), ind(V("TP"), V("LP", 0, 4)))
-        tt(V("MP", 0, 48), V("LMH", 0, 48), V("LMH", 48, 96), A.is_equal)
         tt(V("TT"), ind(V("TP"), V("LP", 4, 8)), V("TQ"), A.add)
-        ts(V("MP", 48, 96), V("MP", 0, 48), 100.0, A.mult)
-        lo = 128 + K * r
-        send(dst, "rh%d" % r, u8(V("LQ", lo, lo + K)), u8(V("QH%d" % r, 0, K)))
-        send(dst, "rh%d" % r, V("LS", lo, lo + K), V("SH%d" % r, 0, K))
-        tt(V("MP", 96, 144), V("MP", 48, 96), V("LMH", 48, 96), A.add)
         ar = "AR%d" % r
+        act(V("AC", 96, 192), ind(V("TT", 16, 32), V(ar, 6, 12)), F.Copy)
         cp(V("AC", 0, 96), ind(V("TT", 0, 16), V(ar, 0, 6)))
-        cp(V("AC", 96, 192), ind(V("TT", 16, 32), V(ar, 6, 12)))
         tt(V("AC", 192, 288), ind(V("TT", 32, 48), V(ar, 12, 18)), V("AC", 0, 96), A.add)
-        tt(V("CHS", 0, 96), ind(V("TT", 48, 64), V(ar, 18, 24)), V("AC", 96, 192), A.add)
+        tt(V("AC", 288, 384), ind(V("TT", 48, 64), V(ar, 18, 24)), V("AC", 96, 192), A.add)
+        tt(V("ACI"), V("AC", 192, 288), V("AC", 288, 384), A.add)
+        for c in range(3):
+            ts(V("CHI", 98 * c, 98 * c + 96), V("ACI"), 15 << (8 - 4 * c), A.bitwise_and)
+        for c in range(3):
+            scan(V("CHS", 98 * c, 98 * c + 97), V("KD"), V("CHI", 98 * c, 98 * c + 97), A.add, A.min)
+        ts(V("KI", 0, 3), V("CHS", 96, 294, 98), WHOLE, A.add, WHOLE, A.subtract)
+        for c in range(3):
+            ts(V("KL", c, c + 1), V("CHS", 98 * c + 96, 98 * c + 97), V("KI", c, c + 1), A.subtract, 256.0, A.mult)
+        tr(V("LMH", 96, 288), V("LMC"))
+        act(V("LMH", 0, 96), ind(V("LMH", 96, 288), V("LA", 12, 18)), F.Copy)
+        tt(V("MP", 0, 48), V("LMH", 0, 48), V("LMH", 48, 96), A.is_equal)
+        tt(V("MP", 48, 96), V("MP", 0, 48), V("LMH", 48, 96), A.add)
         cp(V("RF"), V(ar, 24, 48))
-        tt(V("ACI"), V("AC", 192, 288), V("CHS", 0, 96), A.add)
-        tt(V("RF", 1, 24, 2), V("RF", 1, 24, 2), V("RF", 0, 24, 2), A.subtract)
-        act(V("XF"), ind(V("RF"), V("LFW")), F.Copy)
-        for c in range(3):
-            ts(V("CHI", 96 * c, 96 * c + 96), V("ACI"), 8 - 4 * c, A.logical_shift_right, 15, A.bitwise_and)
-        for c in range(3):
-            ts(V("CHF", 96 * c, 96 * c + 96), V("CHI", 96 * c, 96 * c + 96), 256.0, A.mult, col(cKl), A.add)
-        for c in range(3):
-            scan(V("CHS", 96 * c, 96 * c + 96), V("KD"), V("CHF", 96 * c, 96 * c + 96), A.add, A.min)
-        for c in range(3):
-            ts(V("KI", c, c + 1), V("CHS", 96 * c + 95, 96 * c + 96), 1.0 / 256.0, A.mult)
-        for c in range(3):
-            ts(V("KL", c, c + 1), V("KI", c, c + 1), -256.0, A.mult, V("CHS", 96 * c + 95, 96 * c + 96), A.add)
+        act(V("XF"), ind(V("RF"), V("LFW")), F.Identity, -15.0, 2.0)
         tr(V("FW"), V("XF"))
-
-        def constants(b):
-            if r == 0:
-                quant(V("QC", 128 * b, 128 * b + 128), V("SC", 128 * b, 128 * b + 128), V("EC", 3 - b, 515 - b))
-
+        act(JB, JJ, F.Identity, float(C + K * r) * S, 1.0)
+        act(V("UP", 144, 288, 3), V("VA", 18, 160, 3), F.Copy)
+        lo = 128 + K * r
+        for b in range(4):
+            mm(V("PH%d" % b, 0, C), V("QW", 128 * b, 128 * b + 128), V("SW", 128 * b, 128 * b + 128), V("QE%d" % r),
+               V("SE%d" % r))
+            act(V("HT", b, C, 4), V("PH%d" % b, 0, C, 4), F.Copy, None, 0.03125)
+        quant(V("QH%d" % r), V("SH%d" % r), V("HT"))
+        send(dst, "rh%d" % r, [(u8(V("LQ", lo, lo + K)), u8(V("QH%d" % r, 0, K))),
+                               (V("LS", lo, lo + K), V("SH%d" % r, 0, K))])
         kl = V("KL", 0, 3)
-        tt(V("UP", 0, 48), ind(JK, kl), JB, A.add)
-        tt(V("UP", 48, 96), ind(V("FW"), kl), V("LMH", 0, 48), A.not_equal)
-        tt(V("UP", 96, 144), ind(V("FW"), kl), V("MP", 96, 144), A.not_equal)
-        tt(V("UP", 144, 192), V("UP", 48, 96), V(vin, 16, 64), A.add)
-        tt(V("UP", 192, 240), V("UP", 0, 48), V("UP", 96, 144), A.min)
-        constants(0)
-        tt(V(vout, 16, 64), V("UP", 144, 192), V("UP", 192, 240), A.min)
-        tt(V(vout, 80, 128), V("UP", 144, 192), V("UP", 192, 240), A.min)
-        vin, vout = vout, vin
-        for k in range(4):
-            if k < 3:
-                constants(k + 1)
-            local(k, vin)
-            if k == 0 and r == 2:
-                act(V("OF"), V(vin, 16, 64), F.Sign)
-                for G in range(8):
-                    dma("y", "dout", T.ofl[:, 48 * G:48 * G + 48], V("OF", 0, 48, 1, 16 * G, 16 * G + 16, 2))
+        tt(V("UP", 1, 144, 3), ind(V("FW"), kl), V("LMH", 0, 48), A.not_equal)
+        tt(V("UP", 145, 288, 3), ind(V("FW"), kl), V("MP", 48, 96), A.not_equal)
+        tt(V("UP", 146, 288, 3), ind(JK, kl), JB, A.add)
+        for at in (16, 176):
+            scan(V("VA", at, at + 144), V("UP", 0, 144), V("UP", 144, 288), A.add, A.min)
         for b in range(4):
             mm(V("PH%d" % b, 0, 128), V("QC", 128 * b, 128 * b + 128), V("SC", 128 * b, 128 * b + 128),
                V("LQ", lo - 32, lo + K), V("LS", lo - 32, lo + K))
-        seq("HB", 1)
-        seq("HB", 2)
-        swap("HB", "HX")
-        mid("HB", "CP")
-        top(lambda: [act(V("TAB", TW * b + C + K * r, TW * b + C + K * r + K), V("PH%d" % b, 32, 128), F.Copy)
-                     for b in range(4)], [lambda: None] * 3)
+            act(V("TAB", TW * b + C + K * r, TW * b + C + K * r + K), V("PH%d" % b, 32, 128), F.Copy)
 
-    inherit(3, V("QV"), V("SV"), lambda: dma("y", "dend", T.oc[:, 0:4 * CUT], u8(V("QE3", 0, CUT))))
-    dma("y", "dend", T.oc[:, 4 * CUT:4 * C], u8(V("QE3", CUT, C)))
+    act(V("OF"), V("VA", 18, 160, 3), F.Sign)
+    for G in range(8):
+        dma("y", "dout", T.ofl[:, 48 * G:48 * G + 48], V("OF", 0, 48, 1, 16 * G, 16 * G + 16, 2))
+    inherit(3, V("QV"), V("SV"))
     act(V("YO", 0, CUT), V("PK", 0, CUT), F.Copy)
     cp(V("YO", CUT, C), V("PA", 0, C - CUT))
-    dma("s", "dend", T.y[:, 0:CUT], V("YO", 0, CUT))
-    dma("y", "dend", T.y[:, CUT:C], V("YO", CUT, C))
+    for p, (lo, hi, _bank) in enumerate(PARTS):
+        dma("y", "dout", T.oc[:, 4 * lo:4 * hi], u8(V("QE3", lo, hi)))
+        dma("sy"[p], "dout", T.y[:, lo:hi], V("YO", lo, hi))
     for k in range(4):
-        dma("s", "dend", T.osc[4 * k:4 * k + 4, :], V("SE3", 0, C, 1, 32 * k, 32 * k + 4))
-    for sem in SEMAPHORES:
-        if total[sem]:
-            wait("g", sem, total[sem])
+        dma("s", "dout", T.osc[4 * k:4 * k + 4, :], V("SE3", 0, C, 1, 32 * k, 32 * k + 4))
+    issue()

@@ -10,13 +10,17 @@ WHOLE = 1.5 * 2 ** 23
 CUT = 256
 OUT = C - 48
 NEAR = 1000
-PLANES = (("v", 0, 0, 16), ("v", 1, 0, 16), ("s", 2, 0, 16), ("s", 3, 0, 16),
+PLANES = (("s", 0, 0, 6), ("s", 1, 0, 6), ("s", 2, 0, 6), ("s", 3, 0, 6),
+          ("v", 0, 6, 16), ("v", 1, 6, 16), ("s", 2, 6, 16), ("s", 3, 6, 16),
           ("v", 0, 16, 24), ("q", 0, 0, 16), ("v", 1, 16, 20), ("s", 2, 16, 24), ("s", 3, 16, 24), ("s", 1, 20, 24),
           ("q", 1, 16, 24))
 SOON = 600.0
-TOP = (("step", 1), ("step", 2), ("turn", 2), ("step", 3), ("turn", 0), ("turn", 1), ("turn", 3))
+PIECES = ((0, 6), (6, 16), (16, 24))
+TOP = (("step", 1), ("step", 2), ("turn", 0), ("pick", 0), ("turn", 2), ("step", 3), ("low", 0), ("turn", 1),
+       ("out", 0), ("turn", 3), ("pick", 1), ("pick", 2), ("low", 1), ("low", 2), ("out", 1), ("out", 2))
 FP8, U8, U16, I32, F32, BF = "float8_e4m3fn_x4", "uint8", "uint16", "int32", "float32", "bfloat16"
 CYCLE, WAKE, FAR = 0.92, 170.0, 1600.0
+CROSS = 220.0
 
 
 def _sb(n, d):
@@ -32,20 +36,20 @@ SCRATCH = {
     "PI": _sb(1, I32), "CI": _sb(12, I32), "CF": _sb(40, F32),
     "T16": _sb(96, F32), "M1": _sb(192, F32), "MM": _sb(96, F32), "IO": _sb(C, F32),
     "SRC": _sb(2 * OUT, F32), "R6": _sb(6, F32), "RTX": _sb(48, F32), "RX": _sb(192, F32), "SCN": _sb(288, F32),
-    "HR": _sb(96, F32), "KD": _sb(97, F32), "JJ": _sb(240, F32), "D01": _sb(192, BF),
+    "HR": _sb(192, F32), "KD": _sb(200, F32), "JJ": _sb(240, F32), "D01": _sb(192, BF),
     "LU": _sb(8, U16), "LA": _sb(18, U16), "LP": _sb(8, U16), "LTX": _sb(4, U16), "LX": _sb(44, U16),
-    "LFW": _sb(6, U16), "LL": _sb(12, U16), "LFL": _sb(4, U16), "LEX": _sb(8, U16), "PW": _sb(14, U16),
+    "LFW": _sb(6, U16), "LL": _sb(12, U16), "LFL": _sb(4, U16), "LEX": _sb(12, U16), "PW": _sb(14, U16),
     "PL": _sb(28, U16), "LM": _sb(8, U16), "LT": _sb(18, U16), "KL": _sb(4, U16), "PTR": _sb(24, U16),
     "PR": _sb(4, I32), "FLR": _sb(C, I32),
     "RB": _sb(C, F32), "SCO": _sb(624, F32), "XS": _sb(OUT + 176, F32), "XO": _sb(OUT + 96, F32),
     "WX": _sb(96, F32), "WC": _sb(96, F32),
     "VA": _sb(320, F32), "AA": _sb(128, F32), "AB": _sb(128, F32), "HB": _sb(192, F32),
-    "HX": _sb(96, F32), "CP": _sb(C, F32), "YY": _sb(C, F32), "OI": _sb(96, I32), "OJ": _sb(96, I32),
+    "HX": _sb(96, F32), "CP": _sb(C, F32), "YY": _sb(C, F32), "OI": _sb(192, I32), "OJ": _sb(192, I32),
     "YK": _sb(192, BF), "ZL": _sb(192, BF),
     "SG": _sb(C + 64, BF), "T1H": _sb(192, BF), "T2H": _sb(192, BF), "LMH": _sb(288, BF), "LMC": _sb(192, BF),
-    "TA": _sb(288, F32), "TP": _sb(96, F32), "TQ": _sb(64, F32), "TT": _sb(64, F32), "MP": _sb(96, F32),
-    "AC": _sb(C, F32), "ACI": _sb(96, I32), "CHI": _sb(294, I32), "CHS": _sb(294, F32),
-    "KI": _sb(4, F32), "RF": _sb(24, F32), "XF": _sb(96, BF), "FW": _sb(96, BF), "UP": _sb(288, F32),
+    "TA": _sb(192, F32), "TP": _sb(192, I32), "TQ": _sb(128, I32), "TT": _sb(64, F32), "MP": _sb(96, F32),
+    "AC": _sb(C, F32), "CHI": _sb(300, I32), "CHS": _sb(300, F32),
+    "RF": _sb(24, F32), "XF": _sb(96, BF), "FW": _sb(96, BF), "UP": _sb(288, F32),
     "OF": _sb(48, F32), "YO": _sb(C, F32),
 }
 for _r in range(4):
@@ -87,8 +91,8 @@ def rank_program(g, core, T, topo):
         ap = win[0].bitcast(dt.uint32) if words else win[0]
         return (ap.indirect(off[0]), win[1] + off[1], 16 * off[2], False, True)
 
-    def record(q, fn, busy, late, outs, ins, sem, inc, after=()):
-        before = set(after)
+    def record(q, fn, busy, late, outs, ins, sem, inc):
+        before = set()
         regs = [(r, True) for o in outs if isinstance(o, tuple) for r in o[1]]
         regs += [(r, False) for o in ins if isinstance(o, tuple) for r in o[1]]
         for (name, p0, p1, cols), writing in regs:
@@ -127,7 +131,7 @@ def rank_program(g, core, T, topo):
             for m in sorted(before):
                 if m not in at:
                     place(m)
-            t = max([0.0] + [at[m] + calls[m][3] + WAKE for m in before])
+            t = max([0.0] + [at[m] + calls[m][3] + (WAKE if calls[m][0] == q else CROSS) for m in before])
             if q is not None:
                 for lo, hi in taken[q]:
                     if t + busy <= lo:
@@ -220,8 +224,8 @@ def rank_program(g, core, T, topo):
         else:
             op("g", lambda: g.iota(o[0], pat, base, cm), [o], [], 2.0, 130.0)
 
-    def dma(q, sem, o, i):
-        record(q, lambda: Q[q].dma_start(a_(o), a_(i)), 60.0, FAR, [o], [i], sem, 16)
+    def dma(q, sem, o, i, long=1.0):
+        record(q, lambda: Q[q].dma_start(a_(o), a_(i)), 60.0, long * FAR, [o], [i], sem, 16)
 
     def u8(x):
         return (x[0].bitcast(dt.uint8),) + x[1:]
@@ -247,12 +251,12 @@ def rank_program(g, core, T, topo):
         dma("ys"[G % 2], "dpar", V("PR", 0, 3, 1, 16 * G, 16 * G + 16), T.par[:, 3 * G:3 * G + 3])
     ms(V("FLR"), 0)
     for G in range(8):
-        dma("y", "dfl", V("FLR", 0, C, 1, 16 * G, 16 * G + 16, 2), T.fl[:, :])
-    dma("s", "du", V("UT"), T.u[:, :])
-    dma("s", "dx", V("XR"), T.x[:, :])
-    dma("y", "dw", u8(V("QW")), T.wc[:, :])
-    dma("y", "dw", V("SW"), T.ws[:, :])
-    dma("y", "dv", V("VT"), T.v[:, :])
+        dma("y", "dfl", V("FLR", 0, C, 1, 16 * G, 16 * G + 16, 2), T.fl[:, :], 1.4)
+    dma("s", "du", V("UT"), T.u[:, :], 2.0)
+    dma("s", "dx", V("XR"), T.x[:, :], 2.5)
+    dma("y", "dw", u8(V("QW")), T.wc[:, :], 3.5)
+    dma("y", "dw", V("SW"), T.ws[:, :], 3.5)
+    dma("y", "dv", V("VT"), T.v[:, :], 3.5)
 
     iota(V("PI"), [[0, 1]], 0, 1, False)
     iota(V("T16"), [[0, 6], [1, 16]], 0)
@@ -270,17 +274,19 @@ def rank_program(g, core, T, topo):
     iota(V("RX", 24, 48), [[0, 24]], 18)
     for s, d in ((0, 82), (1, -78), (4, -46)):
         iota(V("RX", 24 + s, 48, 6), [[0, 4]], d)
-    iota(V("SCN", 192, 288), [[2, 8], [0, 4], [32, 3]], 0)
-    iota(V("SCN", 0, 192), [[0, 16], [2, 4], [0, 3]], -3)
+    for x in range(2):
+        iota(V("SCN", 192 + x, 288, 2), [[2, 4], [0, 4], [32, 3]], 96 * x)
+    iota(V("SCN", 0, 192), [[0, 8], [2, 4], [0, 6]], -3)
     iota(V("D01", 0, 192, 4), [[0, 48]], 0)
     iota(V("D01", 1, 192, 2), [[0, 96]], 2)
     iota(V("D01", 2, 192, 4), [[0, 6], [-2, 2], [0, 4]], 2)
-    iota(V("HR", 0, 96, 3), [[0, 32]], 0)
-    iota(V("HR", 1, 96, 3), [[0, 32]], 16)
-    iota(V("HR", 2, 96, 3), [[0, 32]], 16)
+    iota(V("HR", 1, 192, 2), [[0, 96]], 1)
+    iota(V("HR", 0, 192, 6), [[0, 32]], 0)
+    iota(V("HR", 2, 192, 6), [[0, 32]], 4096)
+    iota(V("HR", 4, 192, 6), [[0, 32]], 16)
     iota(V("UP", 0, 144, 3), [[0, 48]], 2)
-    iota(V("UP", 2, 144, 3), [[0, 48]], 0)
-    iota(V("CHI", 96, 294, 98), [[0, 3]], 8192, 0, False)
+    for k in (96, 97, 98):
+        iota(V("CHI", k, 300, 100), [[0, 3]], 2 ** 23, 0, False)
     iota(V("LMC", 1, 192, 2), [[0, 96]], 0)
     iota(V("HT", C, 512), [[0, 128]], 0)
     iota(V("ONE"), [[0, 520]], 1)
@@ -302,8 +308,8 @@ def rank_program(g, core, T, topo):
             (cUk, cIh, 16.0, col(cB0)), (cG3, cG, 3.0, 0.0), (cLk, cG, 48.0, col(cI)), (cD3, cG, -144.0, 18.0),
             (cJx, cG, 49200.0 * S, 1024.0 * S), (cFl, cI, 24.0, col(cG3)), (cWk, cB0, -1.0, 2.0),
             (cKl, cH16, -5.0 / 256, 95.0 / 256), (cK80, cH16, 6.0 / 256, -17.0 / 256),
-            (cJ, cG, 49152.0 * S, 1024.0 * S), (cCA, cH16, -1.0, col(cFix)), (cP1, cI12, 0.75, 2.0),
-            (cP2, cI3, 3.0, 14.0), (cNear, cFix, 1.0, -float(NEAR)), (cXs, cH16, 24.0, col(cI)),
+            (cJ, cG, 49152.0 * S, 1024.0 * S), (cCA, cH16, -1.0, col(cFix)), (cP1, cI12, 1.5, 5.0),
+            (cP2, cI3, 6.0, 29.0), (cNear, cFix, 1.0, -float(NEAR)), (cXs, cH16, 24.0, col(cI)),
             (cXo, cH16, -18.0, col(cI)), (cEx, cI3, -4.0, col(cFix))]:
         act(col(k), col(src), F.Identity, bi, sc)
 
@@ -338,28 +344,32 @@ def rank_program(g, core, T, topo):
     ts(V("LL", 0, 6), V("R6"), col(cLk), A.add)
     ts(V("LFL", 0, 3), V("T16", 0, 3), col(cFl), A.add)
     ts(V("LA", 12, 18), V("T16", 0, 6), 32.0, A.mult, col(cI), A.add)
-    ts(V("LP", 0, 4), V("T16", 0, 4), 24.0, A.mult, col(cP1), A.add)
-    ts(V("LP", 4, 8), V("T16", 0, 4), 24.0, A.mult, col(cP2), A.add)
+    ts(V("LP", 0, 4), V("T16", 0, 4), 48.0, A.mult, col(cP1), A.add)
+    ts(V("LP", 4, 8), V("T16", 0, 4), 48.0, A.mult, col(cP2), A.add)
     ts(V("LFW"), V("R6"), 0.5, A.mult, col(cIh), A.add)
     ts(V("LX", 0, 21), V("IO", 0, OUT, 16), col(cXs), A.add, -48.0, A.add)
     ts(V("LX", 22, 43), V("IO", 0, OUT, 16), col(cXo), A.add, 288.0, A.add)
     ts(V("LTX", 0, 3), listed(V("RTX"))(), col(cFix), A.subtract)
     ts(V("LA", 0, 6), listed(V("SCN", 192, 288))(), col(cCA), A.subtract)
-    ts(V("LA", 6, 12), V("LA", 0, 6), 96.0, A.add)
-    NA = CUT // 16
+    ts(V("LA", 6, 12), V("LA", 0, 6), 8.0, A.add)
     act(V("RX", 48, 72), V("RX", 24, 48), F.Identity, 0.0, col(cH))
     tt(V("RX", 72, 96), V("RX", 48, 72), V("RX", 0, 24), A.add)
     for a in range(4):
         act(V("RX", 96 + a, 192, 4), V("RX", 72, 96), F.Copy)
     ex = listed(V("RX", 96, 192))
-    ts(V("LEX", 0, NA // 4), ex(0, NA // 4), col(cEx), A.subtract)
-    ts(V("LEX", 4, 10 - NA // 4), ex(NA // 4, 6), col(cEx), A.subtract)
-    const(V("KD"), -1.0 / 256)
-    const(V("KD", 16, 96, 16), -17.0 / 256)
-    const(V("KD", 0, 1), 8192.0)
-    const(V("KD", 48, 49), 63.0 / 256)
-    const(V("KD", 80, 81), col(cK80))
-    const(V("KD", 96, 97), col(cKl))
+    for k, (m0, m1) in enumerate(PIECES):
+        n0, n1 = m0 // 4, -(-m1 // 4)
+        ts(V("LEX", 4 * k, 4 * k + n1 - n0), ex(n0, n1), col(cEx), A.subtract, -(-m1 // 6) * 96 - 1.0, A.min)
+    const(V("KD", 100, 196), -1.0 / 256)
+    const(V("KD", 116, 196, 16), -17.0 / 256)
+    const(V("KD", 100, 101), 8192.0)
+    const(V("KD", 148, 149), 63.0 / 256)
+    const(V("KD", 180, 181), col(cK80))
+    const(V("KD", 196, 197), col(cKl))
+    const(V("KD", 197, 198), -WHOLE)
+    const(V("KD", 198, 199), WHOLE)
+    act(V("KD", 0, 99), V("KD", 100, 199), F.Identity, 0.0, 65536.0)
+    act(V("KD", 96, 97), V("KD", 196, 197), F.Identity, -68.0, 65536.0)
     act(JJ, V("IO", 0, 48), F.Identity, col(cJ), 1024.0 * S)
     act(JX, V("IO", 0, 48), F.Identity, col(cJx), 1025.0 * S)
     act(JK, V("IO", 0, 96), F.Identity, 0.0, S)
@@ -454,21 +464,24 @@ def rank_program(g, core, T, topo):
         cp(part(1), part(0, 32))
         act(part(2), part(0, 64), F.Copy)
         act(part(3), part(0, 96), F.Copy)
-        for what, a in TOP:
+        for what, k in TOP:
             if what == "step":
-                tt(V("CP", 96 * a, 96 * a + 96), ind(V("CP", 0, 96 * a), V("LT", 6 * a - 6, 6 * a)),
-                   V("CP", 96 * a, 96 * a + 96), A.max)
+                tt(V("CP", 96 * k, 96 * k + 96), ind(V("CP", 0, 96 * k), V("LT", 6 * k - 6, 6 * k)),
+                   V("CP", 96 * k, 96 * k + 96), A.max)
+            elif what == "turn":
+                tr(V("YY", 96 * k, 96 * k + 96, 1, 0, 32), part(k))
             else:
-                tr(V("YY", 96 * a, 96 * a + 96, 1, 0, 32), part(a))
-        span = [(lo // 16, hi // 16) for lo, hi, _bank in PARTS]
-        for p, (m0, m1) in enumerate(span):
-            ts(V("OI", 4 * m0, 4 * m1), ind(V("YY", 0, -(-m1 // 6) * 96), V("LEX", 4 * p, 4 * p + (m1 - m0) // 4)),
-               BIG, A.mult)
-        for m0, m1 in span:
-            ts(V("OJ", 4 * m0, 4 * m1, 1, 0, 32), V("OI", 4 * m0, 4 * m1, 1, 0, 32), 1023, A.bitwise_and)
-        for m0, m1 in span:
-            for a in range(4):
-                cp(V("PTR", m0, m1, 1, 32 * a, 32 * a + 32), V("OJ", 4 * m0 + a, 4 * m1, 4, 0, 32))
+                m0, m1 = PIECES[k]
+                n0, n1, lo = m0 // 4, -(-m1 // 4), 64 * k
+                hi = lo + 16 * (n1 - n0)
+                if what == "pick":
+                    ts(V("OI", lo, hi), ind(V("YY", 0, -(-m1 // 6) * 96), V("LEX", 4 * k, 4 * k + n1 - n0)), BIG, A.mult)
+                elif what == "low":
+                    ts(V("OJ", lo, hi, 1, 0, 32), V("OI", lo, hi, 1, 0, 32), 1023, A.bitwise_and)
+                else:
+                    for a in range(4):
+                        cp(V("PTR", m0, m1, 1, 32 * a, 32 * a + 32),
+                           V("OJ", lo + 4 * m0 - 16 * n0 + a, lo + 4 * m1 - 16 * n0, 4, 0, 32))
         for q, b, m0, m1 in PLANES:
             if q == "q":
                 lo, hi, bank = PARTS[b]
@@ -500,24 +513,26 @@ def rank_program(g, core, T, topo):
         ts(V("TX%d" % r), ind(V("ZL"), V("LTX", 0, 3)), 0.5, A.mult, 7.5, A.add)
         send(dst, "ra%d" % r, [(V("AR%d" % r), V("TX%d" % r))])
         tt(V("LMC", 0, 192, 2), V("T2H", 0, 192, 2), V("T2H", 1, 192, 2), A.add)
-        tt(V("TA", 0, 192), ind(V("LMC"), V("LA", 0, 12)), V("SCN", 0, 192), A.not_equal)
-        tt(V("TA", 192, 288), V("TA", 0, 96), V("TA", 96, 192), A.mult)
-        scan(V("TP"), V("HR"), V("TA", 192, 288), A.mult, A.add)
-        cp(V("TQ"), ind(V("TP"), V("LP", 0, 4)))
-        tt(V("TT"), ind(V("TP"), V("LP", 4, 8)), V("TQ"), A.add)
+        tt(V("TA"), ind(V("LMC"), V("LA", 0, 12)), V("SCN", 0, 192), A.not_equal)
+        scan(V("TP"), V("HR"), V("TA"), A.mult, A.add)
+        for x in range(2):
+            ts(V("TQ", 64 * x, 64 * x + 64), ind(V("TP"), V("LP", 4 * x, 4 * x + 4)), 1, A.logical_shift_right,
+               0x10011, A.bitwise_and)
+        tt(V("TT"), V("TQ", 0, 64), V("TQ", 64, 128), A.add)
         ar = "AR%d" % r
         act(V("AC", 96, 192), ind(V("TT", 16, 32), V(ar, 6, 12)), F.Copy)
         cp(V("AC", 0, 96), ind(V("TT", 0, 16), V(ar, 0, 6)))
         tt(V("AC", 192, 288), ind(V("TT", 32, 48), V(ar, 12, 18)), V("AC", 0, 96), A.add)
         tt(V("AC", 288, 384), ind(V("TT", 48, 64), V(ar, 18, 24)), V("AC", 96, 192), A.add)
-        tt(V("ACI"), V("AC", 192, 288), V("AC", 288, 384), A.add)
+        tt(V("CHI", 0, 96), V("AC", 192, 288), V("AC", 288, 384), A.add)
+        for c in (1, 2):
+            ts(V("CHI", 100 * c, 100 * c + 96), V("CHI", 0, 96), 15 << (8 - 4 * c), A.bitwise_and)
         for c in range(3):
-            ts(V("CHI", 98 * c, 98 * c + 96), V("ACI"), 15 << (8 - 4 * c), A.bitwise_and)
+            kd = 100 * min(c, 1)
+            scan(V("CHS", 100 * c, 100 * c + 99), V("KD", kd, kd + 99), V("CHI", 100 * c, 100 * c + 99), A.add, A.min)
         for c in range(3):
-            scan(V("CHS", 98 * c, 98 * c + 97), V("KD"), V("CHI", 98 * c, 98 * c + 97), A.add, A.min)
-        ts(V("KI", 0, 3), V("CHS", 96, 294, 98), WHOLE, A.add, WHOLE, A.subtract)
-        for c in range(3):
-            ts(V("KL", c, c + 1), V("CHS", 98 * c + 96, 98 * c + 97), V("KI", c, c + 1), A.subtract, 256.0, A.mult)
+            ts(V("KL", c, c + 1), V("CHS", 100 * c + 96, 100 * c + 97), V("CHS", 100 * c + 98, 100 * c + 99),
+               A.subtract, 256.0 if c else 1.0 / 256, A.mult)
         tr(V("LMH", 96, 288), V("LMC"))
         act(V("LMH", 0, 96), ind(V("LMH", 96, 288), V("LA", 12, 18)), F.Copy)
         tt(V("MP", 0, 48), V("LMH", 0, 48), V("LMH", 48, 96), A.is_equal)
@@ -525,8 +540,8 @@ def rank_program(g, core, T, topo):
         cp(V("RF"), V(ar, 24, 48))
         act(V("XF"), ind(V("RF"), V("LFW")), F.Identity, -15.0, 2.0)
         tr(V("FW"), V("XF"))
-        act(JB, JJ, F.Identity, float(C + K * r) * S, 1.0)
-        act(V("UP", 144, 288, 3), V("VA", 18, 160, 3), F.Copy)
+        act(V("UP", 2, 144, 3), JJ, F.Identity, float(C + K * r) * S, 1.0)
+        tt(V("UP", 144, 288, 3), V("VA", 18, 160, 3), V("UP", 2, 144, 3), A.subtract)
         lo = 128 + K * r
         for b in range(4):
             mm(V("PH%d" % b, 0, C), V("QW", 128 * b, 128 * b + 128), V("SW", 128 * b, 128 * b + 128), V("QE%d" % r),
@@ -537,8 +552,8 @@ def rank_program(g, core, T, topo):
                                (V("LS", lo, lo + K), V("SH%d" % r, 0, K))])
         kl = V("KL", 0, 3)
         tt(V("UP", 1, 144, 3), ind(V("FW"), kl), V("LMH", 0, 48), A.not_equal)
-        tt(V("UP", 145, 288, 3), ind(V("FW"), kl), V("MP", 48, 96), A.not_equal)
-        tt(V("UP", 146, 288, 3), ind(JK, kl), JB, A.add)
+        act(V("UP", 145, 288, 3), ind(JK, kl), F.Copy)
+        tt(V("UP", 146, 288, 3), ind(V("FW"), kl), V("MP", 48, 96), A.not_equal)
         for at in (16, 176):
             scan(V("VA", at, at + 144), V("UP", 0, 144), V("UP", 144, 288), A.add, A.min)
         for b in range(4):
@@ -550,11 +565,13 @@ def rank_program(g, core, T, topo):
     for G in range(8):
         dma("y", "dout", T.ofl[:, 48 * G:48 * G + 48], V("OF", 0, 48, 1, 16 * G, 16 * G + 16, 2))
     inherit(3, V("QV"), V("SV"))
-    act(V("YO", 0, CUT), V("PK", 0, CUT), F.Copy)
     cp(V("YO", CUT, C), V("PA", 0, C - CUT))
-    for p, (lo, hi, _bank) in enumerate(PARTS):
+    dma("y", "dout", T.y[:, CUT:C], V("YO", CUT, C))
+    for lo in (0, 128):
+        act(V("YO", lo, lo + 128), V("PK", lo, lo + 128), F.Copy)
+        dma("s", "dout", T.y[:, lo:lo + 128], V("YO", lo, lo + 128))
+    for lo, hi, _bank in PARTS:
         dma("y", "dout", T.oc[:, 4 * lo:4 * hi], u8(V("QE3", lo, hi)))
-        dma("sy"[p], "dout", T.y[:, lo:hi], V("YO", lo, hi))
     for k in range(4):
         dma("s", "dout", T.osc[4 * k:4 * k + 4, :], V("SE3", 0, C, 1, 32 * k, 32 * k + 4))
     issue()

@@ -1,4 +1,4 @@
-from concourse.mybir import dt, AluOpType as A, ActivationFunctionType as F
+from concourse.mybir import dt, AluOpType as A, ActivationFunctionType as F, AxisListType
 
 C, K = 384, 96
 DIST = [1, 2, 3]
@@ -16,11 +16,13 @@ PLANES = (("s", 0, 0, 6), ("s", 1, 0, 6), ("s", 2, 0, 6), ("s", 3, 0, 6),
           ("q", 1, 16, 24))
 SOON = 600.0
 PIECES = ((0, 6), (6, 16), (16, 24))
-TOP = (("step", 1), ("step", 2), ("turn", 0), ("pick", 0), ("turn", 2), ("step", 3), ("low", 0), ("turn", 1),
-       ("out", 0), ("turn", 3), ("pick", 1), ("pick", 2), ("low", 1), ("low", 2), ("out", 1), ("out", 2))
+OUTS = ("ssss", "vvvv", "vvvv")
+TOP = (("in", 0), ("in", 1), ("in", 2), ("in", 3), ("turn", 0), ("step", 1), ("pick", 0), ("step", 2), ("out", 0),
+       ("step", 3), ("turn", 1), ("turn", 2), ("turn", 3), ("pick", 1), ("pick", 2), ("out", 1), ("out", 2))
 FP8, U8, U16, I32, F32, BF = "float8_e4m3fn_x4", "uint8", "uint16", "int32", "float32", "bfloat16"
-CYCLE, WAKE, FAR = 0.92, 170.0, 1600.0
-CROSS = 220.0
+CYCLE, WAKE, FAR = 1.0, 175.0, 1600.0
+TOL = 40.0
+CROSS = 200.0
 
 
 def _sb(n, d):
@@ -41,14 +43,14 @@ SCRATCH = {
     "LFW": _sb(6, U16), "LL": _sb(12, U16), "LFL": _sb(4, U16), "LEX": _sb(12, U16), "PW": _sb(14, U16),
     "PL": _sb(28, U16), "LM": _sb(8, U16), "LT": _sb(18, U16), "KL": _sb(4, U16), "PTR": _sb(24, U16),
     "PR": _sb(4, I32), "FLR": _sb(C, I32),
-    "RB": _sb(C, F32), "SCO": _sb(624, F32), "XS": _sb(OUT + 176, F32), "XO": _sb(OUT + 96, F32),
+    "RB": _sb(C, F32), "RC": _sb(192, F32), "EYE": _sb(48, F32), "SCO": _sb(624, F32), "XS": _sb(OUT + 176, F32), "XO": _sb(OUT + 96, F32),
     "WX": _sb(96, F32), "WC": _sb(96, F32),
     "VA": _sb(320, F32), "AA": _sb(128, F32), "AB": _sb(128, F32), "HB": _sb(192, F32),
-    "HX": _sb(96, F32), "CP": _sb(C, F32), "YY": _sb(C, F32), "OI": _sb(192, I32), "OJ": _sb(192, I32),
+    "HX": _sb(96, F32), "MD": _sb(C, F32), "CP": _sb(C, I32), "YY": _sb(C, I32), "OJ": _sb(192, I32),
     "YK": _sb(192, BF), "ZL": _sb(192, BF),
-    "SG": _sb(C + 64, BF), "T1H": _sb(192, BF), "T2H": _sb(192, BF), "LMH": _sb(288, BF), "LMC": _sb(192, BF),
+    "SG": _sb(C + 64, BF), "T1H": _sb(192, BF), "T2H": _sb(192, BF), "LMH": _sb(288, BF), "LMC": _sb(208, BF), "D2": _sb(192, BF),
     "TA": _sb(192, F32), "TP": _sb(192, I32), "TQ": _sb(128, I32), "TT": _sb(64, F32), "MP": _sb(96, F32),
-    "AC": _sb(C, F32), "CHI": _sb(300, I32), "CHS": _sb(300, F32),
+    "AC": _sb(C, F32), "ACI": _sb(C + 12, I32), "D4": _sb(C, F32), "CHI": _sb(300, I32), "CHS": _sb(300, F32),
     "RF": _sb(24, F32), "XF": _sb(96, BF), "FW": _sb(96, BF), "UP": _sb(288, F32),
     "OF": _sb(48, F32), "YO": _sb(C, F32),
 }
@@ -134,7 +136,7 @@ def rank_program(g, core, T, topo):
             t = max([0.0] + [at[m] + calls[m][3] + (WAKE if calls[m][0] == q else CROSS) for m in before])
             if q is not None:
                 for lo, hi in taken[q]:
-                    if t + busy <= lo:
+                    if t + busy <= lo + TOL and t < lo and q != "y":
                         break
                     t = max(t, hi)
                 taken[q].append((t, t + busy))
@@ -230,9 +232,7 @@ def rank_program(g, core, T, topo):
     def u8(x):
         return (x[0].bitcast(dt.uint8),) + x[1:]
 
-    NE = 8
-
-    def send(dst, sem, pairs):
+    def send(dst, sem, pairs, NE=8):
         rid, pid, _se = topo.addr(dst)
         m = 0
         for e in topo.engines(core, dst)[:NE]:
@@ -252,8 +252,8 @@ def rank_program(g, core, T, topo):
     ms(V("FLR"), 0)
     for G in range(8):
         dma("y", "dfl", V("FLR", 0, C, 1, 16 * G, 16 * G + 16, 2), T.fl[:, :], 1.4)
-    dma("s", "du", V("UT"), T.u[:, :], 2.0)
-    dma("s", "dx", V("XR"), T.x[:, :], 2.5)
+    dma("y", "dx", V("XR"), T.x[:, :], 3.0)
+    dma("y", "du", V("UT"), T.u[:, :], 3.0)
     dma("y", "dw", u8(V("QW")), T.wc[:, :], 3.5)
     dma("y", "dw", V("SW"), T.ws[:, :], 3.5)
     dma("y", "dv", V("VT"), T.v[:, :], 3.5)
@@ -285,9 +285,12 @@ def rank_program(g, core, T, topo):
     iota(V("HR", 2, 192, 6), [[0, 32]], 4096)
     iota(V("HR", 4, 192, 6), [[0, 32]], 16)
     iota(V("UP", 0, 144, 3), [[0, 48]], 2)
-    for k in (96, 97, 98):
-        iota(V("CHI", k, 300, 100), [[0, 3]], 2 ** 23, 0, False)
-    iota(V("LMC", 1, 192, 2), [[0, 96]], 0)
+    for tail in (V("ACI", C, C + 12), V("CHI", 196, 200), V("CHI", 296, 300)):
+        iota(tail, [[0, tail[2]]], 2 ** 23, 0, False)
+    iota(V("D4"), [[0, C]], 1)
+    iota(V("D4", 0, C, 4), [[0, 96]], 0)
+    iota(V("LMC", 207, 208), [[0, 1]], 0)
+    iota(V("D2"), [[0, 96], [1, 2]], 0)
     iota(V("HT", C, 512), [[0, 128]], 0)
     iota(V("ONE"), [[0, 520]], 1)
     op("g", lambda: g.affine_select(T.EC[:, :], T.ONE[:, :], [[-1, 520]], A.is_equal, 0.0, 3, 4), [V("EC")], [V("ONE")],
@@ -325,8 +328,9 @@ def rank_program(g, core, T, topo):
                          ("HB", 176, 192), ("XS", C, C + 48), ("XS", OUT + 160, OUT + 176), ("XO", C + 32, C + 48),
                          ("VA", 0, 320)):
         const(V(name, lo, hi), 0.0)
-    iota(V("CP", 96, C), [[0, C - 96]], 0)
-    iota(V("YY"), [[0, C]], 0)
+    iota(V("CP", 0, 96), [[0, 96]], 0, 0, False)
+    iota(V("MD", 96, C), [[0, C - 96]], 0)
+    iota(V("YY"), [[0, C]], 0, 0, False)
     ms(V("LT"), 0)
     ts(V("M1", 0, 96), V("T16"), col(cI), A.is_equal, -3.0 * BIG, A.mult)
     ts(V("M1", 96, 192), V("T16"), col(cI1), A.is_equal, BIG, A.mult)
@@ -396,21 +400,29 @@ def rank_program(g, core, T, topo):
     def near(o, row):
         ts(o, row(), col(cFix), A.subtract, 16.0 - OUT, A.add)
 
+    def aside(src, lo):
+        act(V("RC", lo, lo + 48), V(src, OUT, C), F.Copy)
+        return V("RC", lo, lo + 48)
+
+    def own(src, lo, o, st, at):
+        tt(V("RC", at, at + 48), ind(V(src), V("PW", lo, lo + 3)), V("EYE"), A.mult)
+        for c in range(3):
+            x, y = V("PW", o + st * c, o + st * c + 1), V("RC", at + 16 * c, at + 16 * c + 16)
+            op("v", lambda x=x, y=y: g.vector.tensor_reduce(x[0], y[0], AxisListType.X, A.max), [x], [y])
+
+    ts(V("EYE"), V("T16", 0, 48), col(cI), A.is_equal)
     up("IO", "RB", 0)
     up("RB", "IO", 0)
-    near(V("PL", 4, 7), listed(V("IO", OUT, C)))
+    near(V("PL", 4, 7), listed(aside("IO", 0)))
     up("IO", "RB", 0)
+    own("RB", 0, 4, 1, 96)
     up("RB", "IO", 0)
-    row = listed(V("IO", OUT, C))
-    ts(V("PW", 4, 7), row(), col(cFix), A.subtract)
-    near(V("PL", 8, 11), row)
+    ts(V("PL", 8, 11), V("PW", 4, 7), 16.0 - OUT, A.add)
     up("IO", "RB", 4)
-    near(V("PL", 12, 15), listed(V("RB", OUT, C)))
+    near(V("PL", 12, 15), listed(aside("RB", 48)))
     up("RB", "IO", 4)
-    up("IO", "RB", 4)
-    row = listed(V("RB", OUT, C))
-    ts(V("PW", 8, 14, 2), row(), col(cFix), A.subtract)
-    near(V("PL", 16, 22, 2), row)
+    own("IO", 4, 8, 2, 144)
+    ts(V("PL", 16, 22, 2), V("PW", 8, 14, 2), 16.0 - OUT, A.add)
     act(V("XS", 0, OUT), ind(V("SRC"), V("LX", 0, 21)), F.Copy)
     act(V("XO", 0, OUT), ind(V("SRC"), V("LX", 22, 43)), F.Copy)
     for c in range(3):
@@ -453,21 +465,22 @@ def rank_program(g, core, T, topo):
         for c in (1, 2):
             own = V("HB", 16 + 16 * c, 32 + 16 * c)
             tt(own, ind(V("HB", 0, 16 + 16 * c), V("PL", 16 + 2 * c, 17 + 2 * c)), own, A.max)
-            cp(V("HB", 96 - 16 * c, 112 - 16 * c), V("HB", 16 * c, 16 * c + 16))
+            act(V("HB", 96 - 16 * c, 112 - 16 * c), V("HB", 16 * c, 16 * c + 16), F.Copy)
         swap("HB", 16, "HX", "HB", 112)
-        mid("HB", 16, "CP")
+        mid("HB", 16, "MD")
 
-        def part(a, p0=0):
-            return V("CP", 96 * a, 96 * a + 96, 1, p0, p0 + 32)
+        def part(a):
+            return V("CP", 96 * a, 96 * a + 96, 1, 0, 32)
 
         marks.append(len(calls))
-        cp(part(1), part(0, 32))
-        act(part(2), part(0, 64), F.Copy)
-        act(part(3), part(0, 96), F.Copy)
         for what, k in TOP:
-            if what == "step":
+            if what == "in" and k == 0:
+                ts(part(0), V("MD", 0, 96, 1, 0, 32), BIG, A.mult)
+            elif what == "in":
+                act(V("MD", 96 * k, 96 * k + 96, 1, 0, 32), V("MD", 0, 96, 1, 32 * k, 32 * k + 32), F.Copy, None, BIG)
+            elif what == "step":
                 tt(V("CP", 96 * k, 96 * k + 96), ind(V("CP", 0, 96 * k), V("LT", 6 * k - 6, 6 * k)),
-                   V("CP", 96 * k, 96 * k + 96), A.max)
+                   V("MD", 96 * k, 96 * k + 96), A.max)
             elif what == "turn":
                 tr(V("YY", 96 * k, 96 * k + 96, 1, 0, 32), part(k))
             else:
@@ -475,13 +488,16 @@ def rank_program(g, core, T, topo):
                 n0, n1, lo = m0 // 4, -(-m1 // 4), 64 * k
                 hi = lo + 16 * (n1 - n0)
                 if what == "pick":
-                    ts(V("OI", lo, hi), ind(V("YY", 0, -(-m1 // 6) * 96), V("LEX", 4 * k, 4 * k + n1 - n0)), BIG, A.mult)
-                elif what == "low":
-                    ts(V("OJ", lo, hi, 1, 0, 32), V("OI", lo, hi, 1, 0, 32), 1023, A.bitwise_and)
+                    ts(V("OJ", lo, hi), ind(V("YY", 0, -(-m1 // 6) * 96), V("LEX", 4 * k, 4 * k + n1 - n0)), 1023,
+                       A.bitwise_and)
                 else:
                     for a in range(4):
-                        cp(V("PTR", m0, m1, 1, 32 * a, 32 * a + 32),
-                           V("OJ", lo + 4 * m0 - 16 * n0 + a, lo + 4 * m1 - 16 * n0, 4, 0, 32))
+                        o = V("PTR", m0, m1, 1, 32 * a, 32 * a + 32)
+                        i = V("OJ", lo + 4 * m0 - 16 * n0 + a, lo + 4 * m1 - 16 * n0, 4, 0, 32)
+                        if OUTS[k][a] == "v":
+                            cp(o, i)
+                        else:
+                            act(o, i, F.Copy)
         for q, b, m0, m1 in PLANES:
             if q == "q":
                 lo, hi, bank = PARTS[b]
@@ -504,36 +520,39 @@ def rank_program(g, core, T, topo):
         act(V("SG", 0, CUT), V("PK", 0, CUT), F.Sign, -TINY)
         act(V("SG", CUT, C), V("PA", 0, C - CUT), F.Sign, -TINY)
         cp(V("SG", C, C + 64, 4), V("SG", 0, 64, 4))
-        act(V("T1H", 0, 96), ind(V("SG", 0, C), V("LL", 0, 6)), F.Identity, None, col(cWk))
-        tr(V("YK", 0, 96), V("SG", 0, C, 4))
-        tr(V("YK", 96, 192), V("SG", 64, C + 64, 4))
-        ts(V("T1H", 96, 192), ind(V("SG", 0, C), V("LL", 6, 12)), col(cWk), A.mult)
-        scan(V("ZL"), V("D01"), V("YK"), A.mult, A.add)
-        tr(V("T2H"), V("T1H"))
-        ts(V("TX%d" % r), ind(V("ZL"), V("LTX", 0, 3)), 0.5, A.mult, 7.5, A.add)
-        send(dst, "ra%d" % r, [(V("AR%d" % r), V("TX%d" % r))])
-        tt(V("LMC", 0, 192, 2), V("T2H", 0, 192, 2), V("T2H", 1, 192, 2), A.add)
-        tt(V("TA"), ind(V("LMC"), V("LA", 0, 12)), V("SCN", 0, 192), A.not_equal)
+        keys = [lambda: tr(V("YK", 0, 96), V("SG", 0, C, 4)),
+                lambda: tr(V("YK", 96, 192), V("SG", 64, C + 64, 4)),
+                lambda: scan(V("ZL"), V("D01"), V("YK"), A.mult, A.add),
+                lambda: ts(V("TX%d" % r), ind(V("ZL"), V("LTX", 0, 3)), 0.5, A.mult, 7.5, A.add),
+                lambda: send(dst, "ra%d" % r, [(V("AR%d" % r), V("TX%d" % r))])]
+        locks = [lambda: act(V("T1H", 0, 96), ind(V("SG", 0, C), V("LL", 0, 6)), F.Identity, None, col(cWk)),
+                 lambda: ts(V("T1H", 96, 192), ind(V("SG", 0, C), V("LL", 6, 12)), col(cWk), A.mult),
+                 lambda: tr(V("T2H"), V("T1H")),
+                 lambda: scan(V("LMC", 15, 207), V("D2"), V("T2H"), A.mult, A.add)]
+        for call in (keys[:2] + locks[:2] + keys[2:] + locks[2:] if r == 0 else locks + keys):
+            call()
+        tt(V("TA"), ind(V("LMC", 16, 208), V("LA", 0, 12)), V("SCN", 0, 192), A.not_equal)
         scan(V("TP"), V("HR"), V("TA"), A.mult, A.add)
-        for x in range(2):
-            ts(V("TQ", 64 * x, 64 * x + 64), ind(V("TP"), V("LP", 4 * x, 4 * x + 4)), 1, A.logical_shift_right,
-               0x10011, A.bitwise_and)
+        ts(V("TQ"), ind(V("TP"), V("LP")), 1, A.logical_shift_right, 0x10011, A.bitwise_and)
         tt(V("TT"), V("TQ", 0, 64), V("TQ", 64, 128), A.add)
         ar = "AR%d" % r
-        act(V("AC", 96, 192), ind(V("TT", 16, 32), V(ar, 6, 12)), F.Copy)
-        cp(V("AC", 0, 96), ind(V("TT", 0, 16), V(ar, 0, 6)))
-        tt(V("AC", 192, 288), ind(V("TT", 32, 48), V(ar, 12, 18)), V("AC", 0, 96), A.add)
-        tt(V("AC", 288, 384), ind(V("TT", 48, 64), V(ar, 18, 24)), V("AC", 96, 192), A.add)
-        tt(V("CHI", 0, 96), V("AC", 192, 288), V("AC", 288, 384), A.add)
+        for q in range(4):
+            o, i = V("AC", q, C, 4), ind(V("TT", 16 * q, 16 * q + 16), V(ar, 6 * q, 6 * q + 6))
+            if q % 2:
+                act(o, i, F.Copy)
+            else:
+                cp(o, i)
+        scan(V("ACI", 0, C), V("D4"), V("AC"), A.mult, A.add)
         for c in (1, 2):
-            ts(V("CHI", 100 * c, 100 * c + 96), V("CHI", 0, 96), 15 << (8 - 4 * c), A.bitwise_and)
+            ts(V("CHI", 100 * c, 100 * c + 96), V("ACI", 3, C, 4), 15 << (8 - 4 * c), A.bitwise_and)
         for c in range(3):
             kd = 100 * min(c, 1)
-            scan(V("CHS", 100 * c, 100 * c + 99), V("KD", kd, kd + 99), V("CHI", 100 * c, 100 * c + 99), A.add, A.min)
+            scan(V("CHS", 100 * c, 100 * c + 99), V("KD", kd, kd + 99),
+                 V("CHI", 100 * c, 100 * c + 99) if c else V("ACI", 3, C + 12, 4), A.add, A.min)
         for c in range(3):
             ts(V("KL", c, c + 1), V("CHS", 100 * c + 96, 100 * c + 97), V("CHS", 100 * c + 98, 100 * c + 99),
                A.subtract, 256.0 if c else 1.0 / 256, A.mult)
-        tr(V("LMH", 96, 288), V("LMC"))
+        tr(V("LMH", 96, 288), V("LMC", 16, 208))
         act(V("LMH", 0, 96), ind(V("LMH", 96, 288), V("LA", 12, 18)), F.Copy)
         tt(V("MP", 0, 48), V("LMH", 0, 48), V("LMH", 48, 96), A.is_equal)
         tt(V("MP", 48, 96), V("MP", 0, 48), V("LMH", 48, 96), A.add)
@@ -565,13 +584,13 @@ def rank_program(g, core, T, topo):
     for G in range(8):
         dma("y", "dout", T.ofl[:, 48 * G:48 * G + 48], V("OF", 0, 48, 1, 16 * G, 16 * G + 16, 2))
     inherit(3, V("QV"), V("SV"))
+    for lo, hi, _bank in PARTS:
+        dma("y", "dout", T.oc[:, 4 * lo:4 * hi], u8(V("QE3", lo, hi)))
     cp(V("YO", CUT, C), V("PA", 0, C - CUT))
     dma("y", "dout", T.y[:, CUT:C], V("YO", CUT, C))
     for lo in (0, 128):
         act(V("YO", lo, lo + 128), V("PK", lo, lo + 128), F.Copy)
         dma("s", "dout", T.y[:, lo:lo + 128], V("YO", lo, lo + 128))
-    for lo, hi, _bank in PARTS:
-        dma("y", "dout", T.oc[:, 4 * lo:4 * hi], u8(V("QE3", lo, hi)))
     for k in range(4):
         dma("s", "dout", T.osc[4 * k:4 * k + 4, :], V("SE3", 0, C, 1, 32 * k, 32 * k + 4))
     issue()

@@ -14,9 +14,13 @@ PLANES = (("s", 0, 0, 6), ("s", 1, 0, 6), ("s", 2, 0, 6), ("s", 3, 0, 6),
           ("v", 0, 6, 16), ("v", 1, 6, 16), ("s", 2, 6, 16), ("s", 3, 6, 16),
           ("v", 0, 16, 24), ("q", 0, 0, 16), ("v", 1, 16, 20), ("s", 2, 16, 24), ("s", 3, 16, 24), ("s", 1, 20, 24),
           ("q", 1, 16, 24))
+FIRST = 0.8
+FLAGS = 1.4
 SOON = 600.0
 PIECES = ((0, 6), (6, 16), (16, 24))
-OUTS = ("ssss", "vvvv", "vvvv")
+OUTS = ("ssss", "vvss", "vvvv")
+LANES = ((0, 2), (2, 3))
+SCANS = ((0, 1), (1, 2), (2, 3))
 TOP = (("in", 0), ("in", 1), ("in", 2), ("in", 3), ("turn", 0), ("step", 1), ("pick", 0), ("step", 2), ("out", 0),
        ("step", 3), ("turn", 1), ("turn", 2), ("turn", 3), ("pick", 1), ("pick", 2), ("out", 1), ("out", 2))
 FP8, U8, U16, I32, F32, BF = "float8_e4m3fn_x4", "uint8", "uint16", "int32", "float32", "bfloat16"
@@ -38,14 +42,14 @@ SCRATCH = {
     "PI": _sb(1, I32), "CI": _sb(12, I32), "CF": _sb(40, F32),
     "T16": _sb(96, F32), "M1": _sb(192, F32), "MM": _sb(96, F32), "IO": _sb(C, F32),
     "SRC": _sb(2 * OUT, F32), "R6": _sb(6, F32), "RTX": _sb(48, F32), "RX": _sb(192, F32), "SCN": _sb(288, F32),
-    "HR": _sb(192, F32), "KD": _sb(200, F32), "JJ": _sb(240, F32), "D01": _sb(192, BF),
-    "LU": _sb(8, U16), "LA": _sb(18, U16), "LP": _sb(8, U16), "LTX": _sb(4, U16), "LX": _sb(44, U16),
+    "HR": _sb(96, F32), "KD": _sb(200, F32), "JJ": _sb(240, F32), "D01": _sb(192, BF),
+    "LU": _sb(8, U16), "LA": _sb(18, U16), "LP": _sb(4, U16), "LTX": _sb(4, U16), "LX": _sb(44, U16),
     "LFW": _sb(6, U16), "LL": _sb(12, U16), "LFL": _sb(4, U16), "LEX": _sb(12, U16), "PW": _sb(14, U16),
-    "PL": _sb(28, U16), "LM": _sb(8, U16), "LT": _sb(18, U16), "KL": _sb(4, U16), "PTR": _sb(24, U16),
+    "PL": _sb(28, U16), "LM": _sb(8, U16), "LT": _sb(18, U16), "KL": _sb(6, U16), "PTR": _sb(24, U16),
     "PR": _sb(4, I32), "FLR": _sb(C, I32),
     "RB": _sb(C, F32), "RC": _sb(192, F32), "EYE": _sb(48, F32), "SCO": _sb(624, F32), "XS": _sb(OUT + 176, F32), "XO": _sb(OUT + 96, F32),
     "WX": _sb(96, F32), "WC": _sb(96, F32),
-    "VA": _sb(320, F32), "AA": _sb(128, F32), "AB": _sb(128, F32), "HB": _sb(192, F32),
+    "VA": _sb(320, F32), "AA": _sb(128, F32), "AB": _sb(128, F32), "AD": _sb(128, F32), "HB": _sb(192, F32),
     "HX": _sb(96, F32), "MD": _sb(C, F32), "CP": _sb(C, I32), "YY": _sb(C, I32), "OJ": _sb(192, I32),
     "YK": _sb(192, BF), "ZL": _sb(192, BF),
     "SG": _sb(C + 64, BF), "T1H": _sb(192, BF), "T2H": _sb(192, BF), "LMH": _sb(288, BF), "LMC": _sb(208, BF), "D2": _sb(192, BF),
@@ -66,7 +70,7 @@ for _n in ("PK", "PA", "PH0", "PH1", "PH2", "PH3"):
     SCRATCH[_n] = ("psum", [128, 512], F32)
 
 SEMAPHORES = ["cv", "cs", "ct", "cg", "dpar", "dx", "du", "dfl", "dw", "dv", "dq", "dout", "sent",
-              "ra0", "ra1", "ra2", "rh0", "rh1", "rh2"]
+              "ra0", "ra1", "ra2", "rb0", "rb1", "rb2", "rh0", "rh1", "rh2"]
 
 
 def rank_program(g, core, T, topo):
@@ -175,7 +179,7 @@ def rank_program(g, core, T, topo):
                 fn()
             else:
                 fn().then_inc(T.sem[sem], inc)
-        for s in SEMAPHORES:
+        for s in sorted(SEMAPHORES, key=lambda s: max(at[k] + calls[k][3] for k in range(n) if calls[k][5] == s)):
             g.wait_ge(T.sem[s], whole[s])
 
     def a_(x):
@@ -208,13 +212,13 @@ def rank_program(g, core, T, topo):
     def quant(qo, so, i):
         op("v", lambda: g.vector.quantize_mx(qo[0], so[0], i[0]), [qo, so], [i], 0.27, 12.0)
 
-    def act(o, i, f, bias=None, scale=None):
+    def act(o, i, f, bias=None, scale=None, behind=None):
         kw = {}
         if bias is not None:
             kw["bias"] = a_(bias)
         if scale is not None:
             kw["scale"] = a_(scale)
-        op("s", lambda: g.scalar.activation(o[0], i[0], f, **kw), [o], [i, bias, scale])
+        op("s", lambda: g.scalar.activation(o[0], i[0], f, **kw), [o], [i, bias, scale, behind])
 
     def mm(o, wq, wsc, xq, xsc):
         op("t", lambda: g.tensor.matmul_mx(o[0], wq[0], wsc[0], xq[0], xsc[0], True, True), [o], [xq, xsc, wq, wsc],
@@ -232,7 +236,9 @@ def rank_program(g, core, T, topo):
     def u8(x):
         return (x[0].bitcast(dt.uint8),) + x[1:]
 
-    def send(dst, sem, pairs, NE=8):
+    NE = 8
+
+    def send(dst, sem, pairs, long=1.0):
         rid, pid, _se = topo.addr(dst)
         m = 0
         for e in topo.engines(core, dst)[:NE]:
@@ -242,16 +248,16 @@ def rank_program(g, core, T, topo):
             return record("g", lambda: g.remote_dma(o[0], i[0], T.sem[sem], T.sem["sent"], pid, rid, m), 200.0, 200.0,
                           [], [i], "sent", NE)
         sent = [one(o, i) for o, i in pairs]
-        calls.append((None, None, 0.0, FAR, set(sent), sem, NE * len(pairs)))
+        calls.append((None, None, 0.0, long * FAR, set(sent), sem, NE * len(pairs)))
         for o, _i in pairs:
             for (name, p0, p1, cols) in o[1]:
                 log.setdefault(name, []).append((True, len(calls) - 1, p0, p1, cols))
 
     for G in range(8):
-        dma("ys"[G % 2], "dpar", V("PR", 0, 3, 1, 16 * G, 16 * G + 16), T.par[:, 3 * G:3 * G + 3])
+        dma("ys"[G % 2], "dpar", V("PR", 0, 3, 1, 16 * G, 16 * G + 16), T.par[:, 3 * G:3 * G + 3], FIRST)
     ms(V("FLR"), 0)
     for G in range(8):
-        dma("y", "dfl", V("FLR", 0, C, 1, 16 * G, 16 * G + 16, 2), T.fl[:, :], 1.4)
+        dma("y", "dfl", V("FLR", 0, C, 1, 16 * G, 16 * G + 16, 2), T.fl[:, :], FLAGS)
     dma("y", "dx", V("XR"), T.x[:, :], 3.0)
     dma("y", "du", V("UT"), T.u[:, :], 3.0)
     dma("y", "dw", u8(V("QW")), T.wc[:, :], 3.5)
@@ -276,14 +282,14 @@ def rank_program(g, core, T, topo):
         iota(V("RX", 24 + s, 48, 6), [[0, 4]], d)
     for x in range(2):
         iota(V("SCN", 192 + x, 288, 2), [[2, 4], [0, 4], [32, 3]], 96 * x)
-    iota(V("SCN", 0, 192), [[0, 8], [2, 4], [0, 6]], -3)
+    iota(V("SCN", 0, 96), [[0, 4], [2, 4], [0, 6]], -3)
     iota(V("D01", 0, 192, 4), [[0, 48]], 0)
     iota(V("D01", 1, 192, 2), [[0, 96]], 2)
     iota(V("D01", 2, 192, 4), [[0, 6], [-2, 2], [0, 4]], 2)
-    iota(V("HR", 1, 192, 2), [[0, 96]], 1)
-    iota(V("HR", 0, 192, 6), [[0, 32]], 0)
-    iota(V("HR", 2, 192, 6), [[0, 32]], 4096)
-    iota(V("HR", 4, 192, 6), [[0, 32]], 16)
+    iota(V("HR", 1, 96, 2), [[0, 48]], 1)
+    iota(V("HR", 0, 96, 6), [[0, 16]], 0)
+    iota(V("HR", 2, 96, 6), [[0, 16]], 4096)
+    iota(V("HR", 4, 96, 6), [[0, 16]], 16)
     iota(V("UP", 0, 144, 3), [[0, 48]], 2)
     for tail in (V("ACI", C, C + 12), V("CHI", 196, 200), V("CHI", 296, 300)):
         iota(tail, [[0, tail[2]]], 2 ** 23, 0, False)
@@ -324,7 +330,8 @@ def rank_program(g, core, T, topo):
     act(V("SRC", OUT + 48, OUT + 96), V("IO", 0, 48), F.Copy)
     for a in (1, 2):
         act(V("SRC", OUT + 96 * a, OUT + 96 * a + 96), V("SRC", OUT, OUT + 96), F.Identity, 96.0 * a, 1.0)
-    for name, lo, hi in (("AA", 0, 16), ("AA", 64, 80), ("AB", 0, 16), ("AB", 64, 80), ("HB", 0, 16), ("HB", 96, 112),
+    for name, lo, hi in (("AA", 0, 16), ("AA", 64, 80), ("AB", 0, 16), ("AB", 64, 80), ("AD", 0, 16),
+                         ("HB", 0, 16), ("HB", 96, 112),
                          ("HB", 176, 192), ("XS", C, C + 48), ("XS", OUT + 160, OUT + 176), ("XO", C + 32, C + 48),
                          ("VA", 0, 320)):
         const(V(name, lo, hi), 0.0)
@@ -348,8 +355,8 @@ def rank_program(g, core, T, topo):
     ts(V("LL", 0, 6), V("R6"), col(cLk), A.add)
     ts(V("LFL", 0, 3), V("T16", 0, 3), col(cFl), A.add)
     ts(V("LA", 12, 18), V("T16", 0, 6), 32.0, A.mult, col(cI), A.add)
-    ts(V("LP", 0, 4), V("T16", 0, 4), 48.0, A.mult, col(cP1), A.add)
-    ts(V("LP", 4, 8), V("T16", 0, 4), 48.0, A.mult, col(cP2), A.add)
+    ts(V("LP", 0, 2), V("T16", 0, 2), 48.0, A.mult, col(cP1), A.add)
+    ts(V("LP", 2, 4), V("T16", 0, 2), 48.0, A.mult, col(cP2), A.add)
     ts(V("LFW"), V("R6"), 0.5, A.mult, col(cIh), A.add)
     ts(V("LX", 0, 21), V("IO", 0, OUT, 16), col(cXs), A.add, -48.0, A.add)
     ts(V("LX", 22, 43), V("IO", 0, OUT, 16), col(cXo), A.add, 288.0, A.add)
@@ -433,7 +440,8 @@ def rank_program(g, core, T, topo):
         act(V("XS", lo, lo + 16), ind(V("XS", 0, lo), off), F.Copy)
 
     def swap(src, lo, hx, dst, at):
-        tr(V(hx), V(src, lo, lo + 96))
+        for k in (0, 64, 32):
+            tr(V(hx, k, k + 32), V(src, lo + k, lo + k + 32))
         tr(V(dst, at, at + 64), V(hx, 16, 80))
 
     def mid(hb, lo, out):
@@ -452,16 +460,15 @@ def rank_program(g, core, T, topo):
     for lo in (18, 178):
         tt(V("VA", lo, lo + 142, 3), ind(V("FLR"), V("LFL", 0, 3)), JX, A.mult)
 
-    PARTS = ((0, CUT, "PK"), (CUT, C, "PA"))
-
     def inherit(r, wq, wsc):
-        tt(V("AA", 16, 64), ind(V("VA", 0, 160), V("PL", 24, 27)), V("VA", 178, 320, 3), A.max)
-        tt(V("AA", 80, 128), ind(V("VA", 160, 320), V("PL", 24, 27)), V("VA", 18, 160, 3), A.max)
-        for k, (src, dst) in enumerate((("AA", "AB"), ("AB", "AA"), ("AA", "HB"))):
-            off = V("PL", 4 * k + 4, 4 * k + 7)
-            tt(V(dst, 16, 64), ind(V(src, 0, 64), off), V(src, 80, 128), A.max)
-            if k < 2:
-                tt(V(dst, 80, 128), ind(V(src, 64, 128), off), V(src, 16, 64), A.max)
+        for k, (src, dst) in enumerate((("VA", "AA"), ("AA", "AB"), ("AB", "AD"), ("AD", "HB"))):
+            st, wide, at = (3, 160, 24) if k == 0 else (1, 64, 4 * k)
+            for c0, c1 in (LANES if r else ((0, 3),)):
+                for x in range(2 if k < 3 else 1):
+                    a, b = wide * x, wide * (1 - x) + 16
+                    tt(V(dst, 64 * x + 16 + 16 * c0, 64 * x + 16 + 16 * c1),
+                       ind(V(src, a, a + 16 + 16 * st * c1), V("PL", at + c0, at + c1)),
+                       V(src, b + 16 * st * c0 + st - 1, b + 16 * st * c1, st), A.max)
         for c in (1, 2):
             own = V("HB", 16 + 16 * c, 32 + 16 * c)
             tt(own, ind(V("HB", 0, 16 + 16 * c), V("PL", 16 + 2 * c, 17 + 2 * c)), own, A.max)
@@ -500,7 +507,7 @@ def rank_program(g, core, T, topo):
                             act(o, i, F.Copy)
         for q, b, m0, m1 in PLANES:
             if q == "q":
-                lo, hi, bank = PARTS[b]
+                lo, hi, bank = 16 * m0, 16 * m1, ("PK", "PA")[b]
                 quant(V("QE%d" % r, lo, hi), V("SE%d" % r, lo, hi), V("ET", 4 * lo, 4 * hi))
                 mm(V(bank, 0, hi - lo), wq, wsc, V("QE%d" % r, lo, hi), V("SE%d" % r, lo, hi))
                 continue
@@ -523,18 +530,26 @@ def rank_program(g, core, T, topo):
         keys = [lambda: tr(V("YK", 0, 96), V("SG", 0, C, 4)),
                 lambda: tr(V("YK", 96, 192), V("SG", 64, C + 64, 4)),
                 lambda: scan(V("ZL"), V("D01"), V("YK"), A.mult, A.add),
-                lambda: ts(V("TX%d" % r), ind(V("ZL"), V("LTX", 0, 3)), 0.5, A.mult, 7.5, A.add),
-                lambda: send(dst, "ra%d" % r, [(V("AR%d" % r), V("TX%d" % r))])]
-        locks = [lambda: act(V("T1H", 0, 96), ind(V("SG", 0, C), V("LL", 0, 6)), F.Identity, None, col(cWk)),
-                 lambda: ts(V("T1H", 96, 192), ind(V("SG", 0, C), V("LL", 6, 12)), col(cWk), A.mult),
+                lambda: ts(V("TX%d" % r, 0, 32), ind(V("ZL"), V("LTX", 0, 2)), 0.5, A.mult, 7.5, A.add),
+                lambda: send(dst, "ra%d" % r, [(V("AR%d" % r, 0, 24), V("TX%d" % r, 0, 24))], 0.3 if r else 1.0)]
+        locks = [lambda: act(V("T1H", 0, 128), ind(V("SG", 0, C), V("LL", 0, 8)), F.Identity, None, col(cWk)),
+                 lambda: ts(V("T1H", 128, 192), ind(V("SG", 0, C), V("LL", 8, 12)), col(cWk), A.mult),
                  lambda: tr(V("T2H"), V("T1H")),
                  lambda: scan(V("LMC", 15, 207), V("D2"), V("T2H"), A.mult, A.add)]
-        for call in (keys[:2] + locks[:2] + keys[2:] + locks[2:] if r == 0 else locks + keys):
+        for call in keys[:2] + locks[:2] + keys[2:] + locks[2:]:
             call()
-        tt(V("TA"), ind(V("LMC", 16, 208), V("LA", 0, 12)), V("SCN", 0, 192), A.not_equal)
-        scan(V("TP"), V("HR"), V("TA"), A.mult, A.add)
-        ts(V("TQ"), ind(V("TP"), V("LP")), 1, A.logical_shift_right, 0x10011, A.bitwise_and)
-        tt(V("TT"), V("TQ", 0, 64), V("TQ", 64, 128), A.add)
+        act(V("TX%d" % r, 32, 48), ind(V("ZL"), V("LTX", 2, 3)), F.Identity, 7.5, 0.5)
+        send(dst, "rb%d" % r, [(V("AR%d" % r, 24, 48), V("TX%d" % r, 24, 48))], 0.3 if r else 1.0)
+        for x in range(2):
+            tt(V("TA", 96 * x, 96 * x + 96), ind(V("LMC", 16, 208), V("LA", 6 * x, 6 * x + 6)), V("SCN", 0, 96),
+               A.not_equal)
+        for x in range(2):
+            scan(V("TP", 96 * x, 96 * x + 96), V("HR"), V("TA", 96 * x, 96 * x + 96), A.mult, A.add)
+        for x in range(2):
+            ts(V("TQ", 64 * x, 64 * x + 64), ind(V("TP", 96 * x, 96 * x + 96), V("LP")), 1, A.logical_shift_right,
+               0x10011, A.bitwise_and)
+        for x in range(2):
+            tt(V("TT", 32 * x, 32 * x + 32), V("TQ", 64 * x, 64 * x + 32), V("TQ", 64 * x + 32, 64 * x + 64), A.add)
         ar = "AR%d" % r
         for q in range(4):
             o, i = V("AC", q, C, 4), ind(V("TT", 16 * q, 16 * q + 16), V(ar, 6 * q, 6 * q + 6))
@@ -550,13 +565,13 @@ def rank_program(g, core, T, topo):
             scan(V("CHS", 100 * c, 100 * c + 99), V("KD", kd, kd + 99),
                  V("CHI", 100 * c, 100 * c + 99) if c else V("ACI", 3, C + 12, 4), A.add, A.min)
         for c in range(3):
-            ts(V("KL", c, c + 1), V("CHS", 100 * c + 96, 100 * c + 97), V("CHS", 100 * c + 98, 100 * c + 99),
+            ts(V("KL", 2 * c, 2 * c + 1), V("CHS", 100 * c + 96, 100 * c + 97), V("CHS", 100 * c + 98, 100 * c + 99),
                A.subtract, 256.0 if c else 1.0 / 256, A.mult)
         tr(V("LMH", 96, 288), V("LMC", 16, 208))
         act(V("LMH", 0, 96), ind(V("LMH", 96, 288), V("LA", 12, 18)), F.Copy)
         tt(V("MP", 0, 48), V("LMH", 0, 48), V("LMH", 48, 96), A.is_equal)
         tt(V("MP", 48, 96), V("MP", 0, 48), V("LMH", 48, 96), A.add)
-        cp(V("RF"), V(ar, 24, 48))
+        act(V("RF"), V(ar, 24, 48), F.Copy, behind=V("AC", 1, C, 4))
         act(V("XF"), ind(V("RF"), V("LFW")), F.Identity, -15.0, 2.0)
         tr(V("FW"), V("XF"))
         act(V("UP", 2, 144, 3), JJ, F.Identity, float(C + K * r) * S, 1.0)
@@ -569,12 +584,15 @@ def rank_program(g, core, T, topo):
         quant(V("QH%d" % r), V("SH%d" % r), V("HT"))
         send(dst, "rh%d" % r, [(u8(V("LQ", lo, lo + K)), u8(V("QH%d" % r, 0, K))),
                                (V("LS", lo, lo + K), V("SH%d" % r, 0, K))])
-        kl = V("KL", 0, 3)
-        tt(V("UP", 1, 144, 3), ind(V("FW"), kl), V("LMH", 0, 48), A.not_equal)
-        act(V("UP", 145, 288, 3), ind(JK, kl), F.Copy)
-        tt(V("UP", 146, 288, 3), ind(V("FW"), kl), V("MP", 48, 96), A.not_equal)
-        for at in (16, 176):
-            scan(V("VA", at, at + 144), V("UP", 0, 144), V("UP", 144, 288), A.add, A.min)
+        for c in range(3):
+            kl, a, b = V("KL", 2 * c, 2 * c + 1), 48 * c, 48 * c + 48
+            tt(V("UP", a + 1, b, 3), ind(V("FW"), kl), V("LMH", 16 * c, 16 * c + 16), A.not_equal)
+            act(V("UP", a + 145, b + 144, 3), ind(JK, kl), F.Copy)
+            tt(V("UP", a + 146, b + 144, 3), ind(V("FW"), kl), V("MP", 48 + 16 * c, 64 + 16 * c), A.not_equal)
+        for c0, c1 in SCANS:
+            for at in (16, 176):
+                scan(V("VA", at + 48 * c0, at + 48 * c1), V("UP", 48 * c0, 48 * c1),
+                     V("UP", 144 + 48 * c0, 144 + 48 * c1), A.add, A.min)
         for b in range(4):
             mm(V("PH%d" % b, 0, 128), V("QC", 128 * b, 128 * b + 128), V("SC", 128 * b, 128 * b + 128),
                V("LQ", lo - 32, lo + K), V("LS", lo - 32, lo + K))
@@ -584,13 +602,14 @@ def rank_program(g, core, T, topo):
     for G in range(8):
         dma("y", "dout", T.ofl[:, 48 * G:48 * G + 48], V("OF", 0, 48, 1, 16 * G, 16 * G + 16, 2))
     inherit(3, V("QV"), V("SV"))
-    for lo, hi, _bank in PARTS:
+    for lo, hi in ((0, CUT), (CUT, C)):
         dma("y", "dout", T.oc[:, 4 * lo:4 * hi], u8(V("QE3", lo, hi)))
-    cp(V("YO", CUT, C), V("PA", 0, C - CUT))
-    dma("y", "dout", T.y[:, CUT:C], V("YO", CUT, C))
+    for k in range(4):
+        dma("ys"[k % 2], "dout", T.osc[4 * k:4 * k + 4, :], V("SE3", 0, C, 1, 32 * k, 32 * k + 4))
+    for q, lo in (("y", CUT), ("s", CUT + 64)):
+        cp(V("YO", lo, lo + 64), V("PA", lo - CUT, lo - CUT + 64))
+        dma(q, "dout", T.y[:, lo:lo + 64], V("YO", lo, lo + 64))
     for lo in (0, 128):
         act(V("YO", lo, lo + 128), V("PK", lo, lo + 128), F.Copy)
         dma("s", "dout", T.y[:, lo:lo + 128], V("YO", lo, lo + 128))
-    for k in range(4):
-        dma("s", "dout", T.osc[4 * k:4 * k + 4, :], V("SE3", 0, C, 1, 32 * k, 32 * k + 4))
     issue()

from concourse.mybir import dt, AluOpType as A, ActivationFunctionType as F, AxisListType

C, K = 384, 96
DIST = [1, 2, 3]
TW = C + 3 * K
BIG = float(2 ** 21)
S = 1.0 / BIG
TINY = 2.0 ** -120
WHOLE = 1.5 * 2 ** 23
CUT = 256
OUT = C - 48
NEAR = 1000
PLANES = (("s", 0, 0, 6), ("s", 1, 0, 6), ("s", 2, 0, 6), ("s", 3, 0, 6),
          ("v", 0, 6, 16), ("v", 1, 6, 16), ("s", 2, 6, 16), ("s", 3, 6, 16),
          ("v", 0, 16, 24), ("q", 0, 0, 16), ("v", 1, 16, 20), ("s", 2, 16, 24), ("s", 3, 16, 24), ("s", 1, 20, 24),
          ("q", 1, 16, 24))
FIRST = 0.8
FLAGS = 1.4
SOON = 600.0
PIECES = ((0, 6), (6, 16), (16, 24))
OUTS = ("ssss", "vvss", "vvvv")
LANES = ((0, 2), (2, 3))
SCANS = ((0, 1), (1, 2), (2, 3))
TOP = (("in", 0), ("in", 1), ("in", 2), ("in", 3), ("turn", 0), ("step", 1), ("pick", 0), ("step", 2), ("out", 0),
       ("step", 3), ("turn", 1), ("turn", 2), ("turn", 3), ("pick", 1), ("pick", 2), ("out", 1), ("out", 2))
FP8, U8, U16, I32, F32, BF = "float8_e4m3fn_x4", "uint8", "uint16", "int32", "float32", "bfloat16"
CYCLE, WAKE, FAR = 1.0, 175.0, 1600.0
TOL = 40.0
CROSS = 200.0


def _sb(n, d):
    return ("sbuf", [128, n], d)


SCRATCH = {
    "XR": _sb(4 * C, BF), "TAB": _sb(4 * TW, BF), "ET": _sb(4 * C, BF), "HT": _sb(512, BF), "UT": _sb(512, BF),
    "VT": _sb(512, BF), "ONE": _sb(520, BF), "EC": _sb(520, BF),
    "QU0": _sb(128, FP8), "SU0": _sb(128, U8), "QU": _sb(128, FP8), "SU": _sb(128, U8), "QV": _sb(128, FP8),
    "SV": _sb(128, U8), "QW": _sb(512, FP8), "SW": _sb(512, U8), "QC": _sb(512, FP8), "SC": _sb(512, U8),
    "LQ": _sb(128 + 3 * K, FP8), "LS": _sb(128 + 3 * K, U8),
    "PI": _sb(1, I32), "CI": _sb(12, I32), "CF": _sb(40, F32),
    "T16": _sb(96, F32), "M1": _sb(192, F32), "MM": _sb(96, F32), "IO": _sb(C, F32),
    "SRC": _sb(2 * OUT, F32), "R6": _sb(6, F32), "RTX": _sb(48, F32), "RX": _sb(192, F32), "SCN": _sb(288, F32),
    "HR": _sb(96, F32), "KD": _sb(200, F32), "JJ": _sb(240, F32), "D01": _sb(192, BF),
    "LU": _sb(8, U16), "LA": _sb(18, U16), "LP": _sb(4, U16), "LTX": _sb(4, U16), "LX": _sb(44, U16),
    "LFW": _sb(6, U16), "LL": _sb(12, U16), "LFL": _sb(4, U16), "LEX": _sb(12, U16), "PW": _sb(14, U16),
    "PL": _sb(28, U16), "LM": _sb(8, U16), "LT": _sb(18, U16), "KL": _sb(6, U16), "PTR": _sb(24, U16),
    "PR": _sb(4, I32), "FLR": _sb(C, I32),
    "RB": _sb(C, F32), "RC": _sb(192, F32), "EYE": _sb(48, F32), "SCO": _sb(624, F32), "XS": _sb(OUT + 176, F32), "XO": _sb(OUT + 96, F32),
    "WX": _sb(96, F32), "WC": _sb(96, F32),
    "VA": _sb(320, F32), "AA": _sb(128, F32), "AB": _sb(128, F32), "AD": _sb(128, F32), "HB": _sb(192, F32),
    "HX": _sb(96, F32), "MD": _sb(C, F32), "CP": _sb(C, I32), "YY": _sb(C, I32), "OJ": _sb(192, I32),
    "YK": _sb(192, BF), "ZL": _sb(192, BF),
    "SG": _sb(C + 64, BF), "T1H": _sb(192, BF), "T2H": _sb(192, BF), "LMH": _sb(288, BF), "LMC": _sb(208, BF), "D2": _sb(192, BF),
    "TA": _sb(192, F32), "TP": _sb(192, I32), "TQ": _sb(128, I32), "TT": _sb(64, F32), "MP": _sb(96, F32),
    "AC": _sb(C, F32), "ACI": _sb(C + 12, I32), "D4": _sb(C, F32), "CHI": _sb(300, I32), "CHS": _sb(300, F32),
    "RF": _sb(24, F32), "XF": _sb(96, BF), "FW": _sb(96, BF), "UP": _sb(288, F32),
    "OF": _sb(48, F32), "YO": _sb(C, F32),
}
for _r in range(4):
    SCRATCH["QE%d" % _r] = _sb(C, FP8)
    SCRATCH["SE%d" % _r] = _sb(C, U8)
for _r in range(3):
    SCRATCH["TX%d" % _r] = _sb(48, U16)
    SCRATCH["AR%d" % _r] = _sb(48, U16)
    SCRATCH["QH%d" % _r] = _sb(128, FP8)
    SCRATCH["SH%d" % _r] = _sb(128, U8)
for _n in ("PK", "PA", "PH0", "PH1", "PH2", "PH3"):
    SCRATCH[_n] = ("psum", [128, 512], F32)

SEMAPHORES = ["cv", "cs", "ct", "cg", "dpar", "dx", "du", "dfl", "dw", "dv", "dq", "dout", "sent",
              "ra0", "ra1", "ra2", "rb0", "rb1", "rb2", "rh0", "rh1", "rh2"]


def rank_program(g, core, T, topo):
    rank = T.rank_of(core)
    if rank is None:
        return
    N = len(T.cores)
    Q = {"v": g.vector, "s": g.scalar, "t": g.tensor, "g": g, "y": g.sync}
    calls = []
    log = {}

    def V(name, c0=0, c1=None, st=1, p0=0, p1=128, ps=1):
        if c1 is None:
            c1 = SCRATCH[name][1][1]
        t = T[name]
        ap = t[p0:p1:ps, c0:c1] if ps > 1 else (t[p0:p1, c0:c1] if st == 1 else t[p0:p1, c0:c1:st])
        n = len(range(c0, c1, st))
        return (ap, [(name, p0, p1, frozenset(range(c0, c1, st)))], n, SCRATCH[name][2] in (BF, U16), False)

    def col(k, p0=0, p1=128):
        return V("CF", k, k + 1, 1, p0, p1)

    def ind(win, off, words=False):
        ap = win[0].bitcast(dt.uint32) if words else win[0]
        return (ap.indirect(off[0]), win[1] + off[1], 16 * off[2], False, True)

    def record(q, fn, busy, late, outs, ins, sem, inc):
        before = set()
        regs = [(r, True) for o in outs if isinstance(o, tuple) for r in o[1]]
        regs += [(r, False) for o in ins if isinstance(o, tuple) for r in o[1]]
        for (name, p0, p1, cols), writing in regs:
            bank = SCRATCH[name][0] == "psum"
            for (w, k, a0, a1, cs) in log.get(name, []):
                if bank:
                    hit = w or writing or calls[k][0] != q
                else:
                    hit = (w or writing) and a0 < p1 and p0 < a1 and not cols.isdisjoint(cs)
                if hit:
                    before.add(k)
        for k in list(before):
            if calls[k][6] != 1:
                before.update(m for m in range(len(calls)) if calls[m][5] == calls[k][5])
        calls.append((q, fn, busy, late, before, sem, inc))
        for (name, p0, p1, cols), writing in regs:
            log.setdefault(name, []).append((writing, len(calls) - 1, p0, p1, cols))
        return len(calls) - 1

    def op(q, fn, outs, ins, per=1.0, fixed=None):
        n = ins[0][2] if ins else outs[0][2]
        if ins and ins[0][4]:
            busy = 60.0 + 1.56 * n * CYCLE
        elif fixed is None:
            busy = max(64.0, per * n) * CYCLE
        else:
            busy = fixed + per * n * CYCLE
        record(q, fn, busy, busy, outs, ins, "c" + q, 1)

    def issue():
        n = len(calls)
        at, taken = {}, {q: [] for q in Q}

        def place(k):
            q, _fn, busy, _late, before = calls[k][:5]
            for m in sorted(before):
                if m not in at:
                    place(m)
            t = max([0.0] + [at[m] + calls[m][3] + (WAKE if calls[m][0] == q else CROSS) for m in before])
            if q is not None:
                for lo, hi in taken[q]:
                    if t + busy <= lo + TOL and t < lo and q != "y":
                        break
                    t = max(t, hi)
                taken[q].append((t, t + busy))
                taken[q].sort()
            at[k] = t

        chain = [0.0] * n
        for k in range(n - 1, -1, -1):
            chain[k] += calls[k][3] + WAKE
            for m in calls[k][4]:
                chain[m] = max(chain[m], chain[k])
        early = sorted(range(marks[0], marks[1]), key=lambda k: chain[k])
        for k in list(range(marks[0])) + list(range(marks[1], n)):
            while early and k >= marks[1] and (chain[early[-1]] + SOON > chain[k] or k == n - 1):
                m = early.pop()
                if m not in at:
                    place(m)
            if k not in at:
                place(k)
        total, count, seen = {s: 0 for s in SEMAPHORES}, {}, {q: {} for q in Q}
        whole = {s: sum(c[6] for c in calls if c[5] == s) for s in SEMAPHORES}
        for k in sorted(range(n), key=lambda k: at[k]):
            q, fn, busy, late, before, sem, inc = calls[k]
            total[sem] += inc
            count[k] = total[sem] if inc == 1 else whole[sem]
            if q is None:
                continue
            need = {}
            for m in before:
                need[calls[m][5]] = max(need.get(calls[m][5], 0), count[m])
            for s in need:
                if seen[q].get(s, 0) < need[s]:
                    Q[q].wait_ge(T.sem[s], need[s])
                    seen[q][s] = need[s]
            if sem == "sent":
                fn()
            else:
                fn().then_inc(T.sem[sem], inc)
        for s in sorted(SEMAPHORES, key=lambda s: max(at[k] + calls[k][3] for k in range(n) if calls[k][5] == s)):
            g.wait_ge(T.sem[s], whole[s])

    def a_(x):
        return x[0] if isinstance(x, tuple) else x

    def half(*xs):
        return 0.5 if all(x[3] for x in xs) else 1.0

    def cp(o, i):
        op("v", lambda: g.vector.tensor_copy(o[0], i[0]), [o], [i], half(o, i))

    def tt(o, a, b, f):
        op("v", lambda: g.vector.tensor_tensor(o[0], a[0], b[0], f), [o], [a, b], 2.0)

    def ts(o, a, s1, f0, s2=None, f1=None):
        if f1 is None:
            op("v", lambda: g.vector.tensor_scalar(o[0], a[0], a_(s1), None, f0), [o], [a, s1])
        else:
            op("v", lambda: g.vector.tensor_scalar(o[0], a[0], a_(s1), a_(s2), f0, f1), [o], [a, s1, s2])

    def ms(o, c):
        op("v", lambda: g.vector.memset(o[0], c), [o], [])

    def scan(o, d0, d1, f0, f1):
        op("v", lambda: g.vector.tensor_tensor_scan(o[0], d0[0], d1[0], 0.0, f0, f1), [o], [d0, d1], half(o, d0, d1))

    def tr(o, i):
        op("v", lambda: g.vector.transpose(o[0], i[0]), [o], [i], half(o, i))

    def quant(qo, so, i):
        op("v", lambda: g.vector.quantize_mx(qo[0], so[0], i[0]), [qo, so], [i], 0.27, 12.0)

    def act(o, i, f, bias=None, scale=None, behind=None):
        kw = {}
        if bias is not None:
            kw["bias"] = a_(bias)
        if scale is not None:
            kw["scale"] = a_(scale)
        op("s", lambda: g.scalar.activation(o[0], i[0], f, **kw), [o], [i, bias, scale, behind])

    def mm(o, wq, wsc, xq, xsc):
        op("t", lambda: g.tensor.matmul_mx(o[0], wq[0], wsc[0], xq[0], xsc[0], True, True), [o], [xq, xsc, wq, wsc],
           1.0, 16.0)

    def iota(o, pat, base, cm=0, small=True):
        if small:
            op("g", lambda: g.iota(o[0], pat, base, cm, allow_small_or_imprecise_dtypes=True), [o], [], 2.0, 130.0)
        else:
            op("g", lambda: g.iota(o[0], pat, base, cm), [o], [], 2.0, 130.0)

    def dma(q, sem, o, i, long=1.0):
        record(q, lambda: Q[q].dma_start(a_(o), a_(i)), 60.0, long * FAR, [o], [i], sem, 16)

    def u8(x):
        return (x[0].bitcast(dt.uint8),) + x[1:]

    NE = 8

    def send(dst, sem, pairs, long=1.0):
        rid, pid, _se = topo.addr(dst)
        m = 0
        for e in topo.engines(core, dst)[:NE]:
            m |= 1 << e

        def one(o, i):
            return record("g", lambda: g.remote_dma(o[0], i[0], T.sem[sem], T.sem["sent"], pid, rid, m), 200.0, 200.0,
                          [], [i], "sent", NE)
        sent = [one(o, i) for o, i in pairs]
        calls.append((None, None, 0.0, long * FAR, set(sent), sem, NE * len(pairs)))
        for o, _i in pairs:
            for (name, p0, p1, cols) in o[1]:
                log.setdefault(name, []).append((True, len(calls) - 1, p0, p1, cols))

    for G in range(8):
        dma("ys"[G % 2], "dpar", V("PR", 0, 3, 1, 16 * G, 16 * G + 16), T.par[:, 3 * G:3 * G + 3], FIRST)
    ms(V("FLR"), 0)
    for G in range(8):
        dma("y", "dfl", V("FLR", 0, C, 1, 16 * G, 16 * G + 16, 2), T.fl[:, :], FLAGS)
    dma("y", "dx", V("XR"), T.x[:, :], 3.0)
    dma("y", "du", V("UT"), T.u[:, :], 3.0)
    dma("y", "dw", u8(V("QW")), T.wc[:, :], 3.5)
    dma("y", "dw", V("SW"), T.ws[:, :], 3.5)
    dma("y", "dv", V("VT"), T.v[:, :], 3.5)

    iota(V("PI"), [[0, 1]], 0, 1, False)
    iota(V("T16"), [[0, 6], [1, 16]], 0)
    iota(V("R6"), [[16, 3], [0, 2]], 0)
    iota(V("IO"), [[1, C]], 0)
    marks = [len(calls)]
    iota(V("SRC", 288, OUT), [[1, 48]], -NEAR)
    iota(V("SRC", OUT, OUT + 48), [[-16, 3], [1, 16]], 80)
    iota(V("SRC", OUT + 288, 2 * OUT), [[-16, 3], [1, 16]], 32 - NEAR)
    iota(V("RTX", 0, 24), [[4, 4], [32, 6]], 3)
    iota(V("RTX", 24, 48), [[32, 3], [2, 8]], 17)
    iota(V("RX", 0, 24, 2), [[32, 12]], 0)
    iota(V("RX", 1, 24, 2), [[32, 12]], -16)
    iota(V("RX", 1, 24, 6), [[96, 4]], 80)
    iota(V("RX", 24, 48), [[0, 24]], 18)
    for s, d in ((0, 82), (1, -78), (4, -46)):
        iota(V("RX", 24 + s, 48, 6), [[0, 4]], d)
    for x in range(2):
        iota(V("SCN", 192 + x, 288, 2), [[2, 4], [0, 4], [32, 3]], 96 * x)
    iota(V("SCN", 0, 96), [[0, 4], [2, 4], [0, 6]], -3)
    iota(V("D01", 0, 192, 4), [[0, 48]], 0)
    iota(V("D01", 1, 192, 2), [[0, 96]], 2)
    iota(V("D01", 2, 192, 4), [[0, 6], [-2, 2], [0, 4]], 2)
    iota(V("HR", 1, 96, 2), [[0, 48]], 1)
    iota(V("HR", 0, 96, 6), [[0, 16]], 0)
    iota(V("HR", 2, 96, 6), [[0, 16]], 4096)
    iota(V("HR", 4, 96, 6), [[0, 16]], 16)
    iota(V("UP", 0, 144, 3), [[0, 48]], 2)
    for tail in (V("ACI", C, C + 12), V("CHI", 196, 200), V("CHI", 296, 300)):
        iota(tail, [[0, tail[2]]], 2 ** 23, 0, False)
    iota(V("D4"), [[0, C]], 1)
    iota(V("D4", 0, C, 4), [[0, 96]], 0)
    iota(V("LMC", 207, 208), [[0, 1]], 0)
    iota(V("D2"), [[0, 96], [1, 2]], 0)
    iota(V("HT", C, 512), [[0, 128]], 0)
    iota(V("ONE"), [[0, 520]], 1)
    op("g", lambda: g.affine_select(T.EC[:, :], T.ONE[:, :], [[-1, 520]], A.is_equal, 0.0, 3, 4), [V("EC")], [V("ONE")],
       2.0, 170.0)

    cI, cI3, cI12, cIh, cB0, cG, cH16, cH = range(8)
    for k, (sh, m) in enumerate([(0, 15), (0, 3), (0, 12), (1, 7), (0, 1), (4, 7), (0, 16), (4, 1)]):
        ts(V("CI", k, k + 1), V("PI"), sh, A.logical_shift_right, m, A.bitwise_and)
    cp(V("CF", 0, 8), V("CI", 0, 8))
    (cI1, cFix, cG3, cFl, cD3, cWk, cKl, cK80, cD, cJ, cJx, cUk, cCA, cP1, cP2, cLk, cRoot, cNear, cXs, cXo,
     cEx) = range(10, 31)
    JJ, JX, JB, JK = V("JJ", 0, 48), V("JJ", 48, 96), V("JJ", 96, 144), V("JJ", 144, 240)
    ts(col(cI1), col(cI), 1.0, A.add)
    ts(col(cD), col(cG), -48.0, A.mult, float(OUT), A.add)
    ts(col(cRoot), col(cI), OUT - 1.0, A.add)
    ts(col(cFix), col(cI), 15.0, A.is_lt, BIG, A.mult)
    for k, src, sc, bi in [
            (cUk, cIh, 16.0, col(cB0)), (cG3, cG, 3.0, 0.0), (cLk, cG, 48.0, col(cI)), (cD3, cG, -144.0, 18.0),
            (cJx, cG, 49200.0 * S, 1024.0 * S), (cFl, cI, 24.0, col(cG3)), (cWk, cB0, -1.0, 2.0),
            (cKl, cH16, -5.0 / 256, 95.0 / 256), (cK80, cH16, 6.0 / 256, -17.0 / 256),
            (cJ, cG, 49152.0 * S, 1024.0 * S), (cCA, cH16, -1.0, col(cFix)), (cP1, cI12, 1.5, 5.0),
            (cP2, cI3, 6.0, 29.0), (cNear, cFix, 1.0, -float(NEAR)), (cXs, cH16, 24.0, col(cI)),
            (cXo, cH16, -18.0, col(cI)), (cEx, cI3, -4.0, col(cFix))]:
        act(col(k), col(src), F.Identity, bi, sc)

    def const(o, c):
        act(o, V("T16" if o[2] <= 96 else "IO", 0, o[2]), F.Identity, c, 0.0)

    act(V("RB", 0, OUT), V("IO", 0, OUT), F.Copy)
    act(V("SRC", 0, 288), V("IO", 0, 288), F.Copy)
    act(V("SRC", OUT + 48, OUT + 96), V("IO", 0, 48), F.Copy)
    for a in (1, 2):
        act(V("SRC", OUT + 96 * a, OUT + 96 * a + 96), V("SRC", OUT, OUT + 96), F.Identity, 96.0 * a, 1.0)
    for name, lo, hi in (("AA", 0, 16), ("AA", 64, 80), ("AB", 0, 16), ("AB", 64, 80), ("AD", 0, 16),
                         ("HB", 0, 16), ("HB", 96, 112),
                         ("HB", 176, 192), ("XS", C, C + 48), ("XS", OUT + 160, OUT + 176), ("XO", C + 32, C + 48),
                         ("VA", 0, 320)):
        const(V(name, lo, hi), 0.0)
    iota(V("CP", 0, 96), [[0, 96]], 0, 0, False)
    iota(V("MD", 96, C), [[0, C - 96]], 0)
    iota(V("YY"), [[0, C]], 0, 0, False)
    ms(V("LT"), 0)
    ts(V("M1", 0, 96), V("T16"), col(cI), A.is_equal, -3.0 * BIG, A.mult)
    ts(V("M1", 96, 192), V("T16"), col(cI1), A.is_equal, BIG, A.mult)
    tt(V("MM", 0, 48), V("M1", 0, 48), V("M1", 96, 144), A.add)
    tt(V("MM", 48, 96), V("M1", 48, 96), V("M1", 144, 192), A.add)
    used = [0]

    def listed(row):
        lo = used[0]
        used[0] += row[2]
        scan(V("SCO", lo, lo + row[2]), V("MM", 0, row[2]), row, A.add, A.max)
        return lambda a=0, b=row[2] // 16, p0=0, p1=128: V("SCO", lo + 15 + 16 * a, lo + 16 * b, 16, p0, p1)

    ts(V("LU"), V("T16", 0, 8), 0.0, A.mult, col(cUk), A.add)
    ts(V("LL", 0, 6), V("R6"), col(cLk), A.add)
    ts(V("LFL", 0, 3), V("T16", 0, 3), col(cFl), A.add)
    ts(V("LA", 12, 18), V("T16", 0, 6), 32.0, A.mult, col(cI), A.add)
    ts(V("LP", 0, 2), V("T16", 0, 2), 48.0, A.mult, col(cP1), A.add)
    ts(V("LP", 2, 4), V("T16", 0, 2), 48.0, A.mult, col(cP2), A.add)
    ts(V("LFW"), V("R6"), 0.5, A.mult, col(cIh), A.add)
    ts(V("LX", 0, 21), V("IO", 0, OUT, 16), col(cXs), A.add, -48.0, A.add)
    ts(V("LX", 22, 43), V("IO", 0, OUT, 16), col(cXo), A.add, 288.0, A.add)
    ts(V("LTX", 0, 3), listed(V("RTX"))(), col(cFix), A.subtract)
    ts(V("LA", 0, 6), listed(V("SCN", 192, 288))(), col(cCA), A.subtract)
    ts(V("LA", 6, 12), V("LA", 0, 6), 8.0, A.add)
    act(V("RX", 48, 72), V("RX", 24, 48), F.Identity, 0.0, col(cH))
    tt(V("RX", 72, 96), V("RX", 48, 72), V("RX", 0, 24), A.add)
    for a in range(4):
        act(V("RX", 96 + a, 192, 4), V("RX", 72, 96), F.Copy)
    ex = listed(V("RX", 96, 192))
    for k, (m0, m1) in enumerate(PIECES):
        n0, n1 = m0 // 4, -(-m1 // 4)
        ts(V("LEX", 4 * k, 4 * k + n1 - n0), ex(n0, n1), col(cEx), A.subtract, -(-m1 // 6) * 96 - 1.0, A.min)
    const(V("KD", 100, 196), -1.0 / 256)
    const(V("KD", 116, 196, 16), -17.0 / 256)
    const(V("KD", 100, 101), 8192.0)
    const(V("KD", 148, 149), 63.0 / 256)
    const(V("KD", 180, 181), col(cK80))
    const(V("KD", 196, 197), col(cKl))
    const(V("KD", 197, 198), -WHOLE)
    const(V("KD", 198, 199), WHOLE)
    act(V("KD", 0, 99), V("KD", 100, 199), F.Identity, 0.0, 65536.0)
    act(V("KD", 96, 97), V("KD", 196, 197), F.Identity, -68.0, 65536.0)
    act(JJ, V("IO", 0, 48), F.Identity, col(cJ), 1024.0 * S)
    act(JX, V("IO", 0, 48), F.Identity, col(cJx), 1025.0 * S)
    act(JK, V("IO", 0, 96), F.Identity, 0.0, S)

    quant(V("QU0"), V("SU0"), V("UT"))
    for lo in (0, 64):
        off, o = V("LU", lo // 16, lo // 16 + 4), V("QU", lo, lo + 64)
        cp((o[0].bitcast(dt.uint32),) + o[1:], ind(V("QU0"), off, True))
        act(V("SU", lo, lo + 64), ind(V("SU0"), off), F.Copy)
    quant(V("QV"), V("SV"), V("VT"))
    for b in range(4):
        quant(V("QC", 128 * b, 128 * b + 128), V("SC", 128 * b, 128 * b + 128), V("EC", 3 - b, 515 - b))
        act(V("TAB", TW * b, TW * b + C), V("XR", b, 4 * C, 4), F.Copy)

    ts(V("PW", 0, 1), V("PR", 0, 1), col(cD), A.add, col(cRoot), A.min)
    ts(V("PW", 1, 3), V("PR", 1, 3), col(cD), A.add)
    ts(V("PL", 24, 27), V("PR", 0, 3), 3.0, A.mult, col(cD3), A.add)
    cp(V("LL", 6, 12, 2), V("PR", 0, 3))
    cp(V("LL", 7, 12, 2), V("PR", 0, 3))

    def up(src, dst, lo):
        cp(V(dst, OUT, C), ind(V(src), V("PW", lo, lo + 3)))

    def near(o, row):
        ts(o, row(), col(cFix), A.subtract, 16.0 - OUT, A.add)

    def aside(src, lo):
        act(V("RC", lo, lo + 48), V(src, OUT, C), F.Copy)
        return V("RC", lo, lo + 48)

    def own(src, lo, o, st, at):
        tt(V("RC", at, at + 48), ind(V(src), V("PW", lo, lo + 3)), V("EYE"), A.mult)
        for c in range(3):
            x, y = V("PW", o + st * c, o + st * c + 1), V("RC", at + 16 * c, at + 16 * c + 16)
            op("v", lambda x=x, y=y: g.vector.tensor_reduce(x[0], y[0], AxisListType.X, A.max), [x], [y])

    ts(V("EYE"), V("T16", 0, 48), col(cI), A.is_equal)
    up("IO", "RB", 0)
    up("RB", "IO", 0)
    near(V("PL", 4, 7), listed(aside("IO", 0)))
    up("IO", "RB", 0)
    own("RB", 0, 4, 1, 96)
    up("RB", "IO", 0)
    ts(V("PL", 8, 11), V("PW", 4, 7), 16.0 - OUT, A.add)
    up("IO", "RB", 4)
    near(V("PL", 12, 15), listed(aside("RB", 48)))
    up("RB", "IO", 4)
    own("IO", 4, 8, 2, 144)
    ts(V("PL", 16, 22, 2), V("PW", 8, 14, 2), 16.0 - OUT, A.add)
    act(V("XS", 0, OUT), ind(V("SRC"), V("LX", 0, 21)), F.Copy)
    act(V("XO", 0, OUT), ind(V("SRC"), V("LX", 22, 43)), F.Copy)
    for c in range(3):
        lo, off = OUT + 16 * c, V("PW", 8 + 2 * c, 9 + 2 * c)
        cp(V("XO", lo, lo + 16), ind(V("XO", 0, lo), off))
        if c < 2:
            act(V("XO", C + 16 - 16 * c, C + 32 - 16 * c), ind(V("XO", 0, lo), off), F.Copy)
        act(V("XS", lo, lo + 16), ind(V("XS", 0, lo), off), F.Copy)

    def swap(src, lo, hx, dst, at):
        for k in (0, 64, 32):
            tr(V(hx, k, k + 32), V(src, lo + k, lo + k + 32))
        tr(V(dst, at, at + 64), V(hx, 16, 80))

    def mid(hb, lo, out):
        tt(V(out, 0, 48), ind(V(hb, lo + 96, lo + 176), V("LM", 0, 3)), V(hb, lo, lo + 48), A.max)
        tt(V(out, 48, 96), ind(V(hb, lo, lo + 96), V("LM", 4, 7)), V(hb, lo + 96, lo + 144), A.max)

    swap("XO", OUT, "WX", "XS", OUT + 96)
    ts(V("LM", 0, 3), listed(V("XS", OUT, C))(), col(cNear), A.subtract, 64.0, A.min)
    ts(V("LM", 4, 7), listed(V("XS", OUT + 96, OUT + 144))(), col(cNear), A.subtract, 80.0, A.min)
    mid("XS", OUT, "WC")
    row = listed(V("WC"))
    for a in range(1, 4):
        ts(V("LT", 6 * a - 6, 6 * a, 1, 0, 32), row(0, 6, 32 * a, 32 * a + 32), col(cFix, 32 * a, 32 * a + 32),
           A.subtract, 96.0 * a - 288.0, A.add)

    for lo in (18, 178):
        tt(V("VA", lo, lo + 142, 3), ind(V("FLR"), V("LFL", 0, 3)), JX, A.mult)

    def inherit(r, wq, wsc):
        for k, (src, dst) in enumerate((("VA", "AA"), ("AA", "AB"), ("AB", "AD"), ("AD", "HB"))):
            st, wide, at = (3, 160, 24) if k == 0 else (1, 64, 4 * k)
            for c0, c1 in (LANES if r else ((0, 3),)):
                for x in range(2 if k < 3 else 1):
                    a, b = wide * x, wide * (1 - x) + 16
                    tt(V(dst, 64 * x + 16 + 16 * c0, 64 * x + 16 + 16 * c1),
                       ind(V(src, a, a + 16 + 16 * st * c1), V("PL", at + c0, at + c1)),
                       V(src, b + 16 * st * c0 + st - 1, b + 16 * st * c1, st), A.max)
        for c in (1, 2):
            own = V("HB", 16 + 16 * c, 32 + 16 * c)
            tt(own, ind(V("HB", 0, 16 + 16 * c), V("PL", 16 + 2 * c, 17 + 2 * c)), own, A.max)
            act(V("HB", 96 - 16 * c, 112 - 16 * c), V("HB", 16 * c, 16 * c + 16), F.Copy)
        swap("HB", 16, "HX", "HB", 112)
        mid("HB", 16, "MD")

        def part(a):
            return V("CP", 96 * a, 96 * a + 96, 1, 0, 32)

        marks.append(len(calls))
        for what, k in TOP:
            if what == "in" and k == 0:
                ts(part(0), V("MD", 0, 96, 1, 0, 32), BIG, A.mult)
            elif what == "in":
                act(V("MD", 96 * k, 96 * k + 96, 1, 0, 32), V("MD", 0, 96, 1, 32 * k, 32 * k + 32), F.Copy, None, BIG)
            elif what == "step":
                tt(V("CP", 96 * k, 96 * k + 96), ind(V("CP", 0, 96 * k), V("LT", 6 * k - 6, 6 * k)),
                   V("MD", 96 * k, 96 * k + 96), A.max)
            elif what == "turn":
                tr(V("YY", 96 * k, 96 * k + 96, 1, 0, 32), part(k))
            else:
                m0, m1 = PIECES[k]
                n0, n1, lo = m0 // 4, -(-m1 // 4), 64 * k
                hi = lo + 16 * (n1 - n0)
                if what == "pick":
                    ts(V("OJ", lo, hi), ind(V("YY", 0, -(-m1 // 6) * 96), V("LEX", 4 * k, 4 * k + n1 - n0)), 1023,
                       A.bitwise_and)
                else:
                    for a in range(4):
                        o = V("PTR", m0, m1, 1, 32 * a, 32 * a + 32)
                        i = V("OJ", lo + 4 * m0 - 16 * n0 + a, lo + 4 * m1 - 16 * n0, 4, 0, 32)
                        if OUTS[k][a] == "v":
                            cp(o, i)
                        else:
                            act(o, i, F.Copy)
        for q, b, m0, m1 in PLANES:
            if q == "q":
                lo, hi, bank = 16 * m0, 16 * m1, ("PK", "PA")[b]
                quant(V("QE%d" % r, lo, hi), V("SE%d" % r, lo, hi), V("ET", 4 * lo, 4 * hi))
                mm(V(bank, 0, hi - lo), wq, wsc, V("QE%d" % r, lo, hi), V("SE%d" % r, lo, hi))
                continue
            o = V("ET", 64 * m0 + b, 64 * m1, 4)
            i = ind(V("TAB", TW * b, TW * b + C + K * r), V("PTR", m0, m1))
            if q == "v":
                cp(o, i)
            else:
                act(o, i, F.Copy)

    for r, h in enumerate(DIST):
        dst = T.cores[(rank - h) % N]
        inherit(r, V("QU"), V("SU"))
        if r == 0:
            dma("y", "dq", u8(V("LQ", 96, 128)), u8(V("QE0", 0, 32)))
            dma("y", "dq", V("LS", 96, 128), V("SE0", 0, 32))
        act(V("SG", 0, CUT), V("PK", 0, CUT), F.Sign, -TINY)
        act(V("SG", CUT, C), V("PA", 0, C - CUT), F.Sign, -TINY)
        cp(V("SG", C, C + 64, 4), V("SG", 0, 64, 4))
        keys = [lambda: tr(V("YK", 0, 96), V("SG", 0, C, 4)),
                lambda: tr(V("YK", 96, 192), V("SG", 64, C + 64, 4)),
                lambda: scan(V("ZL"), V("D01"), V("YK"), A.mult, A.add),
                lambda: ts(V("TX%d" % r, 0, 32), ind(V("ZL"), V("LTX", 0, 2)), 0.5, A.mult, 7.5, A.add),
                lambda: send(dst, "ra%d" % r, [(V("AR%d" % r, 0, 24), V("TX%d" % r, 0, 24))], 0.3 if r else 1.0)]
        locks = [lambda: act(V("T1H", 0, 128), ind(V("SG", 0, C), V("LL", 0, 8)), F.Identity, None, col(cWk)),
                 lambda: ts(V("T1H", 128, 192), ind(V("SG", 0, C), V("LL", 8, 12)), col(cWk), A.mult),
                 lambda: tr(V("T2H"), V("T1H")),
                 lambda: scan(V("LMC", 15, 207), V("D2"), V("T2H"), A.mult, A.add)]
        for call in keys[:2] + locks[:2] + keys[2:] + locks[2:]:
            call()
        act(V("TX%d" % r, 32, 48), ind(V("ZL"), V("LTX", 2, 3)), F.Identity, 7.5, 0.5)
        send(dst, "rb%d" % r, [(V("AR%d" % r, 24, 48), V("TX%d" % r, 24, 48))], 0.3 if r else 1.0)
        for x in range(2):
            tt(V("TA", 96 * x, 96 * x + 96), ind(V("LMC", 16, 208), V("LA", 6 * x, 6 * x + 6)), V("SCN", 0, 96),
               A.not_equal)
        for x in range(2):
            scan(V("TP", 96 * x, 96 * x + 96), V("HR"), V("TA", 96 * x, 96 * x + 96), A.mult, A.add)
        for x in range(2):
            ts(V("TQ", 64 * x, 64 * x + 64), ind(V("TP", 96 * x, 96 * x + 96), V("LP")), 1, A.logical_shift_right,
               0x10011, A.bitwise_and)
        for x in range(2):
            tt(V("TT", 32 * x, 32 * x + 32), V("TQ", 64 * x, 64 * x + 32), V("TQ", 64 * x + 32, 64 * x + 64), A.add)
        ar = "AR%d" % r
        for q in range(4):
            o, i = V("AC", q, C, 4), ind(V("TT", 16 * q, 16 * q + 16), V(ar, 6 * q, 6 * q + 6))
            if q % 2:
                act(o, i, F.Copy)
            else:
                cp(o, i)
        scan(V("ACI", 0, C), V("D4"), V("AC"), A.mult, A.add)
        for c in (1, 2):
            ts(V("CHI", 100 * c, 100 * c + 96), V("ACI", 3, C, 4), 15 << (8 - 4 * c), A.bitwise_and)
        for c in range(3):
            kd = 100 * min(c, 1)
            scan(V("CHS", 100 * c, 100 * c + 99), V("KD", kd, kd + 99),
                 V("CHI", 100 * c, 100 * c + 99) if c else V("ACI", 3, C + 12, 4), A.add, A.min)
        for c in range(3):
            ts(V("KL", 2 * c, 2 * c + 1), V("CHS", 100 * c + 96, 100 * c + 97), V("CHS", 100 * c + 98, 100 * c + 99),
               A.subtract, 256.0 if c else 1.0 / 256, A.mult)
        tr(V("LMH", 96, 288), V("LMC", 16, 208))
        act(V("LMH", 0, 96), ind(V("LMH", 96, 288), V("LA", 12, 18)), F.Copy)
        tt(V("MP", 0, 48), V("LMH", 0, 48), V("LMH", 48, 96), A.is_equal)
        tt(V("MP", 48, 96), V("MP", 0, 48), V("LMH", 48, 96), A.add)
        act(V("RF"), V(ar, 24, 48), F.Copy, behind=V("AC", 1, C, 4))
        act(V("XF"), ind(V("RF"), V("LFW")), F.Identity, -15.0, 2.0)
        tr(V("FW"), V("XF"))
        act(V("UP", 2, 144, 3), JJ, F.Identity, float(C + K * r) * S, 1.0)
        tt(V("UP", 144, 288, 3), V("VA", 18, 160, 3), V("UP", 2, 144, 3), A.subtract)
        lo = 128 + K * r
        for b in range(4):
            mm(V("PH%d" % b, 0, C), V("QW", 128 * b, 128 * b + 128), V("SW", 128 * b, 128 * b + 128), V("QE%d" % r),
               V("SE%d" % r))
            act(V("HT", b, C, 4), V("PH%d" % b, 0, C, 4), F.Copy, None, 0.03125)
        quant(V("QH%d" % r), V("SH%d" % r), V("HT"))
        send(dst, "rh%d" % r, [(u8(V("LQ", lo, lo + K)), u8(V("QH%d" % r, 0, K))),
                               (V("LS", lo, lo + K), V("SH%d" % r, 0, K))])
        for c in range(3):
            kl, a, b = V("KL", 2 * c, 2 * c + 1), 48 * c, 48 * c + 48
            tt(V("UP", a + 1, b, 3), ind(V("FW"), kl), V("LMH", 16 * c, 16 * c + 16), A.not_equal)
            act(V("UP", a + 145, b + 144, 3), ind(JK, kl), F.Copy)
            tt(V("UP", a + 146, b + 144, 3), ind(V("FW"), kl), V("MP", 48 + 16 * c, 64 + 16 * c), A.not_equal)
        for c0, c1 in SCANS:
            for at in (16, 176):
                scan(V("VA", at + 48 * c0, at + 48 * c1), V("UP", 48 * c0, 48 * c1),
                     V("UP", 144 + 48 * c0, 144 + 48 * c1), A.add, A.min)
        for b in range(4):
            mm(V("PH%d" % b, 0, 128), V("QC", 128 * b, 128 * b + 128), V("SC", 128 * b, 128 * b + 128),
               V("LQ", lo - 32, lo + K), V("LS", lo - 32, lo + K))
            act(V("TAB", TW * b + C + K * r, TW * b + C + K * r + K), V("PH%d" % b, 32, 128), F.Copy)

    act(V("OF"), V("VA", 18, 160, 3), F.Sign)
    for G in range(8):
        dma("y", "dout", T.ofl[:, 48 * G:48 * G + 48], V("OF", 0, 48, 1, 16 * G, 16 * G + 16, 2))
    inherit(3, V("QV"), V("SV"))
    for lo, hi in ((0, CUT), (CUT, C)):
        dma("y", "dout", T.oc[:, 4 * lo:4 * hi], u8(V("QE3", lo, hi)))
    for k in range(4):
        dma("ys"[k % 2], "dout", T.osc[4 * k:4 * k + 4, :], V("SE3", 0, C, 1, 32 * k, 32 * k + 4))
    for q, lo in (("y", CUT), ("s", CUT + 64)):
        cp(V("YO", lo, lo + 64), V("PA", lo - CUT, lo - CUT + 64))
        dma(q, "dout", T.y[:, lo:lo + 64], V("YO", lo, lo + 64))
    for lo in (0, 128):
        act(V("YO", lo, lo + 128), V("PK", lo, lo + 128), F.Copy)
        dma("s", "dout", T.y[:, lo:lo + 128], V("YO", lo, lo + 128))
    issue()
